import numpy as np
import ml_dtypes


def mxq(x, axis, fmt="e4m3"):
    dtype, down = {"e4m3": (ml_dtypes.float8_e4m3fn, 7), "e5m2": (ml_dtypes.float8_e5m2, 14)}[fmt]
    v = np.moveaxis(np.asarray(x, np.float32).astype(ml_dtypes.bfloat16).astype(np.float64), axis, -1)
    blocks = v.reshape(v.shape[:-1] + (-1, 32))
    amax = np.abs(blocks).max(-1, keepdims=True)
    byte = np.maximum(np.where(amax > 0, np.frexp(amax)[1] - 1 + 127, 0) - down, 1)
    scale = np.exp2(byte - 127.0)
    codes = (blocks / scale).astype(np.float32).astype(dtype).astype(np.float64)
    return np.moveaxis((codes * scale).reshape(v.shape), -1, axis)


WIDE = False


def mx_kscale(k):
    if not WIDE:
        return np.ones(k)
    levels = np.array([10, -10, 5, -5, 0])
    if k % 512:
        return np.exp2(np.random.permutation(np.resize(levels, k // 32))).repeat(32)
    a = np.empty((k // 512, 16))
    for p in range(k // 512):
        a[p, :8] = np.random.permutation(np.resize(levels, 8))
        for g in range(8):
            far = levels[np.abs(levels - a[p, g]) >= 10]
            a[p, g + 8] = far[np.random.randint(len(far))]
    return np.exp2(a.ravel()).repeat(32)


def f64(x):
    return np.asarray(x).astype(np.float64)


def striped(idx):
    return np.tile(idx.reshape(-1, 16).T, (8, 1)).astype(np.uint16)


def unstriped(offs):
    return offs[:16].T.reshape(-1).astype(np.int64)


E2M1 = np.array([0.0, 0.5, 1.0, 1.5, 2.0, 3.0, 4.0, 6.0, -0.0, -0.5, -1.0, -1.5, -2.0, -3.0, -4.0, -6.0])


def pack_weight(w, fmt):
    k, n = w.shape
    w = f64(np.asarray(w, np.float32).astype(ml_dtypes.bfloat16)).reshape(k // 32, 32, n)
    amax = np.abs(w).max(1)
    if fmt == "e4m3":
        byte = np.frexp(amax)[1] - 1 + 127 - 7
    else:
        mant, ex = np.frexp(amax / 6.0)
        byte = np.where(mant > 0.5, ex, ex - 1) + 127
    byte = np.clip(np.where(amax > 0, byte, 1), 1, 254)
    scaled = (w * np.exp2(127.0 - byte)[:, None, :]).reshape(k, n).astype(np.float32)
    by_word = np.ascontiguousarray(scaled.reshape(k // 512, 128, 4, n).transpose(0, 1, 3, 2))
    if fmt == "e4m3":
        words = by_word.astype(ml_dtypes.float8_e4m3fn).view(np.uint8)
    else:
        c = by_word.astype(ml_dtypes.float4_e2m1fn).view(np.uint8) & 0xF
        words = (c[..., 0::2] | (c[..., 1::2] << 4)).reshape(k // 512, 128, 2 * n)
    return np.ascontiguousarray(words), np.ascontiguousarray(byte.astype(np.uint8).reshape(k // 512, 16, n))


def unpack_weight(words, scales, fmt):
    g, _, n = scales.shape
    words = np.ascontiguousarray(words).reshape(g, 128, n, -1)
    if fmt == "e4m3":
        vals = words.view(ml_dtypes.float8_e4m3fn).astype(np.float64)
    else:
        nib = np.empty((g, 128, n, 4), np.uint8)
        nib[..., 0::2] = words & 0xF
        nib[..., 1::2] = words >> 4
        vals = E2M1[nib]
    vals = vals * np.repeat(np.exp2(scales.astype(np.float64) - 127.0), 8, axis=1)[..., None]
    return vals.transpose(0, 1, 3, 2).reshape(g * 512, n)


K, T, E, C, N = 512, 1024, 6, 128, 256


def by_expert(wq, xq):
    return np.concatenate([wq[e].T @ xq[:, e * C:(e + 1) * C] for e in range(E)], axis=1)


def setup_inputs():
    n = np.random.standard_normal
    s = mx_kscale(K)
    slot_token = np.random.permutation(T)[:E * C]
    x = pack_weight(n((K, T)) * s[:, None], "e4m3")
    wq = [pack_weight(m, "e2m1") for m in n((E, K, N)) / np.sqrt(K) / s[None, :, None]]
    wk = [pack_weight(m, "e4m3") for m in n((E, K, N)) / np.sqrt(K) / s[None, :, None]]
    return {
        "x_words": x[0],
        "x_scales": x[1],
        "wq_words": np.stack([m[0] for m in wq]),
        "wq_scales": np.stack([m[1] for m in wq]),
        "wk_words": np.stack([m[0] for m in wk]),
        "wk_scales": np.stack([m[1] for m in wk]),
        "wv": (n((E, K, N)) / np.sqrt(K) / s[None, :, None]).astype(np.float32),
        "bias": (0.3 * n((3 * N, E))).astype(np.float32),
        "gate": np.tile(np.random.uniform(0.2, 1.0, E * C), (128, 1)).astype(np.float32),
        "offs": striped(slot_token),
    }


def reference(x_words, x_scales, wq_words, wq_scales, wk_words, wk_scales, wv, bias, gate, offs):
    wq = np.stack([unpack_weight(wq_words[e], wq_scales[e], "e2m1") for e in range(E)])
    wk = np.stack([unpack_weight(wk_words[e], wk_scales[e], "e4m3") for e in range(E)])
    wvq = mxq(f64(wv), 1, "e4m3")
    idx = unstriped(offs)
    xq = unpack_weight(x_words, x_scales, "e4m3")[:, idx]
    y = np.concatenate([by_expert(w, xq) for w in (wq, wk, wvq)])
    y = y + np.repeat(f64(bias), C, axis=1)
    out = np.zeros((3 * N, T))
    out[:, idx] = f64(gate[:1]) * y
    return out

@@ -1,0 +1,160 @@
+from contextlib import ExitStack
+
+import concourse.mybir as mybir
+
+K, T, E, C, N = 512, 1024, 6, 128, 256
+FLOPS = 2 * K * 3 * N * E * C
+
+F32 = mybir.dt.float32
+BF16 = mybir.dt.bfloat16
+I32 = mybir.dt.int32
+U32 = mybir.dt.uint32
+U16 = mybir.dt.uint16
+U8 = mybir.dt.uint8
+FP8X4 = mybir.dt.float8_e4m3fn_x4
+FP4X4 = mybir.dt.float4_e2m1fn_x4
+
+P = 128
+PACK = 4
+S = E * C
+LIST = 16
+HALVES = N // P
+BLOCKS = 3 * HALVES
+PARTS = ((0, 2), (2, E))
+WINDOWS = 3
+QUANT = 2
+
+
+def tile_moe_qkv_kernel(tc, x_words, x_scales, wq_words, wq_scales, wk_words, wk_scales, wv, bias, gate, offs, out):
+    nc = tc.nc
+    mult = mybir.AluOpType.mult
+    identity = mybir.ActivationFunctionType.Identity
+
+    with ExitStack() as ctx:
+        keep = ctx.enter_context(tc.tile_pool(name="keep", bufs=1))
+        psum = ctx.enter_context(tc.psum_pool(name="psum", bufs=4))
+
+        offsets = keep.tile([P, S // LIST], U16, name="offsets")
+        x_w = keep.tile([P, T], I32, name="x_w", align_bytes=64)
+        x_s = keep.tile([P, T], U8, name="x_s", align_bytes=64)
+        q_w = keep.tile([P, E, 2 * N], U8, name="q_w", align_bytes=64)
+        q_s = keep.tile([P, E, N], U8, name="q_s", align_bytes=64)
+        k_w = keep.tile([P, E, N], I32, name="k_w", align_bytes=64)
+        k_s = keep.tile([P, E, N], U8, name="k_s", align_bytes=64)
+        v_w = keep.tile([P, E, N], U32, name="v_w", align_bytes=64)
+        v_s = keep.tile([P, E, N], U8, name="v_s", align_bytes=64)
+        bias_t = keep.tile([P, BLOCKS, 8], F32, name="bias_t")
+        gate_t = keep.tile([P, S], F32, name="gate_t")
+        windows = [keep.tile([P, T], F32, name=f"window{i}") for i in range(WINDOWS)]
+
+        def load_scale_rows(plane, rows):
+            for r in range(4):
+                nc.sync.dma_start(out=plane[r:P:32], in_=rows[r])
+
+        nc.vector.memset(x_s[:].bitcast(I32), 0)
+        nc.vector.memset(q_s[:].bitcast(I32), 0)
+        nc.vector.memset(windows[0][:], 0.0)
+        nc.vector.memset(k_s[:].bitcast(I32), 0)
+        for w in windows[1:]:
+            nc.scalar.copy(out=w[:], in_=windows[0][:])
+
+        nc.sync.dma_start(offsets[:], offs)
+        nc.sync.dma_start(out=x_w[:], in_=x_words[0].rearrange("p t d -> p (t d)").bitcast(I32))
+        load_scale_rows(x_s[:].bitcast(I32), x_scales[0].bitcast(I32).rearrange("(q r) t -> r q t", r=4))
+        nc.sync.dma_start(out=q_w[:].bitcast(I32), in_=wq_words.bitcast(I32).rearrange("e s p b -> p (e s) b"))
+        load_scale_rows(q_s[:].bitcast(I32), wq_scales.bitcast(I32).rearrange("e s (q r) n -> r q (e s) n", r=4))
+        nc.sync.dma_start(out=bias_t[:, :, 0:E], in_=bias.rearrange("(b p) e -> p b e", p=P))
+        nc.sync.dma_start(out=gate_t[:], in_=gate)
+        nc.sync.dma_start(out=k_w[:], in_=wk_words.rearrange("e s p n d -> p (e s) (n d)").bitcast(I32))
+        load_scale_rows(k_s[:].bitcast(I32), wk_scales.bitcast(I32).rearrange("e s (q r) n -> r q (e s) n", r=4))
+        v_raw = []
+        for e in range(E):
+            raw = keep.tile([P, PACK, N], F32, name=f"v_raw{e}")
+            nc.sync.dma_start(out=raw[:], in_=wv[e].rearrange("(p j) n -> p j n", j=PACK))
+            v_raw.append(raw)
+
+        slot_w, slot_s = [], []
+        for i, (e0, e1) in enumerate(PARTS):
+            entries = offsets[:, e0 * C // LIST : e1 * C // LIST]
+            words = keep.tile([P, (e1 - e0) * C], U32, name=f"slot_w{i}", align_bytes=64)
+            scales = keep.tile([P, (e1 - e0) * C], U8, name=f"slot_s{i}", align_bytes=64)
+            nc.vector.tensor_copy(words[:], x_w[:].bitcast(U32).indirect(entries))
+            nc.vector.tensor_copy(scales[:], x_s[:].indirect(entries))
+            slot_w.append(words)
+            slot_s.append(scales)
+
+        def weights(b, e):
+            proj, h = divmod(b, HALVES)
+            cols = slice(h * P, (h + 1) * P)
+            if proj == 0:
+                return q_w[:, e, 2 * h * P : 2 * (h + 1) * P].bitcast(FP4X4), q_s[:, e, cols]
+            if proj == 1:
+                return k_w[:, e, cols].bitcast(FP8X4), k_s[:, e, cols]
+            return v_w[:, e, cols].bitcast(FP8X4), v_s[:, e, cols]
+
+        ys = [keep.tile([P, S], F32, name=f"y{b}") for b in range(BLOCKS)]
+
+        def project(b, i):
+            e0, e1 = PARTS[i]
+            acc = psum.tile([P, (e1 - e0) * C], F32, name=f"acc{i}")
+            for e in range(e0, e1):
+                cols = slice((e - e0) * C, (e - e0 + 1) * C)
+                w_codes, w_scales = weights(b, e)
+                nc.tensor.matmul_mx(
+                    out=acc[:, cols],
+                    lhsT=w_codes,
+                    lhsT_scale=w_scales,
+                    rhs=slot_w[i][:, cols].bitcast(FP8X4),
+                    rhs_scale=slot_s[i][:, cols],
+                    start=True,
+                    stop=True,
+                )
+            for e in range(e0, e1):
+                cols = slice((e - e0) * C, (e - e0 + 1) * C)
+                nc.scalar.activation(
+                    out=ys[b][:, e * C : (e + 1) * C], in_=acc[:, cols], func=identity, bias=bias_t[:, b, e : e + 1]
+                )
+
+        def scatter(b, e0, e1):
+            cols = slice(e0 * C, e1 * C)
+            entries = offsets[:, e0 * C // LIST : e1 * C // LIST]
+            nc.vector.tensor_tensor(windows[b % WINDOWS][:].indirect(entries), ys[b][:, cols], gate_t[:, cols], mult)
+
+        def store(b):
+            nc.sync.dma_start(out=out[b * P : (b + 1) * P, :], in_=windows[b % WINDOWS][:])
+
+        for i in range(len(PARTS)):
+            for b in (0, 1):
+                project(b, i)
+        for i in range(len(PARTS)):
+            for b in (0, 1):
+                scatter(b, *PARTS[i])
+        store(0)
+        store(1)
+
+        for b in (2, 3):
+            for i in range(len(PARTS)):
+                project(b, i)
+        scatter(2, 0, E)
+        store(2)
+
+        for e0 in range(0, E, QUANT):
+            grouped = keep.tile([P, QUANT, N, PACK], BF16, name=f"grouped{e0}", align_bytes=64)
+            for e in range(e0, e0 + QUANT):
+                nc.scalar.copy(
+                    out=grouped[:, e - e0].rearrange("p (c i) t -> p c t i", i=4),
+                    in_=v_raw[e][:].rearrange("p t (c i) -> p c t i", i=4),
+                )
+            nc.vector.quantize_mx(
+                out=v_w[:, e0 : e0 + QUANT].rearrange("p e n -> p (e n)").bitcast(FP8X4),
+                scales=v_s[:, e0 : e0 + QUANT].rearrange("p e n -> p (e n)"),
+                in_=grouped[:].rearrange("p e n t -> p (e n t)"),
+            )
+        scatter(3, 0, E)
+        store(3)
+
+        for b in (4, 5):
+            for i in range(len(PARTS)):
+                project(b, i)
+            scatter(b, 0, E)
+            store(b)

@@ -32,19 +32,16 @@ def tile_moe_qkv_kernel(tc, x_words, x_scales, wq_words, wq_scales, wk_words, wk
 
     with ExitStack() as ctx:
         keep = ctx.enter_context(tc.tile_pool(name="keep", bufs=1))
-        psum = ctx.enter_context(tc.psum_pool(name="psum", bufs=4))
+        psum = ctx.enter_context(tc.psum_pool(name="psum", bufs=8))
 
         offsets = keep.tile([P, S // LIST], U16, name="offsets")
-        x_w = keep.tile([P, T], I32, name="x_w", align_bytes=64)
-        x_s = keep.tile([P, T], U8, name="x_s", align_bytes=64)
-        q_w = keep.tile([P, E, 2 * N], U8, name="q_w", align_bytes=64)
-        q_s = keep.tile([P, E, N], U8, name="q_s", align_bytes=64)
-        k_w = keep.tile([P, E, N], I32, name="k_w", align_bytes=64)
-        k_s = keep.tile([P, E, N], U8, name="k_s", align_bytes=64)
+        x_w = keep.tile([P, T], I32, name="x_w", tag="x_w", align_bytes=64)
+        x_s = keep.tile([P, T], U8, name="x_s", tag="x_s", align_bytes=64)
+        q_w = keep.tile([P, E, 2 * N], U8, name="q_w", tag="q_w", align_bytes=64)
+        q_s = keep.tile([P, E, N], U8, name="q_s", tag="q_s", align_bytes=64)
+        zeros = [keep.tile([P, 8], F32, name=f"zero{i}", tag=f"zero{i}", align_bytes=64) for i in range(WINDOWS - 1)]
         v_w = keep.tile([P, E, N], U32, name="v_w", align_bytes=64)
         v_s = keep.tile([P, E, N], U8, name="v_s", align_bytes=64)
-        bias_t = keep.tile([P, BLOCKS, 8], F32, name="bias_t")
-        gate_t = keep.tile([P, S], F32, name="gate_t")
         windows = [keep.tile([P, T], F32, name=f"window{i}") for i in range(WINDOWS)]
 
         def load_scale_rows(plane, rows):
@@ -53,25 +50,20 @@ def tile_moe_qkv_kernel(tc, x_words, x_scales, wq_words, wq_scales, wk_words, wk
 
         nc.vector.memset(x_s[:].bitcast(I32), 0)
         nc.vector.memset(q_s[:].bitcast(I32), 0)
+        for w, zero in zip(windows[1:], zeros):
+            nc.vector.memset(zero[:], 0.0)
+            nc.scalar.copy(out=w[:], in_=zero[:, 0:1].to_broadcast([P, T]))
         nc.vector.memset(windows[0][:], 0.0)
-        nc.vector.memset(k_s[:].bitcast(I32), 0)
-        for w in windows[1:]:
-            nc.scalar.copy(out=w[:], in_=windows[0][:])
 
         nc.sync.dma_start(offsets[:], offs)
         nc.sync.dma_start(out=x_w[:], in_=x_words[0].rearrange("p t d -> p (t d)").bitcast(I32))
         load_scale_rows(x_s[:].bitcast(I32), x_scales[0].bitcast(I32).rearrange("(q r) t -> r q t", r=4))
         nc.sync.dma_start(out=q_w[:].bitcast(I32), in_=wq_words.bitcast(I32).rearrange("e s p b -> p (e s) b"))
         load_scale_rows(q_s[:].bitcast(I32), wq_scales.bitcast(I32).rearrange("e s (q r) n -> r q (e s) n", r=4))
+        bias_t = keep.tile([P, BLOCKS, 8], F32, name="bias_t", tag="zero0", align_bytes=64)
         nc.sync.dma_start(out=bias_t[:, :, 0:E], in_=bias.rearrange("(b p) e -> p b e", p=P))
-        nc.sync.dma_start(out=gate_t[:], in_=gate)
-        nc.sync.dma_start(out=k_w[:], in_=wk_words.rearrange("e s p n d -> p (e s) (n d)").bitcast(I32))
-        load_scale_rows(k_s[:].bitcast(I32), wk_scales.bitcast(I32).rearrange("e s (q r) n -> r q (e s) n", r=4))
-        v_raw = []
-        for e in range(E):
-            raw = keep.tile([P, PACK, N], F32, name=f"v_raw{e}")
-            nc.sync.dma_start(out=raw[:], in_=wv[e].rearrange("(p j) n -> p j n", j=PACK))
-            v_raw.append(raw)
+        gate_head = keep.tile([P, PARTS[0][1] * C], F32, name="gate_head", tag="zero1", align_bytes=64)
+        nc.sync.dma_start(out=gate_head[:], in_=gate[:, 0 : PARTS[0][1] * C])
 
         slot_w, slot_s = [], []
         for i, (e0, e1) in enumerate(PARTS):
@@ -80,8 +72,16 @@ def tile_moe_qkv_kernel(tc, x_words, x_scales, wq_words, wq_scales, wk_words, wk
             scales = keep.tile([P, (e1 - e0) * C], U8, name=f"slot_s{i}", align_bytes=64)
             nc.vector.tensor_copy(words[:], x_w[:].bitcast(U32).indirect(entries))
             nc.vector.tensor_copy(scales[:], x_s[:].indirect(entries))
-            slot_w.append(words)
-            slot_s.append(scales)
+            for e in range(e0, e1):
+                cols = slice((e - e0) * C, (e - e0 + 1) * C)
+                slot_w.append(words[:, cols].bitcast(FP8X4))
+                slot_s.append(scales[:, cols])
+
+        gate_t = keep.tile([P, S], F32, name="gate_t", tag="x_w", align_bytes=64)
+        nc.sync.dma_start(out=gate_t[:], in_=gate)
+        k_s = keep.tile([P, E, N], U8, name="k_s", tag="x_s", align_bytes=64)
+        nc.gpsimd.memset(k_s[:].bitcast(I32), 0)
+        load_scale_rows(k_s[:].bitcast(I32), wk_scales.bitcast(I32).rearrange("e s (q r) n -> r q (e s) n", r=4))
 
         def weights(b, e):
             proj, h = divmod(b, HALVES)
@@ -92,69 +92,82 @@ def tile_moe_qkv_kernel(tc, x_words, x_scales, wq_words, wq_scales, wk_words, wk
                 return k_w[:, e, cols].bitcast(FP8X4), k_s[:, e, cols]
             return v_w[:, e, cols].bitcast(FP8X4), v_s[:, e, cols]
 
-        ys = [keep.tile([P, S], F32, name=f"y{b}") for b in range(BLOCKS)]
-
-        def project(b, i):
-            e0, e1 = PARTS[i]
-            acc = psum.tile([P, (e1 - e0) * C], F32, name=f"acc{i}")
+        def project(y, b, e0, e1):
+            acc = psum.tile([P, (e1 - e0) * C], F32, name="acc")
             for e in range(e0, e1):
-                cols = slice((e - e0) * C, (e - e0 + 1) * C)
                 w_codes, w_scales = weights(b, e)
                 nc.tensor.matmul_mx(
-                    out=acc[:, cols],
+                    out=acc[:, (e - e0) * C : (e - e0 + 1) * C],
                     lhsT=w_codes,
                     lhsT_scale=w_scales,
-                    rhs=slot_w[i][:, cols].bitcast(FP8X4),
-                    rhs_scale=slot_s[i][:, cols],
+                    rhs=slot_w[e],
+                    rhs_scale=slot_s[e],
                     start=True,
                     stop=True,
                 )
             for e in range(e0, e1):
-                cols = slice((e - e0) * C, (e - e0 + 1) * C)
                 nc.scalar.activation(
-                    out=ys[b][:, e * C : (e + 1) * C], in_=acc[:, cols], func=identity, bias=bias_t[:, b, e : e + 1]
+                    out=y[:, e * C : (e + 1) * C],
+                    in_=acc[:, (e - e0) * C : (e - e0 + 1) * C],
+                    func=identity,
+                    bias=bias_t[:, b, e : e + 1],
                 )
 
-        def scatter(b, e0, e1):
+        def scatter(y, gates, b, e0, e1):
             cols = slice(e0 * C, e1 * C)
             entries = offsets[:, e0 * C // LIST : e1 * C // LIST]
-            nc.vector.tensor_tensor(windows[b % WINDOWS][:].indirect(entries), ys[b][:, cols], gate_t[:, cols], mult)
+            nc.vector.tensor_tensor(windows[b % WINDOWS][:].indirect(entries), y[:, cols], gates[:, cols], mult)
 
         def store(b):
             nc.sync.dma_start(out=out[b * P : (b + 1) * P, :], in_=windows[b % WINDOWS][:])
 
-        for i in range(len(PARTS)):
+        ys = [keep.tile([P, S], F32, name=f"y{b}", tag=f"y{b}", align_bytes=64) for b in range(4)]
+        for part in PARTS:
             for b in (0, 1):
-                project(b, i)
-        for i in range(len(PARTS)):
-            for b in (0, 1):
-                scatter(b, *PARTS[i])
+                project(ys[b], b, *part)
+        k_w = keep.tile([P, E, N], I32, name="k_w", tag="q_w", align_bytes=64)
+        nc.sync.dma_start(out=k_w[:], in_=wk_words.rearrange("e s p n d -> p (e s) (n d)").bitcast(I32))
+
+        def load_v(e0, tag):
+            raw = keep.tile([P, QUANT, PACK, N], F32, name=f"v_raw{e0}", tag=tag, align_bytes=64)
+            nc.sync.dma_start(out=raw[:], in_=wv[e0 : e0 + QUANT].rearrange("e (p j) n -> p e j n", j=PACK))
+            return raw
+
+        v_raw = [load_v(0, "q_s")]
+        for b in (0, 1):
+            scatter(ys[b], gate_head, b, *PARTS[0])
+        v_raw.append(load_v(2, "zero1"))
+        scatter(ys[0], gate_t, 0, *PARTS[1])
+        v_raw.append(load_v(4, "y0"))
         store(0)
+        scatter(ys[1], gate_t, 1, *PARTS[1])
         store(1)
 
         for b in (2, 3):
-            for i in range(len(PARTS)):
-                project(b, i)
-        scatter(2, 0, E)
-        store(2)
+            for part in PARTS:
+                project(ys[b], b, *part)
+            scatter(ys[b], gate_t, b, 0, E)
+            store(b)
 
-        for e0 in range(0, E, QUANT):
+        for raw, e0 in zip(v_raw, range(0, E, QUANT)):
             grouped = keep.tile([P, QUANT, N, PACK], BF16, name=f"grouped{e0}", align_bytes=64)
-            for e in range(e0, e0 + QUANT):
+            for e in range(QUANT):
                 nc.scalar.copy(
-                    out=grouped[:, e - e0].rearrange("p (c i) t -> p c t i", i=4),
-                    in_=v_raw[e][:].rearrange("p t (c i) -> p c t i", i=4),
+                    out=grouped[:, e].rearrange("p (c i) t -> p c t i", i=4),
+                    in_=raw[:, e].rearrange("p t (c i) -> p c t i", i=4),
                 )
             nc.vector.quantize_mx(
                 out=v_w[:, e0 : e0 + QUANT].rearrange("p e n -> p (e n)").bitcast(FP8X4),
                 scales=v_s[:, e0 : e0 + QUANT].rearrange("p e n -> p (e n)"),
                 in_=grouped[:].rearrange("p e n t -> p (e n t)"),
             )
-        scatter(3, 0, E)
-        store(3)
 
-        for b in (4, 5):
-            for i in range(len(PARTS)):
-                project(b, i)
-            scatter(b, 0, E)
-            store(b)
+        y_v = keep.tile([P, HALVES, S], F32, name="y_v", tag="y0", align_bytes=64)
+        for part in PARTS:
+            for b in (4, 5):
+                project(y_v[:, b - 4], b, *part)
+        for part in PARTS:
+            for b in (4, 5):
+                scatter(y_v[:, b - 4], gate_t, b, *part)
+        store(4)
+        store(5)

@@ -20,7 +20,8 @@ S = E * C
 LIST = 16
 HALVES = N // P
 BLOCKS = 3 * HALVES
-PARTS = ((0, 2), (2, E))
+HEAD = 2
+PARTS = ((0, HEAD), (HEAD, E))
 WINDOWS = 3
 QUANT = 2
 
@@ -35,11 +36,11 @@ def tile_moe_qkv_kernel(tc, x_words, x_scales, wq_words, wq_scales, wk_words, wk
         psum = ctx.enter_context(tc.psum_pool(name="psum", bufs=8))
 
         offsets = keep.tile([P, S // LIST], U16, name="offsets")
-        x_w = keep.tile([P, T], I32, name="x_w", tag="x_w", align_bytes=64)
         x_s = keep.tile([P, T], U8, name="x_s", tag="x_s", align_bytes=64)
-        q_w = keep.tile([P, E, 2 * N], U8, name="q_w", tag="q_w", align_bytes=64)
+        q_head = keep.tile([P, HEAD, 2 * N], U8, name="q_head", tag="q_head", align_bytes=64)
         q_s = keep.tile([P, E, N], U8, name="q_s", tag="q_s", align_bytes=64)
         zeros = [keep.tile([P, 8], F32, name=f"zero{i}", tag=f"zero{i}", align_bytes=64) for i in range(WINDOWS - 1)]
+        seeds = [keep.tile([P, 8], F32, name=f"seed{i}", tag=f"seed{i}", align_bytes=64) for i in range(WINDOWS - 1)]
         v_w = keep.tile([P, E, N], U32, name="v_w", align_bytes=64)
         v_s = keep.tile([P, E, N], U8, name="v_s", align_bytes=64)
         windows = [keep.tile([P, T], F32, name=f"window{i}") for i in range(WINDOWS)]
@@ -48,38 +49,45 @@ def tile_moe_qkv_kernel(tc, x_words, x_scales, wq_words, wq_scales, wk_words, wk
             for r in range(4):
                 nc.sync.dma_start(out=plane[r:P:32], in_=rows[r])
 
+        for seed in seeds:
+            nc.vector.memset(seed[:], 0.0)
         nc.vector.memset(x_s[:].bitcast(I32), 0)
+        for seed, zero in zip(seeds, zeros):
+            nc.vector.tensor_copy(zero[:], seed[:])
         nc.vector.memset(q_s[:].bitcast(I32), 0)
-        for w, zero in zip(windows[1:], zeros):
-            nc.vector.memset(zero[:], 0.0)
-            nc.scalar.copy(out=w[:], in_=zero[:, 0:1].to_broadcast([P, T]))
         nc.vector.memset(windows[0][:], 0.0)
+        for w, zero in zip(windows[1:], zeros):
+            nc.scalar.copy(out=w[:], in_=zero[:, 0:1].to_broadcast([P, T]))
 
         nc.sync.dma_start(offsets[:], offs)
-        nc.sync.dma_start(out=x_w[:], in_=x_words[0].rearrange("p t d -> p (t d)").bitcast(I32))
+        q_rows = wq_words.bitcast(I32).rearrange("e s p b -> p (e s) b")
+        nc.sync.dma_start(out=q_head[:].bitcast(I32), in_=q_rows[:, 0:HEAD])
         load_scale_rows(x_s[:].bitcast(I32), x_scales[0].bitcast(I32).rearrange("(q r) t -> r q t", r=4))
-        nc.sync.dma_start(out=q_w[:].bitcast(I32), in_=wq_words.bitcast(I32).rearrange("e s p b -> p (e s) b"))
+        x_w = keep.tile([P, T], I32, name="x_w", tag="seed0", align_bytes=64)
+        nc.sync.dma_start(out=x_w[:], in_=x_words[0].rearrange("p t d -> p (t d)").bitcast(I32))
         load_scale_rows(q_s[:].bitcast(I32), wq_scales.bitcast(I32).rearrange("e s (q r) n -> r q (e s) n", r=4))
-        bias_t = keep.tile([P, BLOCKS, 8], F32, name="bias_t", tag="zero0", align_bytes=64)
-        nc.sync.dma_start(out=bias_t[:, :, 0:E], in_=bias.rearrange("(b p) e -> p b e", p=P))
-        gate_head = keep.tile([P, PARTS[0][1] * C], F32, name="gate_head", tag="zero1", align_bytes=64)
-        nc.sync.dma_start(out=gate_head[:], in_=gate[:, 0 : PARTS[0][1] * C])
+        bias_rows = bias.rearrange("(b p) e -> p b e", p=P)
+        bias_q = keep.tile([P, HALVES, 8], F32, name="bias_q", tag="seed1", align_bytes=64)
+        nc.sync.dma_start(out=bias_q[:, :, 0:E], in_=bias_rows[:, 0:HALVES])
+        gate_head = keep.tile([P, HEAD * C], F32, name="gate_head", tag="zero0", align_bytes=64)
+        nc.sync.dma_start(out=gate_head[:], in_=gate[:, 0 : HEAD * C])
+        q_tail = keep.tile([P, E - HEAD, 2 * N], U8, name="q_tail", tag="zero1", align_bytes=64)
+        nc.sync.dma_start(out=q_tail[:].bitcast(I32), in_=q_rows[:, HEAD:E])
 
-        slot_w, slot_s = [], []
-        for i, (e0, e1) in enumerate(PARTS):
-            entries = offsets[:, e0 * C // LIST : e1 * C // LIST]
-            words = keep.tile([P, (e1 - e0) * C], U32, name=f"slot_w{i}", align_bytes=64)
-            scales = keep.tile([P, (e1 - e0) * C], U8, name=f"slot_s{i}", align_bytes=64)
-            nc.vector.tensor_copy(words[:], x_w[:].bitcast(U32).indirect(entries))
-            nc.vector.tensor_copy(scales[:], x_s[:].indirect(entries))
-            for e in range(e0, e1):
-                cols = slice((e - e0) * C, (e - e0 + 1) * C)
-                slot_w.append(words[:, cols].bitcast(FP8X4))
-                slot_s.append(scales[:, cols])
+        def gather(window, dtype, name, parts):
+            slots = []
+            for e0, e1 in parts:
+                part = keep.tile([P, (e1 - e0) * C], dtype, name=f"{name}{e0}", align_bytes=64)
+                nc.vector.tensor_copy(part[:], window.indirect(offsets[:, e0 * C // LIST : e1 * C // LIST]))
+                slots.extend(part[:, (e - e0) * C : (e - e0 + 1) * C] for e in range(e0, e1))
+            return slots
 
-        gate_t = keep.tile([P, S], F32, name="gate_t", tag="x_w", align_bytes=64)
+        slot_s = gather(x_s[:], U8, "slot_s", [(0, E)])
+        slot_w = gather(x_w[:].bitcast(U32), U32, "slot_w", PARTS)
+
+        gate_t = keep.tile([P, S], F32, name="gate_t", tag="x_s", align_bytes=64)
         nc.sync.dma_start(out=gate_t[:], in_=gate)
-        k_s = keep.tile([P, E, N], U8, name="k_s", tag="x_s", align_bytes=64)
+        k_s = keep.tile([P, E, N], U8, name="k_s", tag="seed0", align_bytes=64)
         nc.gpsimd.memset(k_s[:].bitcast(I32), 0)
         load_scale_rows(k_s[:].bitcast(I32), wk_scales.bitcast(I32).rearrange("e s (q r) n -> r q (e s) n", r=4))
 
@@ -87,7 +95,8 @@ def tile_moe_qkv_kernel(tc, x_words, x_scales, wq_words, wq_scales, wk_words, wk
             proj, h = divmod(b, HALVES)
             cols = slice(h * P, (h + 1) * P)
             if proj == 0:
-                return q_w[:, e, 2 * h * P : 2 * (h + 1) * P].bitcast(FP4X4), q_s[:, e, cols]
+                q_w = q_head[:, e] if e < HEAD else q_tail[:, e - HEAD]
+                return q_w[:, 2 * h * P : 2 * (h + 1) * P].bitcast(FP4X4), q_s[:, e, cols]
             if proj == 1:
                 return k_w[:, e, cols].bitcast(FP8X4), k_s[:, e, cols]
             return v_w[:, e, cols].bitcast(FP8X4), v_s[:, e, cols]
@@ -100,7 +109,7 @@ def tile_moe_qkv_kernel(tc, x_words, x_scales, wq_words, wq_scales, wk_words, wk
                     out=acc[:, (e - e0) * C : (e - e0 + 1) * C],
                     lhsT=w_codes,
                     lhsT_scale=w_scales,
-                    rhs=slot_w[e],
+                    rhs=slot_w[e].bitcast(FP8X4),
                     rhs_scale=slot_s[e],
                     start=True,
                     stop=True,
@@ -110,7 +119,7 @@ def tile_moe_qkv_kernel(tc, x_words, x_scales, wq_words, wq_scales, wk_words, wk
                     out=y[:, e * C : (e + 1) * C],
                     in_=acc[:, (e - e0) * C : (e - e0 + 1) * C],
                     func=identity,
-                    bias=bias_t[:, b, e : e + 1],
+                    bias=(bias_q[:, b] if b < HALVES else bias_kv[:, b - HALVES])[:, e : e + 1],
                 )
 
         def scatter(y, gates, b, e0, e1):
@@ -125,8 +134,10 @@ def tile_moe_qkv_kernel(tc, x_words, x_scales, wq_words, wq_scales, wk_words, wk
         for part in PARTS:
             for b in (0, 1):
                 project(ys[b], b, *part)
-        k_w = keep.tile([P, E, N], I32, name="k_w", tag="q_w", align_bytes=64)
+        k_w = keep.tile([P, E, N], I32, name="k_w", tag="q_head", align_bytes=64)
         nc.sync.dma_start(out=k_w[:], in_=wk_words.rearrange("e s p n d -> p (e s) (n d)").bitcast(I32))
+        bias_kv = keep.tile([P, BLOCKS - HALVES, 8], F32, name="bias_kv", tag="zero1", align_bytes=64)
+        nc.sync.dma_start(out=bias_kv[:, :, 0:E], in_=bias_rows[:, HALVES:BLOCKS])
 
         def load_v(e0, tag):
             raw = keep.tile([P, QUANT, PACK, N], F32, name=f"v_raw{e0}", tag=tag, align_bytes=64)
@@ -136,7 +147,7 @@ def tile_moe_qkv_kernel(tc, x_words, x_scales, wq_words, wq_scales, wk_words, wk
         v_raw = [load_v(0, "q_s")]
         for b in (0, 1):
             scatter(ys[b], gate_head, b, *PARTS[0])
-        v_raw.append(load_v(2, "zero1"))
+        v_raw.append(load_v(2, "zero0"))
         scatter(ys[0], gate_t, 0, *PARTS[1])
         v_raw.append(load_v(4, "y0"))
         store(0)

@@ -154,10 +154,13 @@ def tile_moe_qkv_kernel(tc, x_words, x_scales, wq_words, wq_scales, wk_words, wk
         scatter(ys[1], gate_t, 1, *PARTS[1])
         store(1)
 
+        gated = [keep.tile([P, S], F32, name=f"gated{b}", align_bytes=64) for b in (2, 3)]
         for b in (2, 3):
             for part in PARTS:
                 project(ys[b], b, *part)
-            scatter(ys[b], gate_t, b, 0, E)
+            nc.vector.tensor_tensor(gated[b - 2][:], ys[b][:], gate_t[:], mult)
+        for b in (2, 3):
+            nc.vector.tensor_copy(windows[b % WINDOWS][:].indirect(offsets[:]), gated[b - 2][:])
             store(b)
 
         for raw, e0 in zip(v_raw, range(0, E, QUANT)):

@@ -55,6 +55,8 @@ def tile_moe_qkv_kernel(tc, x_words, x_scales, wq_words, wq_scales, wk_words, wk
         for seed, zero in zip(seeds, zeros):
             nc.vector.tensor_copy(zero[:], seed[:])
         nc.vector.memset(q_s[:].bitcast(I32), 0)
+        k_s = keep.tile([P, E, N], U8, name="k_s", align_bytes=64)
+        nc.vector.memset(k_s[:].bitcast(I32), 0)
         nc.vector.memset(windows[0][:], 0.0)
         for w, zero in zip(windows[1:], zeros):
             nc.scalar.copy(out=w[:], in_=zero[:, 0:1].to_broadcast([P, T]))
@@ -87,8 +89,6 @@ def tile_moe_qkv_kernel(tc, x_words, x_scales, wq_words, wq_scales, wk_words, wk
 
         gate_t = keep.tile([P, S], F32, name="gate_t", tag="x_s", align_bytes=64)
         nc.sync.dma_start(out=gate_t[:], in_=gate)
-        k_s = keep.tile([P, E, N], U8, name="k_s", tag="seed0", align_bytes=64)
-        nc.gpsimd.memset(k_s[:].bitcast(I32), 0)
         load_scale_rows(k_s[:].bitcast(I32), wk_scales.bitcast(I32).rearrange("e s (q r) n -> r q (e s) n", r=4))
 
         def weights(b, e):
@@ -125,12 +125,14 @@ def tile_moe_qkv_kernel(tc, x_words, x_scales, wq_words, wq_scales, wk_words, wk
         def scatter(y, gates, b, e0, e1):
             cols = slice(e0 * C, e1 * C)
             entries = offsets[:, e0 * C // LIST : e1 * C // LIST]
-            nc.vector.tensor_tensor(windows[b % WINDOWS][:].indirect(entries), y[:, cols], gates[:, cols], mult)
+            gated = keep.tile([P, (e1 - e0) * C], F32, name=f"gated{b}_{e0}", align_bytes=64)
+            nc.gpsimd.tensor_tensor(gated[:], y[:, cols], gates[:, cols], mult)
+            nc.vector.tensor_copy(windows[b % WINDOWS][:].indirect(entries), gated[:])
 
         def store(b):
             nc.sync.dma_start(out=out[b * P : (b + 1) * P, :], in_=windows[b % WINDOWS][:])
 
-        ys = [keep.tile([P, S], F32, name=f"y{b}", tag=f"y{b}", align_bytes=64) for b in range(4)]
+        ys = [keep.tile([P, S], F32, name=f"y{b}", tag=f"y{b}", align_bytes=64) for b in range(3)]
         for part in PARTS:
             for b in (0, 1):
                 project(ys[b], b, *part)
@@ -154,14 +156,10 @@ def tile_moe_qkv_kernel(tc, x_words, x_scales, wq_words, wq_scales, wk_words, wk
         scatter(ys[1], gate_t, 1, *PARTS[1])
         store(1)
 
-        gated = [keep.tile([P, S], F32, name=f"gated{b}", align_bytes=64) for b in (2, 3)]
-        for b in (2, 3):
-            for part in PARTS:
-                project(ys[b], b, *part)
-            nc.vector.tensor_tensor(gated[b - 2][:], ys[b][:], gate_t[:], mult)
-        for b in (2, 3):
-            nc.vector.tensor_copy(windows[b % WINDOWS][:].indirect(offsets[:]), gated[b - 2][:])
-            store(b)
+        for part in PARTS:
+            project(ys[2], 2, *part)
+        scatter(ys[2], gate_t, 2, 0, E)
+        store(2)
 
         for raw, e0 in zip(v_raw, range(0, E, QUANT)):
             grouped = keep.tile([P, QUANT, N, PACK], BF16, name=f"grouped{e0}", align_bytes=64)
@@ -175,6 +173,12 @@ def tile_moe_qkv_kernel(tc, x_words, x_scales, wq_words, wq_scales, wk_words, wk
                 scales=v_s[:, e0 : e0 + QUANT].rearrange("p e n -> p (e n)"),
                 in_=grouped[:].rearrange("p e n t -> p (e n t)"),
             )
+
+        y_3 = keep.tile([P, S], F32, name="y3", tag="y0", align_bytes=64)
+        for part in PARTS:
+            project(y_3, 3, *part)
+        scatter(y_3, gate_t, 3, 0, E)
+        store(3)
 
         y_v = keep.tile([P, HALVES, S], F32, name="y_v", tag="y0", align_bytes=64)
         for part in PARTS:

@@ -19,9 +19,9 @@ PACK = 4
 S = E * C
 LIST = 16
 HALVES = N // P
-BLOCKS = 3 * HALVES
 HEAD = 2
 PARTS = ((0, HEAD), (HEAD, E))
+FIRST_PARTS = ((0, 1), (1, HEAD), (HEAD, E))
 WINDOWS = 3
 QUANT = 2
 
@@ -35,19 +35,16 @@ def tile_moe_qkv_kernel(tc, x_words, x_scales, wq_words, wq_scales, wk_words, wk
         keep = ctx.enter_context(tc.tile_pool(name="keep", bufs=1))
         psum = ctx.enter_context(tc.psum_pool(name="psum", bufs=8))
 
-        offsets = keep.tile([P, S // LIST], U16, name="offsets")
-        x_s = keep.tile([P, T], U8, name="x_s", tag="x_s", align_bytes=64)
-        q_head = keep.tile([P, HEAD, 2 * N], U8, name="q_head", tag="q_head", align_bytes=64)
-        q_s = keep.tile([P, E, N], U8, name="q_s", tag="q_s", align_bytes=64)
-        zeros = [keep.tile([P, 8], F32, name=f"zero{i}", tag=f"zero{i}", align_bytes=64) for i in range(WINDOWS - 1)]
-        seeds = [keep.tile([P, 8], F32, name=f"seed{i}", tag=f"seed{i}", align_bytes=64) for i in range(WINDOWS - 1)]
-        v_w = keep.tile([P, E, N], U32, name="v_w", align_bytes=64)
-        v_s = keep.tile([P, E, N], U8, name="v_s", align_bytes=64)
-        windows = [keep.tile([P, T], F32, name=f"window{i}") for i in range(WINDOWS)]
+        def tile(shape, dtype, name, tag=None):
+            return keep.tile(shape, dtype, name=name, tag=tag or name, align_bytes=64)
 
-        def load_scale_rows(plane, rows):
-            for r in range(4):
-                nc.sync.dma_start(out=plane[r:P:32], in_=rows[r])
+        offsets = keep.tile([P, S // LIST], U16, name="offsets")
+        x_s = tile([P, T], U8, "x_s")
+        q_s = tile([P, E, N], U8, "q_s")
+        k_s = tile([P, E, N], U8, "k_s")
+        seeds = [tile([P, 8], F32, f"seed{i}") for i in range(WINDOWS - 1)]
+        zeros = [tile([P, 8], F32, f"zero{i}") for i in range(WINDOWS - 1)]
+        windows = [tile([P, T], F32, f"window{i}") for i in range(WINDOWS)]
 
         for seed in seeds:
             nc.vector.memset(seed[:], 0.0)
@@ -55,56 +52,60 @@ def tile_moe_qkv_kernel(tc, x_words, x_scales, wq_words, wq_scales, wk_words, wk
         for seed, zero in zip(seeds, zeros):
             nc.vector.tensor_copy(zero[:], seed[:])
         nc.vector.memset(q_s[:].bitcast(I32), 0)
-        k_s = keep.tile([P, E, N], U8, name="k_s", align_bytes=64)
-        nc.vector.memset(k_s[:].bitcast(I32), 0)
         nc.vector.memset(windows[0][:], 0.0)
+        nc.vector.memset(k_s[:].bitcast(I32), 0)
         for w, zero in zip(windows[1:], zeros):
             nc.scalar.copy(out=w[:], in_=zero[:, 0:1].to_broadcast([P, T]))
 
-        nc.sync.dma_start(offsets[:], offs)
+        def load_scale_rows(plane, rows):
+            for r in range(4):
+                nc.sync.dma_start(out=plane[r:P:32], in_=rows[r])
+
+        def weight_scale_rows(scales):
+            return scales.bitcast(I32).rearrange("e s (q r) n -> r q (e s) n", r=4)
+
         q_rows = wq_words.bitcast(I32).rearrange("e s p b -> p (e s) b")
+        bias_rows = bias.rearrange("(b p) e -> p b e", p=P)
+
+        nc.sync.dma_start(offsets[:], offs)
+        q_head = tile([P, HEAD, 2 * N], U8, "q_head")
         nc.sync.dma_start(out=q_head[:].bitcast(I32), in_=q_rows[:, 0:HEAD])
         load_scale_rows(x_s[:].bitcast(I32), x_scales[0].bitcast(I32).rearrange("(q r) t -> r q t", r=4))
-        x_w = keep.tile([P, T], I32, name="x_w", tag="seed0", align_bytes=64)
+        x_w = tile([P, T], I32, "x_w", tag="seed0")
         nc.sync.dma_start(out=x_w[:], in_=x_words[0].rearrange("p t d -> p (t d)").bitcast(I32))
-        load_scale_rows(q_s[:].bitcast(I32), wq_scales.bitcast(I32).rearrange("e s (q r) n -> r q (e s) n", r=4))
-        bias_rows = bias.rearrange("(b p) e -> p b e", p=P)
-        bias_q = keep.tile([P, HALVES, 8], F32, name="bias_q", tag="seed1", align_bytes=64)
+        load_scale_rows(q_s[:].bitcast(I32), weight_scale_rows(wq_scales))
+        bias_q = tile([P, HALVES, 8], F32, "bias_q", tag="seed1")
         nc.sync.dma_start(out=bias_q[:, :, 0:E], in_=bias_rows[:, 0:HALVES])
-        gate_head = keep.tile([P, HEAD * C], F32, name="gate_head", tag="zero0", align_bytes=64)
+        gate_head = tile([P, HEAD * C], F32, "gate_head", tag="zero0")
         nc.sync.dma_start(out=gate_head[:], in_=gate[:, 0 : HEAD * C])
-        q_tail = keep.tile([P, E - HEAD, 2 * N], U8, name="q_tail", tag="zero1", align_bytes=64)
+        q_tail = tile([P, E - HEAD, 2 * N], U8, "q_tail", tag="zero1")
         nc.sync.dma_start(out=q_tail[:].bitcast(I32), in_=q_rows[:, HEAD:E])
+
+        def entries(e0, e1):
+            return offsets[:, e0 * C // LIST : e1 * C // LIST]
 
         def gather(window, dtype, name, parts):
             slots = []
             for e0, e1 in parts:
-                part = keep.tile([P, (e1 - e0) * C], dtype, name=f"{name}{e0}", align_bytes=64)
-                nc.vector.tensor_copy(part[:], window.indirect(offsets[:, e0 * C // LIST : e1 * C // LIST]))
+                part = tile([P, (e1 - e0) * C], dtype, f"{name}{e0}")
+                nc.vector.tensor_copy(part[:], window.indirect(entries(e0, e1)))
                 slots.extend(part[:, (e - e0) * C : (e - e0 + 1) * C] for e in range(e0, e1))
             return slots
 
         slot_s = gather(x_s[:], U8, "slot_s", [(0, E)])
-        slot_w = gather(x_w[:].bitcast(U32), U32, "slot_w", PARTS)
+        slot_w = gather(x_w[:].bitcast(U32), U32, "slot_w", FIRST_PARTS)
 
-        gate_t = keep.tile([P, S], F32, name="gate_t", tag="x_s", align_bytes=64)
-        nc.sync.dma_start(out=gate_t[:], in_=gate)
-        load_scale_rows(k_s[:].bitcast(I32), wk_scales.bitcast(I32).rearrange("e s (q r) n -> r q (e s) n", r=4))
+        gate_tail = tile([P, (E - HEAD) * C], F32, "gate_tail", tag="x_s")
+        nc.sync.dma_start(out=gate_tail[:], in_=gate[:, HEAD * C : S])
+        load_scale_rows(k_s[:].bitcast(I32), weight_scale_rows(wk_scales))
 
-        def weights(b, e):
-            proj, h = divmod(b, HALVES)
-            cols = slice(h * P, (h + 1) * P)
-            if proj == 0:
-                q_w = q_head[:, e] if e < HEAD else q_tail[:, e - HEAD]
-                return q_w[:, 2 * h * P : 2 * (h + 1) * P].bitcast(FP4X4), q_s[:, e, cols]
-            if proj == 1:
-                return k_w[:, e, cols].bitcast(FP8X4), k_s[:, e, cols]
-            return v_w[:, e, cols].bitcast(FP8X4), v_s[:, e, cols]
+        def gates(e0, e1):
+            return gate_head[:, e0 * C : e1 * C] if e0 < HEAD else gate_tail[:, (e0 - HEAD) * C : (e1 - HEAD) * C]
 
-        def project(y, b, e0, e1):
+        def project(y, weights, biases, e0, e1):
             acc = psum.tile([P, (e1 - e0) * C], F32, name="acc")
             for e in range(e0, e1):
-                w_codes, w_scales = weights(b, e)
+                w_codes, w_scales = weights(e)
                 nc.tensor.matmul_mx(
                     out=acc[:, (e - e0) * C : (e - e0 + 1) * C],
                     lhsT=w_codes,
@@ -119,50 +120,66 @@ def tile_moe_qkv_kernel(tc, x_words, x_scales, wq_words, wq_scales, wk_words, wk
                     out=y[:, e * C : (e + 1) * C],
                     in_=acc[:, (e - e0) * C : (e - e0 + 1) * C],
                     func=identity,
-                    bias=(bias_q[:, b] if b < HALVES else bias_kv[:, b - HALVES])[:, e : e + 1],
+                    bias=biases[:, e : e + 1],
                 )
 
-        def scatter(y, gates, b, e0, e1):
-            cols = slice(e0 * C, e1 * C)
-            entries = offsets[:, e0 * C // LIST : e1 * C // LIST]
-            gated = keep.tile([P, (e1 - e0) * C], F32, name=f"gated{b}_{e0}", align_bytes=64)
-            nc.gpsimd.tensor_tensor(gated[:], y[:, cols], gates[:, cols], mult)
-            nc.vector.tensor_copy(windows[b % WINDOWS][:].indirect(entries), gated[:])
+        def apply_gate(gated, y, e0, e1):
+            nc.gpsimd.tensor_tensor(gated[:, e0 * C : e1 * C], y[:, e0 * C : e1 * C], gates(e0, e1), mult)
 
-        def store(b):
-            nc.sync.dma_start(out=out[b * P : (b + 1) * P, :], in_=windows[b % WINDOWS][:])
+        def scatter(gated, b, e0, e1):
+            window = windows[b % WINDOWS]
+            nc.vector.tensor_copy(window[:].indirect(entries(e0, e1)), gated[:, e0 * C : e1 * C])
+            if e1 == E:
+                nc.sync.dma_start(out=out[b * P : (b + 1) * P, :], in_=window[:])
 
-        ys = [keep.tile([P, S], F32, name=f"y{b}", tag=f"y{b}", align_bytes=64) for b in range(3)]
-        for part in PARTS:
-            for b in (0, 1):
-                project(ys[b], b, *part)
-        k_w = keep.tile([P, E, N], I32, name="k_w", tag="q_head", align_bytes=64)
-        nc.sync.dma_start(out=k_w[:], in_=wk_words.rearrange("e s p n d -> p (e s) (n d)").bitcast(I32))
-        bias_kv = keep.tile([P, BLOCKS - HALVES, 8], F32, name="bias_kv", tag="zero1", align_bytes=64)
-        nc.sync.dma_start(out=bias_kv[:, :, 0:E], in_=bias_rows[:, HALVES:BLOCKS])
+        def q_weights(e, h):
+            words = q_head[:, e] if e < HEAD else q_tail[:, e - HEAD]
+            return words[:, 2 * h * P : 2 * (h + 1) * P].bitcast(FP4X4), q_s[:, e, h * P : (h + 1) * P]
+
+        y_q = [tile([P, S], F32, f"y_q{h}") for h in range(HALVES)]
+        gated_q = [tile([P, S], F32, f"gated_q{h}") for h in range(HALVES)]
+        for part in FIRST_PARTS:
+            for h in range(HALVES):
+                project(y_q[h], lambda e: q_weights(e, h), bias_q[:, h], *part)
+                apply_gate(gated_q[h], y_q[h], *part)
 
         def load_v(e0, tag):
-            raw = keep.tile([P, QUANT, PACK, N], F32, name=f"v_raw{e0}", tag=tag, align_bytes=64)
+            raw = tile([P, QUANT, PACK, N], F32, f"v_raw{e0}", tag=tag)
             nc.sync.dma_start(out=raw[:], in_=wv[e0 : e0 + QUANT].rearrange("e (p j) n -> p e j n", j=PACK))
             return raw
 
-        v_raw = [load_v(0, "q_s")]
-        for b in (0, 1):
-            scatter(ys[b], gate_head, b, *PARTS[0])
-        v_raw.append(load_v(2, "zero0"))
-        scatter(ys[0], gate_t, 0, *PARTS[1])
-        v_raw.append(load_v(4, "y0"))
-        store(0)
-        scatter(ys[1], gate_t, 1, *PARTS[1])
-        store(1)
+        v_raw = [load_v(0, "q_head")]
+        k_w = tile([P, E, N], I32, "k_w", tag="seed0")
+        nc.sync.dma_start(out=k_w[:], in_=wk_words.rearrange("e s p n d -> p (e s) (n d)").bitcast(I32))
+        bias_kv = tile([P, 2 * HALVES, 8], F32, "bias_kv", tag="zero1")
+        nc.sync.dma_start(out=bias_kv[:, :, 0:E], in_=bias_rows[:, HALVES : 3 * HALVES])
+        v_raw.append(load_v(2, "q_s"))
+        v_raw.append(load_v(4, "seed1"))
 
-        for part in PARTS:
-            project(ys[2], 2, *part)
-        scatter(ys[2], gate_t, 2, 0, E)
-        store(2)
+        for part in FIRST_PARTS:
+            for h in range(HALVES):
+                scatter(gated_q[h], h, *part)
 
+        def k_weights(e, h):
+            return k_w[:, e, h * P : (h + 1) * P].bitcast(FP8X4), k_s[:, e, h * P : (h + 1) * P]
+
+        y_k = [tile([P, S], F32, f"y_k{h}") for h in range(HALVES)]
+        for h in range(HALVES):
+            for part in PARTS:
+                project(y_k[h], lambda e: k_weights(e, h), bias_kv[:, h], *part)
+
+        def finish(y, b, tag=None):
+            gated = tile([P, S], F32, f"gated{b}", tag=tag)
+            for part in PARTS:
+                apply_gate(gated, y, *part)
+            scatter(gated, b, 0, E)
+
+        finish(y_k[0], 2)
+
+        v_w = tile([P, E, N], U32, "v_w")
+        v_s = tile([P, E, N], U8, "v_s")
         for raw, e0 in zip(v_raw, range(0, E, QUANT)):
-            grouped = keep.tile([P, QUANT, N, PACK], BF16, name=f"grouped{e0}", align_bytes=64)
+            grouped = tile([P, QUANT, N, PACK], BF16, f"grouped{e0}")
             for e in range(QUANT):
                 nc.scalar.copy(
                     out=grouped[:, e].rearrange("p (c i) t -> p c t i", i=4),
@@ -174,18 +191,13 @@ def tile_moe_qkv_kernel(tc, x_words, x_scales, wq_words, wq_scales, wk_words, wk
                 in_=grouped[:].rearrange("p e n t -> p (e n t)"),
             )
 
-        y_3 = keep.tile([P, S], F32, name="y3", tag="y0", align_bytes=64)
-        for part in PARTS:
-            project(y_3, 3, *part)
-        scatter(y_3, gate_t, 3, 0, E)
-        store(3)
+        finish(y_k[1], 3, tag="seed1")
 
-        y_v = keep.tile([P, HALVES, S], F32, name="y_v", tag="y0", align_bytes=64)
-        for part in PARTS:
-            for b in (4, 5):
-                project(y_v[:, b - 4], b, *part)
-        for part in PARTS:
-            for b in (4, 5):
-                scatter(y_v[:, b - 4], gate_t, b, *part)
-        store(4)
-        store(5)
+        def v_weights(e, h):
+            return v_w[:, e, h * P : (h + 1) * P].bitcast(FP8X4), v_s[:, e, h * P : (h + 1) * P]
+
+        y_v = tile([P, HALVES, S], F32, "y_v", tag=f"grouped{E - QUANT}")
+        for h in range(HALVES):
+            for part in PARTS:
+                project(y_v[:, h], lambda e: v_weights(e, h), bias_kv[:, HALVES + h], *part)
+            finish(y_v[:, h], 4 + h)

@@ -1,6 +1,7 @@
 from contextlib import ExitStack
 
 import concourse.mybir as mybir
+from concourse.masks import make_identity
 
 K, T, E, C, N = 512, 1024, 6, 128, 256
 FLOPS = 2 * K * 3 * N * E * C
@@ -21,7 +22,6 @@ LIST = 16
 HALVES = N // P
 HEAD = 2
 PARTS = ((0, HEAD), (HEAD, E))
-FIRST_PARTS = ((0, 1), (1, HEAD), (HEAD, E))
 WINDOWS = 3
 QUANT = 2
 
@@ -33,7 +33,8 @@ def tile_moe_qkv_kernel(tc, x_words, x_scales, wq_words, wq_scales, wk_words, wk
 
     with ExitStack() as ctx:
         keep = ctx.enter_context(tc.tile_pool(name="keep", bufs=1))
-        psum = ctx.enter_context(tc.psum_pool(name="psum", bufs=8))
+        psum = ctx.enter_context(tc.psum_pool(name="psum", bufs=4))
+        turns = ctx.enter_context(tc.psum_pool(name="turns", bufs=2))
 
         def tile(shape, dtype, name, tag=None):
             return keep.tile(shape, dtype, name=name, tag=tag or name, align_bytes=64)
@@ -51,6 +52,9 @@ def tile_moe_qkv_kernel(tc, x_words, x_scales, wq_words, wq_scales, wk_words, wk
         nc.vector.memset(x_s[:].bitcast(I32), 0)
         for seed, zero in zip(seeds, zeros):
             nc.vector.tensor_copy(zero[:], seed[:])
+        eye = tile([P, P], F32, "eye")
+        nc.vector.memset(eye[:], 0.0)
+        make_identity(nc, eye[:], nomemset=True)
         nc.vector.memset(q_s[:].bitcast(I32), 0)
         nc.vector.memset(windows[0][:], 0.0)
         nc.vector.memset(k_s[:].bitcast(I32), 0)
@@ -76,8 +80,8 @@ def tile_moe_qkv_kernel(tc, x_words, x_scales, wq_words, wq_scales, wk_words, wk
         load_scale_rows(q_s[:].bitcast(I32), weight_scale_rows(wq_scales))
         bias_q = tile([P, HALVES, 8], F32, "bias_q", tag="seed1")
         nc.sync.dma_start(out=bias_q[:, :, 0:E], in_=bias_rows[:, 0:HALVES])
-        gate_head = tile([P, HEAD * C], F32, "gate_head", tag="zero0")
-        nc.sync.dma_start(out=gate_head[:], in_=gate[:, 0 : HEAD * C])
+        gates = tile([P, S], F32, "gates", tag="zero0")
+        nc.sync.dma_start(out=gates[:], in_=gate)
         q_tail = tile([P, E - HEAD, 2 * N], U8, "q_tail", tag="zero1")
         nc.sync.dma_start(out=q_tail[:].bitcast(I32), in_=q_rows[:, HEAD:E])
 
@@ -93,17 +97,19 @@ def tile_moe_qkv_kernel(tc, x_words, x_scales, wq_words, wq_scales, wk_words, wk
             return slots
 
         slot_s = gather(x_s[:], U8, "slot_s", [(0, E)])
-        slot_w = gather(x_w[:].bitcast(U32), U32, "slot_w", FIRST_PARTS)
+        slot_w = gather(x_w[:].bitcast(U32), U32, "slot_w", PARTS)
 
-        gate_tail = tile([P, (E - HEAD) * C], F32, "gate_tail", tag="x_s")
-        nc.sync.dma_start(out=gate_tail[:], in_=gate[:, HEAD * C : S])
+        def load_v(e0, tag):
+            raw = tile([P, QUANT, PACK, N], F32, f"v_raw{e0}", tag=tag)
+            nc.sync.dma_start(out=raw[:], in_=wv[e0 : e0 + QUANT].rearrange("e (p j) n -> p e j n", j=PACK))
+            return raw
+
+        v_raw = [load_v(0, "x_s")]
         load_scale_rows(k_s[:].bitcast(I32), weight_scale_rows(wk_scales))
 
-        def gates(e0, e1):
-            return gate_head[:, e0 * C : e1 * C] if e0 < HEAD else gate_tail[:, (e0 - HEAD) * C : (e1 - HEAD) * C]
 
-        def project(y, weights, biases, e0, e1):
-            acc = psum.tile([P, (e1 - e0) * C], F32, name="acc")
+        def project(y, weights, biases, e0, e1, late=False):
+            acc = turns.tile([P, (e1 - e0) * C], F32, name="back") if late else psum.tile([P, (e1 - e0) * C], F32, name="acc")
             for e in range(e0, e1):
                 w_codes, w_scales = weights(e)
                 nc.tensor.matmul_mx(
@@ -123,58 +129,65 @@ def tile_moe_qkv_kernel(tc, x_words, x_scales, wq_words, wq_scales, wk_words, wk
                     bias=biases[:, e : e + 1],
                 )
 
-        def apply_gate(gated, y, e0, e1):
-            nc.gpsimd.tensor_tensor(gated[:, e0 * C : e1 * C], y[:, e0 * C : e1 * C], gates(e0, e1), mult)
-
-        def scatter(gated, b, e0, e1):
-            window = windows[b % WINDOWS]
-            nc.vector.tensor_copy(window[:].indirect(entries(e0, e1)), gated[:, e0 * C : e1 * C])
-            if e1 == E:
-                nc.sync.dma_start(out=out[b * P : (b + 1) * P, :], in_=window[:])
+        def store(b):
+            nc.sync.dma_start(out=out[b * P : (b + 1) * P, :], in_=windows[b % WINDOWS][:])
 
         def q_weights(e, h):
             words = q_head[:, e] if e < HEAD else q_tail[:, e - HEAD]
             return words[:, 2 * h * P : 2 * (h + 1) * P].bitcast(FP4X4), q_s[:, e, h * P : (h + 1) * P]
 
         y_q = [tile([P, S], F32, f"y_q{h}") for h in range(HALVES)]
-        gated_q = [tile([P, S], F32, f"gated_q{h}") for h in range(HALVES)]
-        for part in FIRST_PARTS:
+        for part in PARTS:
             for h in range(HALVES):
                 project(y_q[h], lambda e: q_weights(e, h), bias_q[:, h], *part)
-                apply_gate(gated_q[h], y_q[h], *part)
 
-        def load_v(e0, tag):
-            raw = tile([P, QUANT, PACK, N], F32, f"v_raw{e0}", tag=tag)
-            nc.sync.dma_start(out=raw[:], in_=wv[e0 : e0 + QUANT].rearrange("e (p j) n -> p e j n", j=PACK))
-            return raw
-
-        v_raw = [load_v(0, "q_head")]
-        k_w = tile([P, E, N], I32, "k_w", tag="seed0")
+        k_w = tile([P, E, N], I32, "k_w", tag="q_head")
         nc.sync.dma_start(out=k_w[:], in_=wk_words.rearrange("e s p n d -> p (e s) (n d)").bitcast(I32))
         bias_kv = tile([P, 2 * HALVES, 8], F32, "bias_kv", tag="zero1")
         nc.sync.dma_start(out=bias_kv[:, :, 0:E], in_=bias_rows[:, HALVES : 3 * HALVES])
-        v_raw.append(load_v(2, "q_s"))
-        v_raw.append(load_v(4, "seed1"))
+        slot_gate = tile([P, 8], F32, "slot_gate", tag="seed0")
+        with nc.allow_non_contiguous_dma(reason="one gate value a partition and expert"):
+            nc.sync.dma_start(out=slot_gate[:, 0:E], in_=gate[0].rearrange("(e p) -> p e", p=P))
+        v_raw.extend([load_v(2, "q_s"), load_v(4, "seed1")])
 
-        for part in FIRST_PARTS:
+        for e0, e1 in PARTS:
             for h in range(HALVES):
-                scatter(gated_q[h], h, *part)
+                nc.vector.tensor_tensor(windows[h][:].indirect(entries(e0, e1)), y_q[h][:, e0 * C : e1 * C], gates[:, e0 * C : e1 * C], mult)
+        for h in range(HALVES):
+            store(h)
+
+        def gate_part(weights, biases, name, e0, e1, late=False):
+            ys = [tile([P, S], F32, f"y_{name}{e0}_{h}") for h in range(HALVES)]
+            for h in range(HALVES):
+                project(ys[h], lambda e: weights(e, h), biases[:, h], e0, e1, late)
+            back = [turns.tile([P, (e1 - e0) * C], F32, name="back") for h in range(HALVES)]
+            for e in range(e0, e1):
+                turned = turns.tile([P, N], F32, name="turned")
+                for h in range(HALVES):
+                    nc.tensor.transpose(turned[:, h * P : (h + 1) * P], ys[h][:, e * C : (e + 1) * C], eye[:])
+                by_slot = tile([P, N], F32, f"by_slot_{name}{e}")
+                nc.scalar.activation(out=by_slot[:], in_=turned[:], func=identity, scale=slot_gate[:, e : e + 1])
+                for h in range(HALVES):
+                    nc.tensor.transpose(back[h][:, (e - e0) * C : (e - e0 + 1) * C], by_slot[:, h * P : (h + 1) * P], eye[:])
+            return back
+
+        def take_back(back, name, tag=None):
+            gated = tile(list(back.shape), F32, name, tag=tag)
+            nc.scalar.copy(out=gated[:], in_=back[:])
+            return gated
+
+        def scatter(gated, b, e0, e1):
+            nc.vector.tensor_copy(windows[b % WINDOWS][:].indirect(entries(e0, e1)), gated[:])
+            if e1 == E:
+                store(b)
 
         def k_weights(e, h):
             return k_w[:, e, h * P : (h + 1) * P].bitcast(FP8X4), k_s[:, e, h * P : (h + 1) * P]
 
-        y_k = [tile([P, S], F32, f"y_k{h}") for h in range(HALVES)]
+        back = gate_part(k_weights, bias_kv[:, 0:HALVES], "k", 0, HEAD)
         for h in range(HALVES):
-            for part in PARTS:
-                project(y_k[h], lambda e: k_weights(e, h), bias_kv[:, h], *part)
-
-        def finish(y, b, tag=None):
-            gated = tile([P, S], F32, f"gated{b}", tag=tag)
-            for part in PARTS:
-                apply_gate(gated, y, *part)
-            scatter(gated, b, 0, E)
-
-        finish(y_k[0], 2)
+            scatter(take_back(back[h], f"gated_k0_{h}"), HALVES + h, 0, HEAD)
+        back = gate_part(k_weights, bias_kv[:, 0:HALVES], "k", HEAD, E)
 
         v_w = tile([P, E, N], U32, "v_w")
         v_s = tile([P, E, N], U8, "v_s")
@@ -191,13 +204,13 @@ def tile_moe_qkv_kernel(tc, x_words, x_scales, wq_words, wq_scales, wk_words, wk
                 in_=grouped[:].rearrange("p e n t -> p (e n t)"),
             )
 
-        finish(y_k[1], 3, tag="seed1")
+        for h, tag in enumerate(("q_s", "seed1")):
+            scatter(take_back(back[h], f"gated_k2_{h}", tag=tag), HALVES + h, HEAD, E)
 
         def v_weights(e, h):
             return v_w[:, e, h * P : (h + 1) * P].bitcast(FP8X4), v_s[:, e, h * P : (h + 1) * P]
 
-        y_v = tile([P, HALVES, S], F32, "y_v", tag=f"grouped{E - QUANT}")
-        for h in range(HALVES):
-            for part in PARTS:
-                project(y_v[:, h], lambda e: v_weights(e, h), bias_kv[:, HALVES + h], *part)
-            finish(y_v[:, h], 4 + h)
+        for e0, e1 in PARTS:
+            back = gate_part(v_weights, bias_kv[:, HALVES : 2 * HALVES], "v", e0, e1, late=e0 == 0)
+            for h in range(HALVES):
+                scatter(take_back(back[h], f"gated_v{e0}_{h}"), 2 * HALVES + h, e0, e1)

@@ -104,12 +104,12 @@ def tile_moe_qkv_kernel(tc, x_words, x_scales, wq_words, wq_scales, wk_words, wk
             nc.sync.dma_start(out=raw[:], in_=wv[e0 : e0 + QUANT].rearrange("e (p j) n -> p e j n", j=PACK))
             return raw
 
-        v_raw = [load_v(0, "x_s")]
+        v_raw = [load_v(2, "x_s")]
         load_scale_rows(k_s[:].bitcast(I32), weight_scale_rows(wk_scales))
 
 
-        def project(y, weights, biases, e0, e1, late=False):
-            acc = turns.tile([P, (e1 - e0) * C], F32, name="back") if late else psum.tile([P, (e1 - e0) * C], F32, name="acc")
+        def project(y, weights, biases, e0, e1):
+            acc = psum.tile([P, (e1 - e0) * C], F32, name="acc")
             for e in range(e0, e1):
                 w_codes, w_scales = weights(e)
                 nc.tensor.matmul_mx(
@@ -148,7 +148,7 @@ def tile_moe_qkv_kernel(tc, x_words, x_scales, wq_words, wq_scales, wk_words, wk
         slot_gate = tile([P, 8], F32, "slot_gate", tag="seed0")
         with nc.allow_non_contiguous_dma(reason="one gate value a partition and expert"):
             nc.sync.dma_start(out=slot_gate[:, 0:E], in_=gate[0].rearrange("(e p) -> p e", p=P))
-        v_raw.extend([load_v(2, "q_s"), load_v(4, "seed1")])
+        v_raw.extend([load_v(4, "q_s"), load_v(0, "seed1")])
 
         for e0, e1 in PARTS:
             for h in range(HALVES):
@@ -156,24 +156,25 @@ def tile_moe_qkv_kernel(tc, x_words, x_scales, wq_words, wq_scales, wk_words, wk
         for h in range(HALVES):
             store(h)
 
-        def gate_part(weights, biases, name, e0, e1, late=False):
+        def gate_part(weights, biases, name, e0, e1):
             ys = [tile([P, S], F32, f"y_{name}{e0}_{h}") for h in range(HALVES)]
             for h in range(HALVES):
-                project(ys[h], lambda e: weights(e, h), biases[:, h], e0, e1, late)
-            back = [turns.tile([P, (e1 - e0) * C], F32, name="back") for h in range(HALVES)]
-            for e in range(e0, e1):
-                turned = turns.tile([P, N], F32, name="turned")
-                for h in range(HALVES):
-                    nc.tensor.transpose(turned[:, h * P : (h + 1) * P], ys[h][:, e * C : (e + 1) * C], eye[:])
-                by_slot = tile([P, N], F32, f"by_slot_{name}{e}")
-                nc.scalar.activation(out=by_slot[:], in_=turned[:], func=identity, scale=slot_gate[:, e : e + 1])
-                for h in range(HALVES):
-                    nc.tensor.transpose(back[h][:, (e - e0) * C : (e - e0 + 1) * C], by_slot[:, h * P : (h + 1) * P], eye[:])
-            return back
-
-        def take_back(back, name, tag=None):
-            gated = tile(list(back.shape), F32, name, tag=tag)
-            nc.scalar.copy(out=gated[:], in_=back[:])
+                project(ys[h], lambda e: weights(e, h), biases[:, h], e0, e1)
+            by_slot = tile([P, e1 - e0, N], F32, f"by_slot_{name}{e0}")
+            for pair in range(e0, e1, 2):
+                turned = turns.tile([P, 2, N], F32, name="turned")
+                for e in (pair, pair + 1):
+                    for h in range(HALVES):
+                        nc.tensor.transpose(turned[:, e - pair, h * P : (h + 1) * P], ys[h][:, e * C : (e + 1) * C], eye[:])
+                for e in (pair, pair + 1):
+                    nc.scalar.activation(out=by_slot[:, e - e0], in_=turned[:, e - pair], func=identity, scale=slot_gate[:, e : e + 1])
+            gated = []
+            for h in range(HALVES):
+                back = turns.tile([P, (e1 - e0) * C], F32, name="back")
+                for e in range(e0, e1):
+                    nc.tensor.transpose(back[:, (e - e0) * C : (e - e0 + 1) * C], by_slot[:, e - e0, h * P : (h + 1) * P], eye[:])
+                gated.append(tile([P, (e1 - e0) * C], F32, f"gated_{name}{e0}_{h}"))
+                nc.scalar.copy(out=gated[h][:], in_=back[:])
             return gated
 
         def scatter(gated, b, e0, e1):
@@ -184,14 +185,19 @@ def tile_moe_qkv_kernel(tc, x_words, x_scales, wq_words, wq_scales, wk_words, wk
         def k_weights(e, h):
             return k_w[:, e, h * P : (h + 1) * P].bitcast(FP8X4), k_s[:, e, h * P : (h + 1) * P]
 
-        back = gate_part(k_weights, bias_kv[:, 0:HALVES], "k", 0, HEAD)
+        def key_part(y, h, e0, e1):
+            project(y, lambda e: k_weights(e, h), bias_kv[:, h], e0, e1)
+            b = HALVES + h
+            nc.vector.tensor_tensor(windows[b % WINDOWS][:].indirect(entries(e0, e1)), y[:, e0 * C : e1 * C], gates[:, e0 * C : e1 * C], mult)
+            if e1 == E:
+                store(b)
+
         for h in range(HALVES):
-            scatter(take_back(back[h], f"gated_k0_{h}"), HALVES + h, 0, HEAD)
-        back = gate_part(k_weights, bias_kv[:, 0:HALVES], "k", HEAD, E)
+            key_part(tile([P, S], F32, f"y_k{h}"), h, 0, HEAD)
 
         v_w = tile([P, E, N], U32, "v_w")
         v_s = tile([P, E, N], U8, "v_s")
-        for raw, e0 in zip(v_raw, range(0, E, QUANT)):
+        for raw, e0 in zip(v_raw, (2, 4, 0)):
             grouped = tile([P, QUANT, N, PACK], BF16, f"grouped{e0}")
             for e in range(QUANT):
                 nc.scalar.copy(
@@ -204,13 +210,14 @@ def tile_moe_qkv_kernel(tc, x_words, x_scales, wq_words, wq_scales, wk_words, wk
                 in_=grouped[:].rearrange("p e n t -> p (e n t)"),
             )
 
-        for h, tag in enumerate(("q_s", "seed1")):
-            scatter(take_back(back[h], f"gated_k2_{h}", tag=tag), HALVES + h, HEAD, E)
+        y_tail = tile([P, HALVES, S], F32, "y_tail", tag="seed1")
+        key_part(y_tail[:, 0], 0, HEAD, E)
+        key_part(y_tail[:, 1], 1, HEAD, E)
 
         def v_weights(e, h):
             return v_w[:, e, h * P : (h + 1) * P].bitcast(FP8X4), v_s[:, e, h * P : (h + 1) * P]
 
         for e0, e1 in PARTS:
-            back = gate_part(v_weights, bias_kv[:, HALVES : 2 * HALVES], "v", e0, e1, late=e0 == 0)
+            gated = gate_part(v_weights, bias_kv[:, HALVES : 2 * HALVES], "v", e0, e1)
             for h in range(HALVES):
-                scatter(take_back(back[h], f"gated_v{e0}_{h}"), 2 * HALVES + h, e0, e1)
+                scatter(gated[h], 2 * HALVES + h, e0, e1)

@@ -43,23 +43,25 @@ def tile_moe_qkv_kernel(tc, x_words, x_scales, wq_words, wq_scales, wk_words, wk
         x_s = tile([P, T], U8, "x_s")
         q_s = tile([P, E, N], U8, "q_s")
         k_s = tile([P, E, N], U8, "k_s")
-        seeds = [tile([P, 8], F32, f"seed{i}") for i in range(WINDOWS - 1)]
+        seeds = [tile([P, 8], F32, f"seed{i}") for i in range(3)]
         zeros = [tile([P, 8], F32, f"zero{i}") for i in range(WINDOWS - 1)]
         windows = [tile([P, T], F32, f"window{i}") for i in range(WINDOWS)]
 
+        nc.vector.memset(x_s[:].bitcast(I32), 0)
         for seed in seeds:
             nc.vector.memset(seed[:], 0.0)
-        nc.vector.memset(x_s[:].bitcast(I32), 0)
         for seed, zero in zip(seeds, zeros):
             nc.vector.tensor_copy(zero[:], seed[:])
         eye = tile([P, P], F32, "eye")
-        nc.vector.memset(eye[:], 0.0)
+        nc.vector.tensor_copy(eye[:], seeds[2][:, 0:1].to_broadcast([P, P]))
         make_identity(nc, eye[:], nomemset=True)
         nc.vector.memset(q_s[:].bitcast(I32), 0)
-        nc.vector.memset(windows[0][:], 0.0)
         nc.vector.memset(k_s[:].bitcast(I32), 0)
-        for w, zero in zip(windows[1:], zeros):
+        kv_rows = tile([P, P * E], F32, "kv_rows")
+        nc.vector.memset(kv_rows[:], 0.0)
+        for w, zero in zip(windows, zeros):
             nc.scalar.copy(out=w[:], in_=zero[:, 0:1].to_broadcast([P, T]))
+        nc.scalar.copy(out=windows[2][:], in_=windows[0][:])
 
         def load_scale_rows(plane, rows):
             for r in range(4):
@@ -72,13 +74,13 @@ def tile_moe_qkv_kernel(tc, x_words, x_scales, wq_words, wq_scales, wk_words, wk
         bias_rows = bias.rearrange("(b p) e -> p b e", p=P)
 
         nc.sync.dma_start(offsets[:], offs)
-        q_head = tile([P, HEAD, 2 * N], U8, "q_head")
-        nc.sync.dma_start(out=q_head[:].bitcast(I32), in_=q_rows[:, 0:HEAD])
         load_scale_rows(x_s[:].bitcast(I32), x_scales[0].bitcast(I32).rearrange("(q r) t -> r q t", r=4))
         x_w = tile([P, T], I32, "x_w", tag="seed0")
         nc.sync.dma_start(out=x_w[:], in_=x_words[0].rearrange("p t d -> p (t d)").bitcast(I32))
+        q_head = tile([P, HEAD, 2 * N], U8, "q_head", tag="seed1")
+        nc.sync.dma_start(out=q_head[:].bitcast(I32), in_=q_rows[:, 0:HEAD])
         load_scale_rows(q_s[:].bitcast(I32), weight_scale_rows(wq_scales))
-        bias_q = tile([P, HALVES, 8], F32, "bias_q", tag="seed1")
+        bias_q = tile([P, HALVES, 8], F32, "bias_q", tag="seed2")
         nc.sync.dma_start(out=bias_q[:, :, 0:E], in_=bias_rows[:, 0:HALVES])
         gates = tile([P, S], F32, "gates", tag="zero0")
         nc.sync.dma_start(out=gates[:], in_=gate)
@@ -106,6 +108,7 @@ def tile_moe_qkv_kernel(tc, x_words, x_scales, wq_words, wq_scales, wk_words, wk
 
         v_raw = [load_v(2, "x_s")]
         load_scale_rows(k_s[:].bitcast(I32), weight_scale_rows(wk_scales))
+        nc.sync.dma_start(out=kv_rows[0 : 2 * HALVES], in_=bias[N : 3 * N].rearrange("(b p) e -> b (p e)", p=P))
 
 
         def project(y, weights, biases, e0, e1):
@@ -126,7 +129,7 @@ def tile_moe_qkv_kernel(tc, x_words, x_scales, wq_words, wq_scales, wk_words, wk
                     out=y[:, e * C : (e + 1) * C],
                     in_=acc[:, (e - e0) * C : (e - e0 + 1) * C],
                     func=identity,
-                    bias=biases[:, e : e + 1],
+                    bias=biases(e),
                 )
 
         def store(b):
@@ -139,16 +142,23 @@ def tile_moe_qkv_kernel(tc, x_words, x_scales, wq_words, wq_scales, wk_words, wk
         y_q = [tile([P, S], F32, f"y_q{h}") for h in range(HALVES)]
         for part in PARTS:
             for h in range(HALVES):
-                project(y_q[h], lambda e: q_weights(e, h), bias_q[:, h], *part)
+                project(y_q[h], lambda e: q_weights(e, h), lambda e: bias_q[:, h, e : e + 1], *part)
 
-        k_w = tile([P, E, N], I32, "k_w", tag="q_head")
+        k_w = tile([P, E, N], I32, "k_w", tag="seed1")
         nc.sync.dma_start(out=k_w[:], in_=wk_words.rearrange("e s p n d -> p (e s) (n d)").bitcast(I32))
-        bias_kv = tile([P, 2 * HALVES, 8], F32, "bias_kv", tag="zero1")
-        nc.sync.dma_start(out=bias_kv[:, :, 0:E], in_=bias_rows[:, HALVES : 3 * HALVES])
-        slot_gate = tile([P, 8], F32, "slot_gate", tag="seed0")
-        with nc.allow_non_contiguous_dma(reason="one gate value a partition and expert"):
-            nc.sync.dma_start(out=slot_gate[:, 0:E], in_=gate[0].rearrange("(e p) -> p e", p=P))
-        v_raw.extend([load_v(4, "q_s"), load_v(0, "seed1")])
+        bias_kv = tile([P, E, 2 * HALVES], F32, "bias_kv")
+        for e0 in (0, E // 2):
+            turned = psum.tile([P, E // 2, P], F32, name="acc")
+            for e in range(E // 2):
+                nc.tensor.transpose(turned[:, e], kv_rows[:, e0 + e : P * E : E], eye[:])
+            nc.scalar.copy(out=bias_kv[:, e0 : e0 + E // 2], in_=turned[:, :, 0 : 2 * HALVES])
+        slot_gate = tile([P, E], F32, "slot_gate")
+        for e0 in (0, E // 2):
+            turned = psum.tile([P, E // 2, C], F32, name="acc")
+            for e in range(E // 2):
+                nc.tensor.transpose(turned[:, e], gates[:, (e0 + e) * C : (e0 + e + 1) * C], eye[:])
+            nc.scalar.copy(out=slot_gate[:, e0 : e0 + E // 2], in_=turned[:, :, 0])
+        v_raw.extend([load_v(4, "q_s"), load_v(0, "seed2")])
 
         for e0, e1 in PARTS:
             for h in range(HALVES):
@@ -159,7 +169,7 @@ def tile_moe_qkv_kernel(tc, x_words, x_scales, wq_words, wq_scales, wk_words, wk
         def gate_part(weights, biases, name, e0, e1):
             ys = [tile([P, S], F32, f"y_{name}{e0}_{h}") for h in range(HALVES)]
             for h in range(HALVES):
-                project(ys[h], lambda e: weights(e, h), biases[:, h], e0, e1)
+                project(ys[h], lambda e: weights(e, h), lambda e: biases[:, e, h : h + 1], e0, e1)
             by_slot = tile([P, e1 - e0, N], F32, f"by_slot_{name}{e0}")
             for pair in range(e0, e1, 2):
                 turned = turns.tile([P, 2, N], F32, name="turned")
@@ -186,7 +196,7 @@ def tile_moe_qkv_kernel(tc, x_words, x_scales, wq_words, wq_scales, wk_words, wk
             return k_w[:, e, h * P : (h + 1) * P].bitcast(FP8X4), k_s[:, e, h * P : (h + 1) * P]
 
         def key_part(y, h, e0, e1):
-            project(y, lambda e: k_weights(e, h), bias_kv[:, h], e0, e1)
+            project(y, lambda e: k_weights(e, h), lambda e: bias_kv[:, e, h : h + 1], e0, e1)
             b = HALVES + h
             nc.vector.tensor_tensor(windows[b % WINDOWS][:].indirect(entries(e0, e1)), y[:, e0 * C : e1 * C], gates[:, e0 * C : e1 * C], mult)
             if e1 == E:
@@ -210,7 +220,7 @@ def tile_moe_qkv_kernel(tc, x_words, x_scales, wq_words, wq_scales, wk_words, wk
                 in_=grouped[:].rearrange("p e n t -> p (e n t)"),
             )
 
-        y_tail = tile([P, HALVES, S], F32, "y_tail", tag="seed1")
+        y_tail = tile([P, HALVES, S], F32, "y_tail", tag="seed2")
         key_part(y_tail[:, 0], 0, HEAD, E)
         key_part(y_tail[:, 1], 1, HEAD, E)
 
@@ -218,6 +228,6 @@ def tile_moe_qkv_kernel(tc, x_words, x_scales, wq_words, wq_scales, wk_words, wk
             return v_w[:, e, h * P : (h + 1) * P].bitcast(FP8X4), v_s[:, e, h * P : (h + 1) * P]
 
         for e0, e1 in PARTS:
-            gated = gate_part(v_weights, bias_kv[:, HALVES : 2 * HALVES], "v", e0, e1)
+            gated = gate_part(v_weights, bias_kv[:, :, HALVES : 2 * HALVES], "v", e0, e1)
             for h in range(HALVES):
                 scatter(gated[h], 2 * HALVES + h, e0, e1)

@@ -152,12 +152,6 @@ def tile_moe_qkv_kernel(tc, x_words, x_scales, wq_words, wq_scales, wk_words, wk
             for e in range(E // 2):
                 nc.tensor.transpose(turned[:, e], kv_rows[:, e0 + e : P * E : E], eye[:])
             nc.scalar.copy(out=bias_kv[:, e0 : e0 + E // 2], in_=turned[:, :, 0 : 2 * HALVES])
-        slot_gate = tile([P, E], F32, "slot_gate")
-        for e0 in (0, E // 2):
-            turned = psum.tile([P, E // 2, C], F32, name="acc")
-            for e in range(E // 2):
-                nc.tensor.transpose(turned[:, e], gates[:, (e0 + e) * C : (e0 + e + 1) * C], eye[:])
-            nc.scalar.copy(out=slot_gate[:, e0 : e0 + E // 2], in_=turned[:, :, 0])
         v_raw.extend([load_v(4, "q_s"), load_v(0, "seed2")])
 
         for e0, e1 in PARTS:
@@ -166,38 +160,12 @@ def tile_moe_qkv_kernel(tc, x_words, x_scales, wq_words, wq_scales, wk_words, wk
         for h in range(HALVES):
             store(h)
 
-        def gate_part(weights, biases, name, e0, e1):
-            ys = [tile([P, S], F32, f"y_{name}{e0}_{h}") for h in range(HALVES)]
-            for h in range(HALVES):
-                project(ys[h], lambda e: weights(e, h), lambda e: biases[:, e, h : h + 1], e0, e1)
-            by_slot = tile([P, e1 - e0, N], F32, f"by_slot_{name}{e0}")
-            for pair in range(e0, e1, 2):
-                turned = turns.tile([P, 2, N], F32, name="turned")
-                for e in (pair, pair + 1):
-                    for h in range(HALVES):
-                        nc.tensor.transpose(turned[:, e - pair, h * P : (h + 1) * P], ys[h][:, e * C : (e + 1) * C], eye[:])
-                for e in (pair, pair + 1):
-                    nc.scalar.activation(out=by_slot[:, e - e0], in_=turned[:, e - pair], func=identity, scale=slot_gate[:, e : e + 1])
-            gated = []
-            for h in range(HALVES):
-                back = turns.tile([P, (e1 - e0) * C], F32, name="back")
-                for e in range(e0, e1):
-                    nc.tensor.transpose(back[:, (e - e0) * C : (e - e0 + 1) * C], by_slot[:, e - e0, h * P : (h + 1) * P], eye[:])
-                gated.append(tile([P, (e1 - e0) * C], F32, f"gated_{name}{e0}_{h}"))
-                nc.scalar.copy(out=gated[h][:], in_=back[:])
-            return gated
-
-        def scatter(gated, b, e0, e1):
-            nc.vector.tensor_copy(windows[b % WINDOWS][:].indirect(entries(e0, e1)), gated[:])
-            if e1 == E:
-                store(b)
-
         def k_weights(e, h):
             return k_w[:, e, h * P : (h + 1) * P].bitcast(FP8X4), k_s[:, e, h * P : (h + 1) * P]
 
         def key_part(y, h, e0, e1):
-            project(y, lambda e: k_weights(e, h), lambda e: bias_kv[:, e, h : h + 1], e0, e1)
             b = HALVES + h
+            project(y, lambda e: k_weights(e, h), lambda e: bias_kv[:, e, h : h + 1], e0, e1)
             nc.vector.tensor_tensor(windows[b % WINDOWS][:].indirect(entries(e0, e1)), y[:, e0 * C : e1 * C], gates[:, e0 * C : e1 * C], mult)
             if e1 == E:
                 store(b)
@@ -227,7 +195,11 @@ def tile_moe_qkv_kernel(tc, x_words, x_scales, wq_words, wq_scales, wk_words, wk
         def v_weights(e, h):
             return v_w[:, e, h * P : (h + 1) * P].bitcast(FP8X4), v_s[:, e, h * P : (h + 1) * P]
 
+        y_v = [tile([P, S], F32, f"y_v{h}") for h in range(HALVES)]
         for e0, e1 in PARTS:
-            gated = gate_part(v_weights, bias_kv[:, :, HALVES : 2 * HALVES], "v", e0, e1)
             for h in range(HALVES):
-                scatter(gated[h], 2 * HALVES + h, e0, e1)
+                project(y_v[h], lambda e: v_weights(e, h), lambda e: bias_kv[:, e, HALVES + h : HALVES + h + 1], e0, e1)
+        for h in range(HALVES):
+            b = 2 * HALVES + h
+            nc.vector.tensor_tensor(windows[b % WINDOWS][:].indirect(offsets[:]), y_v[h][:], gates[:], mult)
+            store(b)

@@ -20,21 +20,23 @@ PACK = 4
 S = E * C
 LIST = 16
 HALVES = N // P
+EARLY = 3
+QUERY_RUNS = ((0, 1), (1, EARLY), (EARLY, E))
 HEAD = 2
-PARTS = ((0, HEAD), (HEAD, E))
+BANK_RUNS = ((0, HEAD), (HEAD, E))
 WINDOWS = 3
 QUANT = 2
+BANKS = 6
 
 
 def tile_moe_qkv_kernel(tc, x_words, x_scales, wq_words, wq_scales, wk_words, wk_scales, wv, bias, gate, offs, out):
     nc = tc.nc
     mult = mybir.AluOpType.mult
-    identity = mybir.ActivationFunctionType.Identity
+    add_bias = mybir.ActivationFunctionType.Identity
 
     with ExitStack() as ctx:
         keep = ctx.enter_context(tc.tile_pool(name="keep", bufs=1))
-        psum = ctx.enter_context(tc.psum_pool(name="psum", bufs=4))
-        turns = ctx.enter_context(tc.psum_pool(name="turns", bufs=2))
+        psum = ctx.enter_context(tc.psum_pool(name="psum", bufs=BANKS))
 
         def tile(shape, dtype, name, tag=None):
             return keep.tile(shape, dtype, name=name, tag=tag or name, align_bytes=64)
@@ -44,7 +46,7 @@ def tile_moe_qkv_kernel(tc, x_words, x_scales, wq_words, wq_scales, wk_words, wk
         q_s = tile([P, E, N], U8, "q_s")
         k_s = tile([P, E, N], U8, "k_s")
         seeds = [tile([P, 8], F32, f"seed{i}") for i in range(3)]
-        zeros = [tile([P, 8], F32, f"zero{i}") for i in range(WINDOWS - 1)]
+        zeros = [tile([P, 8], F32, f"zero{i}") for i in range(HALVES)]
         windows = [tile([P, T], F32, f"window{i}") for i in range(WINDOWS)]
 
         nc.vector.memset(x_s[:].bitcast(I32), 0)
@@ -52,64 +54,63 @@ def tile_moe_qkv_kernel(tc, x_words, x_scales, wq_words, wq_scales, wk_words, wk
             nc.vector.memset(seed[:], 0.0)
         for seed, zero in zip(seeds, zeros):
             nc.vector.tensor_copy(zero[:], seed[:])
-        eye = tile([P, P], F32, "eye")
-        nc.vector.tensor_copy(eye[:], seeds[2][:, 0:1].to_broadcast([P, P]))
-        make_identity(nc, eye[:], nomemset=True)
         nc.vector.memset(q_s[:].bitcast(I32), 0)
+        eye = tile([P, P], F32, "eye")
+        nc.vector.tensor_copy(eye[:], seeds[-1][:, 0:1].to_broadcast([P, P]))
+        make_identity(nc, eye[:], nomemset=True)
         nc.vector.memset(k_s[:].bitcast(I32), 0)
         kv_rows = tile([P, P * E], F32, "kv_rows")
         nc.vector.memset(kv_rows[:], 0.0)
-        for w, zero in zip(windows, zeros):
-            nc.scalar.copy(out=w[:], in_=zero[:, 0:1].to_broadcast([P, T]))
-        nc.scalar.copy(out=windows[2][:], in_=windows[0][:])
+        for window, zero in zip(windows, zeros):
+            nc.scalar.copy(out=window[:], in_=zero[:, 0:1].to_broadcast([P, T]))
+        nc.scalar.copy(out=windows[-1][:], in_=windows[0][:])
 
         def load_scale_rows(plane, rows):
-            for r in range(4):
+            for r in range(PACK):
                 nc.sync.dma_start(out=plane[r:P:32], in_=rows[r])
 
         def weight_scale_rows(scales):
-            return scales.bitcast(I32).rearrange("e s (q r) n -> r q (e s) n", r=4)
+            return scales.bitcast(I32).rearrange("e s (q r) n -> r q (e s) n", r=PACK)
 
         q_rows = wq_words.bitcast(I32).rearrange("e s p b -> p (e s) b")
-        bias_rows = bias.rearrange("(b p) e -> p b e", p=P)
 
         nc.sync.dma_start(offsets[:], offs)
-        load_scale_rows(x_s[:].bitcast(I32), x_scales[0].bitcast(I32).rearrange("(q r) t -> r q t", r=4))
+        load_scale_rows(x_s[:].bitcast(I32), x_scales[0].bitcast(I32).rearrange("(q r) t -> r q t", r=PACK))
         x_w = tile([P, T], I32, "x_w", tag="seed0")
         nc.sync.dma_start(out=x_w[:], in_=x_words[0].rearrange("p t d -> p (t d)").bitcast(I32))
-        q_head = tile([P, HEAD, 2 * N], U8, "q_head", tag="seed1")
-        nc.sync.dma_start(out=q_head[:].bitcast(I32), in_=q_rows[:, 0:HEAD])
+        q_early = tile([P, EARLY, 2 * N], U8, "q_early", tag="seed1")
+        nc.sync.dma_start(out=q_early[:].bitcast(I32), in_=q_rows[:, 0:EARLY])
         load_scale_rows(q_s[:].bitcast(I32), weight_scale_rows(wq_scales))
         bias_q = tile([P, HALVES, 8], F32, "bias_q", tag="seed2")
-        nc.sync.dma_start(out=bias_q[:, :, 0:E], in_=bias_rows[:, 0:HALVES])
+        nc.sync.dma_start(out=bias_q[:, :, 0:E], in_=bias.rearrange("(b p) e -> p b e", p=P)[:, 0:HALVES])
         gates = tile([P, S], F32, "gates", tag="zero0")
         nc.sync.dma_start(out=gates[:], in_=gate)
-        q_tail = tile([P, E - HEAD, 2 * N], U8, "q_tail", tag="zero1")
-        nc.sync.dma_start(out=q_tail[:].bitcast(I32), in_=q_rows[:, HEAD:E])
+        q_late = tile([P, E - EARLY, 2 * N], U8, "q_late", tag="zero1")
+        nc.sync.dma_start(out=q_late[:].bitcast(I32), in_=q_rows[:, EARLY:E])
 
         def entries(e0, e1):
             return offsets[:, e0 * C // LIST : e1 * C // LIST]
 
-        def gather(window, dtype, name, parts):
+        def gather(table, dtype, name, runs):
             slots = []
-            for e0, e1 in parts:
+            for e0, e1 in runs:
                 part = tile([P, (e1 - e0) * C], dtype, f"{name}{e0}")
-                nc.vector.tensor_copy(part[:], window.indirect(entries(e0, e1)))
+                nc.vector.tensor_copy(part[:], table.indirect(entries(e0, e1)))
                 slots.extend(part[:, (e - e0) * C : (e - e0 + 1) * C] for e in range(e0, e1))
             return slots
 
         slot_s = gather(x_s[:], U8, "slot_s", [(0, E)])
-        slot_w = gather(x_w[:].bitcast(U32), U32, "slot_w", PARTS)
+        slot_w = gather(x_w[:].bitcast(U32), U32, "slot_w", QUERY_RUNS)
 
         def load_v(e0, tag):
             raw = tile([P, QUANT, PACK, N], F32, f"v_raw{e0}", tag=tag)
             nc.sync.dma_start(out=raw[:], in_=wv[e0 : e0 + QUANT].rearrange("e (p j) n -> p e j n", j=PACK))
             return raw
 
-        v_raw = [load_v(2, "x_s")]
+        v_order = (HEAD, HEAD + QUANT, 0)
+        v_raw = [load_v(v_order[0], "x_s")]
         load_scale_rows(k_s[:].bitcast(I32), weight_scale_rows(wk_scales))
         nc.sync.dma_start(out=kv_rows[0 : 2 * HALVES], in_=bias[N : 3 * N].rearrange("(b p) e -> b (p e)", p=P))
-
 
         def project(y, weights, biases, e0, e1):
             acc = psum.tile([P, (e1 - e0) * C], F32, name="acc")
@@ -128,21 +129,25 @@ def tile_moe_qkv_kernel(tc, x_words, x_scales, wq_words, wq_scales, wk_words, wk
                 nc.scalar.activation(
                     out=y[:, e * C : (e + 1) * C],
                     in_=acc[:, (e - e0) * C : (e - e0 + 1) * C],
-                    func=identity,
+                    func=add_bias,
                     bias=biases(e),
                 )
+
+        def scatter(y, b, e0, e1):
+            cols = slice(e0 * C, e1 * C)
+            nc.vector.tensor_tensor(windows[b % WINDOWS][:].indirect(entries(e0, e1)), y[:, cols], gates[:, cols], mult)
 
         def store(b):
             nc.sync.dma_start(out=out[b * P : (b + 1) * P, :], in_=windows[b % WINDOWS][:])
 
         def q_weights(e, h):
-            words = q_head[:, e] if e < HEAD else q_tail[:, e - HEAD]
+            words = q_early[:, e] if e < EARLY else q_late[:, e - EARLY]
             return words[:, 2 * h * P : 2 * (h + 1) * P].bitcast(FP4X4), q_s[:, e, h * P : (h + 1) * P]
 
         y_q = [tile([P, S], F32, f"y_q{h}") for h in range(HALVES)]
-        for part in PARTS:
+        for run in QUERY_RUNS:
             for h in range(HALVES):
-                project(y_q[h], lambda e: q_weights(e, h), lambda e: bias_q[:, h, e : e + 1], *part)
+                project(y_q[h], lambda e: q_weights(e, h), lambda e: bias_q[:, h, e : e + 1], *run)
 
         k_w = tile([P, E, N], I32, "k_w", tag="seed1")
         nc.sync.dma_start(out=k_w[:], in_=wk_words.rearrange("e s p n d -> p (e s) (n d)").bitcast(I32))
@@ -152,30 +157,29 @@ def tile_moe_qkv_kernel(tc, x_words, x_scales, wq_words, wq_scales, wk_words, wk
             for e in range(E // 2):
                 nc.tensor.transpose(turned[:, e], kv_rows[:, e0 + e : P * E : E], eye[:])
             nc.scalar.copy(out=bias_kv[:, e0 : e0 + E // 2], in_=turned[:, :, 0 : 2 * HALVES])
-        v_raw.extend([load_v(4, "q_s"), load_v(0, "seed2")])
+        v_raw.extend([load_v(v_order[1], "q_s"), load_v(v_order[2], "seed2")])
 
-        for e0, e1 in PARTS:
+        for run in QUERY_RUNS:
             for h in range(HALVES):
-                nc.vector.tensor_tensor(windows[h][:].indirect(entries(e0, e1)), y_q[h][:, e0 * C : e1 * C], gates[:, e0 * C : e1 * C], mult)
+                scatter(y_q[h], h, *run)
         for h in range(HALVES):
             store(h)
 
         def k_weights(e, h):
             return k_w[:, e, h * P : (h + 1) * P].bitcast(FP8X4), k_s[:, e, h * P : (h + 1) * P]
 
-        def key_part(y, h, e0, e1):
-            b = HALVES + h
+        def key_run(y, h, e0, e1):
             project(y, lambda e: k_weights(e, h), lambda e: bias_kv[:, e, h : h + 1], e0, e1)
-            nc.vector.tensor_tensor(windows[b % WINDOWS][:].indirect(entries(e0, e1)), y[:, e0 * C : e1 * C], gates[:, e0 * C : e1 * C], mult)
+            scatter(y, HALVES + h, e0, e1)
             if e1 == E:
-                store(b)
+                store(HALVES + h)
 
         for h in range(HALVES):
-            key_part(tile([P, S], F32, f"y_k{h}"), h, 0, HEAD)
+            key_run(tile([P, S], F32, f"y_k{h}"), h, *BANK_RUNS[0])
 
         v_w = tile([P, E, N], U32, "v_w")
         v_s = tile([P, E, N], U8, "v_s")
-        for raw, e0 in zip(v_raw, (2, 4, 0)):
+        for raw, e0 in zip(v_raw, v_order):
             grouped = tile([P, QUANT, N, PACK], BF16, f"grouped{e0}")
             for e in range(QUANT):
                 nc.scalar.copy(
@@ -189,17 +193,16 @@ def tile_moe_qkv_kernel(tc, x_words, x_scales, wq_words, wq_scales, wk_words, wk
             )
 
         y_tail = tile([P, HALVES, S], F32, "y_tail", tag="seed2")
-        key_part(y_tail[:, 0], 0, HEAD, E)
-        key_part(y_tail[:, 1], 1, HEAD, E)
+        for h in range(HALVES):
+            key_run(y_tail[:, h], h, *BANK_RUNS[1])
 
         def v_weights(e, h):
             return v_w[:, e, h * P : (h + 1) * P].bitcast(FP8X4), v_s[:, e, h * P : (h + 1) * P]
 
         y_v = [tile([P, S], F32, f"y_v{h}") for h in range(HALVES)]
-        for e0, e1 in PARTS:
+        for run in BANK_RUNS:
             for h in range(HALVES):
-                project(y_v[h], lambda e: v_weights(e, h), lambda e: bias_kv[:, e, HALVES + h : HALVES + h + 1], e0, e1)
+                project(y_v[h], lambda e: v_weights(e, h), lambda e: bias_kv[:, e, HALVES + h : HALVES + h + 1], *run)
         for h in range(HALVES):
-            b = 2 * HALVES + h
-            nc.vector.tensor_tensor(windows[b % WINDOWS][:].indirect(offsets[:]), y_v[h][:], gates[:], mult)
-            store(b)
+            scatter(y_v[h], 2 * HALVES + h, 0, E)
+            store(2 * HALVES + h)

@@ -1,7 +1,6 @@
 from contextlib import ExitStack
 
 import concourse.mybir as mybir
-from concourse.masks import make_identity
 
 K, T, E, C, N = 512, 1024, 6, 128, 256
 FLOPS = 2 * K * 3 * N * E * C
@@ -20,13 +19,19 @@ PACK = 4
 S = E * C
 LIST = 16
 HALVES = N // P
-EARLY = 3
-QUERY_RUNS = ((0, 1), (1, EARLY), (EARLY, E))
-HEAD = 2
-BANK_RUNS = ((0, HEAD), (HEAD, E))
+QUERY_RUNS = ((0, 1), (1, 3), (3, E))
+BANK_RUNS = ((0, 4), (4, E))
 WINDOWS = 3
 QUANT = 2
-BANKS = 6
+SEED = 64
+ROW = 8
+
+RAW_BYTES = QUANT * PACK * N * 4
+X_AT = RAW_BYTES - 4 * T
+Q_FIRST_AT = RAW_BYTES
+GATES_AT = Q_FIRST_AT + 1024
+BIAS_AT = GATES_AT + 4 * S
+Q_REST_AT = BIAS_AT + 4 * HALVES * ROW
 
 
 def tile_moe_qkv_kernel(tc, x_words, x_scales, wq_words, wq_scales, wk_words, wk_scales, wv, bias, gate, offs, out):
@@ -36,34 +41,36 @@ def tile_moe_qkv_kernel(tc, x_words, x_scales, wq_words, wq_scales, wk_words, wk
 
     with ExitStack() as ctx:
         keep = ctx.enter_context(tc.tile_pool(name="keep", bufs=1))
-        psum = ctx.enter_context(tc.psum_pool(name="psum", bufs=BANKS))
+        laid = ctx.enter_context(tc.tile_pool(name="laid", bufs=1))
+        psum = ctx.enter_context(tc.psum_pool(name="psum", bufs=1))
 
         def tile(shape, dtype, name, tag=None):
             return keep.tile(shape, dtype, name=name, tag=tag or name, align_bytes=64)
+
+        def tile_at(shape, dtype, name, place):
+            return laid.tile(shape, dtype, name=name, align_bytes=64, offset=place)
 
         offsets = keep.tile([P, S // LIST], U16, name="offsets")
         x_s = tile([P, T], U8, "x_s")
         q_s = tile([P, E, N], U8, "q_s")
         k_s = tile([P, E, N], U8, "k_s")
-        seeds = [tile([P, 8], F32, f"seed{i}") for i in range(3)]
-        zeros = [tile([P, 8], F32, f"zero{i}") for i in range(HALVES)]
+        seeds = [tile_at([P, SEED], F32, "seed0", Q_FIRST_AT - 128), tile_at([P, SEED], F32, "seed1", BIAS_AT - 64)]
+        zeros = [tile([P, SEED], F32, f"zero{i}") for i in range(2)]
         windows = [tile([P, T], F32, f"window{i}") for i in range(WINDOWS)]
 
         nc.vector.memset(x_s[:].bitcast(I32), 0)
         for seed in seeds:
             nc.vector.memset(seed[:], 0.0)
-        for seed, zero in zip(seeds, zeros):
-            nc.vector.tensor_copy(zero[:], seed[:])
+        nc.vector.tensor_copy(zeros[0][:], seeds[0][:])
         nc.vector.memset(q_s[:].bitcast(I32), 0)
-        eye = tile([P, P], F32, "eye")
-        nc.vector.tensor_copy(eye[:], seeds[-1][:, 0:1].to_broadcast([P, P]))
-        make_identity(nc, eye[:], nomemset=True)
+        nc.vector.tensor_copy(zeros[1][:], seeds[1][:])
+        nc.vector.memset(windows[2][:], 0.0)
         nc.vector.memset(k_s[:].bitcast(I32), 0)
-        kv_rows = tile([P, P * E], F32, "kv_rows")
-        nc.vector.memset(kv_rows[:], 0.0)
         for window, zero in zip(windows, zeros):
-            nc.scalar.copy(out=window[:], in_=zero[:, 0:1].to_broadcast([P, T]))
-        nc.scalar.copy(out=windows[-1][:], in_=windows[0][:])
+            nc.scalar.copy(
+                out=window[:].rearrange("p (r c) -> p r c", c=SEED),
+                in_=zero[:].unsqueeze(1).to_broadcast([P, T // SEED, SEED]),
+            )
 
         def load_scale_rows(plane, rows):
             for r in range(PACK):
@@ -73,20 +80,21 @@ def tile_moe_qkv_kernel(tc, x_words, x_scales, wq_words, wq_scales, wk_words, wk
             return scales.bitcast(I32).rearrange("e s (q r) n -> r q (e s) n", r=PACK)
 
         q_rows = wq_words.bitcast(I32).rearrange("e s p b -> p (e s) b")
+        bias_rows = bias.rearrange("(b p) e -> p b e", p=P)
 
         nc.sync.dma_start(offsets[:], offs)
         load_scale_rows(x_s[:].bitcast(I32), x_scales[0].bitcast(I32).rearrange("(q r) t -> r q t", r=PACK))
-        x_w = tile([P, T], I32, "x_w", tag="seed0")
+        x_w = tile_at([P, T], I32, "x_w", X_AT)
         nc.sync.dma_start(out=x_w[:], in_=x_words[0].rearrange("p t d -> p (t d)").bitcast(I32))
-        q_early = tile([P, EARLY, 2 * N], U8, "q_early", tag="seed1")
-        nc.sync.dma_start(out=q_early[:].bitcast(I32), in_=q_rows[:, 0:EARLY])
+        q_first = tile_at([P, 1, 2 * N], U8, "q_first", Q_FIRST_AT)
+        nc.sync.dma_start(out=q_first[:].bitcast(I32), in_=q_rows[:, 0:1])
         load_scale_rows(q_s[:].bitcast(I32), weight_scale_rows(wq_scales))
-        bias_q = tile([P, HALVES, 8], F32, "bias_q", tag="seed2")
-        nc.sync.dma_start(out=bias_q[:, :, 0:E], in_=bias.rearrange("(b p) e -> p b e", p=P)[:, 0:HALVES])
-        gates = tile([P, S], F32, "gates", tag="zero0")
+        bias_q = tile_at([P, HALVES, ROW], F32, "bias_q", BIAS_AT)
+        nc.sync.dma_start(out=bias_q[:, :, 0:E], in_=bias_rows[:, 0:HALVES])
+        gates = tile_at([P, S], F32, "gates", GATES_AT)
         nc.sync.dma_start(out=gates[:], in_=gate)
-        q_late = tile([P, E - EARLY, 2 * N], U8, "q_late", tag="zero1")
-        nc.sync.dma_start(out=q_late[:].bitcast(I32), in_=q_rows[:, EARLY:E])
+        q_rest = tile_at([P, E - 1, 2 * N], U8, "q_rest", Q_REST_AT)
+        nc.sync.dma_start(out=q_rest[:].bitcast(I32), in_=q_rows[:, 1:E])
 
         def entries(e0, e1):
             return offsets[:, e0 * C // LIST : e1 * C // LIST]
@@ -102,18 +110,21 @@ def tile_moe_qkv_kernel(tc, x_words, x_scales, wq_words, wq_scales, wk_words, wk
         slot_s = gather(x_s[:], U8, "slot_s", [(0, E)])
         slot_w = gather(x_w[:].bitcast(U32), U32, "slot_w", QUERY_RUNS)
 
-        def load_v(e0, tag):
-            raw = tile([P, QUANT, PACK, N], F32, f"v_raw{e0}", tag=tag)
+        def load_v(raw, e0):
             nc.sync.dma_start(out=raw[:], in_=wv[e0 : e0 + QUANT].rearrange("e (p j) n -> p e j n", j=PACK))
             return raw
 
-        v_order = (HEAD, HEAD + QUANT, 0)
-        v_raw = [load_v(v_order[0], "x_s")]
+        raw_shape = [P, QUANT, PACK, N]
+        v_raw = [load_v(tile(raw_shape, F32, "v_raw0", tag="zero0"), 0)]
         load_scale_rows(k_s[:].bitcast(I32), weight_scale_rows(wk_scales))
-        nc.sync.dma_start(out=kv_rows[0 : 2 * HALVES], in_=bias[N : 3 * N].rearrange("(b p) e -> b (p e)", p=P))
+        k_w = tile([P, E, N], I32, "k_w", tag="zero1")
+        nc.sync.dma_start(out=k_w[:], in_=wk_words.rearrange("e s p n d -> p (e s) (n d)").bitcast(I32))
+        bias_kv = tile([P, 2 * HALVES, ROW], F32, "bias_kv", tag="x_s")
+        nc.sync.dma_start(out=bias_kv[:, :, 0:E], in_=bias_rows[:, HALVES : 3 * HALVES])
+        v_raw.append(load_v(tile_at(raw_shape, F32, "v_raw1", 0), QUANT))
 
-        def project(y, weights, biases, e0, e1):
-            acc = psum.tile([P, (e1 - e0) * C], F32, name="acc")
+        def project(y, weights, biases, bank, e0, e1):
+            acc = psum.tile([P, 4 * C], F32, name="acc", tag=f"bank{bank}")
             for e in range(e0, e1):
                 w_codes, w_scales = weights(e)
                 nc.tensor.matmul_mx(
@@ -141,23 +152,14 @@ def tile_moe_qkv_kernel(tc, x_words, x_scales, wq_words, wq_scales, wk_words, wk
             nc.sync.dma_start(out=out[b * P : (b + 1) * P, :], in_=windows[b % WINDOWS][:])
 
         def q_weights(e, h):
-            words = q_early[:, e] if e < EARLY else q_late[:, e - EARLY]
+            words = q_first[:, 0] if e == 0 else q_rest[:, e - 1]
             return words[:, 2 * h * P : 2 * (h + 1) * P].bitcast(FP4X4), q_s[:, e, h * P : (h + 1) * P]
 
         y_q = [tile([P, S], F32, f"y_q{h}") for h in range(HALVES)]
-        for run in QUERY_RUNS:
+        for i, run in enumerate(QUERY_RUNS):
             for h in range(HALVES):
-                project(y_q[h], lambda e: q_weights(e, h), lambda e: bias_q[:, h, e : e + 1], *run)
-
-        k_w = tile([P, E, N], I32, "k_w", tag="seed1")
-        nc.sync.dma_start(out=k_w[:], in_=wk_words.rearrange("e s p n d -> p (e s) (n d)").bitcast(I32))
-        bias_kv = tile([P, E, 2 * HALVES], F32, "bias_kv")
-        for e0 in (0, E // 2):
-            turned = psum.tile([P, E // 2, P], F32, name="acc")
-            for e in range(E // 2):
-                nc.tensor.transpose(turned[:, e], kv_rows[:, e0 + e : P * E : E], eye[:])
-            nc.scalar.copy(out=bias_kv[:, e0 : e0 + E // 2], in_=turned[:, :, 0 : 2 * HALVES])
-        v_raw.extend([load_v(v_order[1], "q_s"), load_v(v_order[2], "seed2")])
+                project(y_q[h], lambda e: q_weights(e, h), lambda e: bias_q[:, h, e : e + 1], HALVES * i + h, *run)
+        v_raw.append(load_v(tile_at(raw_shape, F32, "v_raw2", Q_REST_AT), 2 * QUANT))
 
         for run in QUERY_RUNS:
             for h in range(HALVES):
@@ -165,21 +167,21 @@ def tile_moe_qkv_kernel(tc, x_words, x_scales, wq_words, wq_scales, wk_words, wk
         for h in range(HALVES):
             store(h)
 
-        def k_weights(e, h):
-            return k_w[:, e, h * P : (h + 1) * P].bitcast(FP8X4), k_s[:, e, h * P : (h + 1) * P]
+        def whole_block(y, b, weights, bank):
+            for i, run in enumerate(BANK_RUNS):
+                project(y, weights, lambda e: bias_kv[:, b - HALVES, e : e + 1], bank + i, *run)
+            scatter(y, b, 0, E)
+            store(b)
 
-        def key_run(y, h, e0, e1):
-            project(y, lambda e: k_weights(e, h), lambda e: bias_kv[:, e, h : h + 1], e0, e1)
-            scatter(y, HALVES + h, e0, e1)
-            if e1 == E:
-                store(HALVES + h)
+        def k_weights(h):
+            return lambda e: (k_w[:, e, h * P : (h + 1) * P].bitcast(FP8X4), k_s[:, e, h * P : (h + 1) * P])
 
-        for h in range(HALVES):
-            key_run(tile([P, S], F32, f"y_k{h}"), h, *BANK_RUNS[0])
+        whole_block(tile([P, S], F32, "y_k0"), HALVES, k_weights(0), 6)
 
         v_w = tile([P, E, N], U32, "v_w")
         v_s = tile([P, E, N], U8, "v_s")
-        for raw, e0 in zip(v_raw, v_order):
+        for i, raw in enumerate(v_raw):
+            e0 = i * QUANT
             grouped = tile([P, QUANT, N, PACK], BF16, f"grouped{e0}")
             for e in range(QUANT):
                 nc.scalar.copy(
@@ -192,17 +194,9 @@ def tile_moe_qkv_kernel(tc, x_words, x_scales, wq_words, wq_scales, wk_words, wk
                 in_=grouped[:].rearrange("p e n t -> p (e n t)"),
             )
 
-        y_tail = tile([P, HALVES, S], F32, "y_tail", tag="seed2")
-        for h in range(HALVES):
-            key_run(y_tail[:, h], h, *BANK_RUNS[1])
+        def v_weights(h):
+            return lambda e: (v_w[:, e, h * P : (h + 1) * P].bitcast(FP8X4), v_s[:, e, h * P : (h + 1) * P])
 
-        def v_weights(e, h):
-            return v_w[:, e, h * P : (h + 1) * P].bitcast(FP8X4), v_s[:, e, h * P : (h + 1) * P]
-
-        y_v = [tile([P, S], F32, f"y_v{h}") for h in range(HALVES)]
-        for run in BANK_RUNS:
-            for h in range(HALVES):
-                project(y_v[h], lambda e: v_weights(e, h), lambda e: bias_kv[:, e, HALVES + h : HALVES + h + 1], *run)
-        for h in range(HALVES):
-            scatter(y_v[h], 2 * HALVES + h, 0, E)
-            store(2 * HALVES + h)
+        y_late = tile_at([P, 3, S], F32, "y_late", Q_REST_AT)
+        for i, weights in enumerate((k_weights(1), v_weights(0), v_weights(1))):
+            whole_block(y_late[:, i], HALVES + 1 + i, weights, 0)

@@ -19,7 +19,8 @@ PACK = 4
 S = E * C
 LIST = 16
 HALVES = N // P
-QUERY_RUNS = ((0, 1), (1, 3), (3, E))
+EARLY = 3
+QUERY_RUNS = ((0, 1), (1, EARLY), (EARLY, E))
 BANK_RUNS = ((0, 4), (4, E))
 WINDOWS = 3
 QUANT = 2
@@ -29,7 +30,7 @@ ROW = 8
 RAW_BYTES = QUANT * PACK * N * 4
 X_AT = RAW_BYTES - 4 * T
 Q_FIRST_AT = RAW_BYTES
-GATES_AT = Q_FIRST_AT + 1024
+GATES_AT = Q_FIRST_AT + EARLY * 2 * N
 BIAS_AT = GATES_AT + 4 * S
 Q_REST_AT = BIAS_AT + 4 * HALVES * ROW
 
@@ -86,15 +87,15 @@ def tile_moe_qkv_kernel(tc, x_words, x_scales, wq_words, wq_scales, wk_words, wk
         load_scale_rows(x_s[:].bitcast(I32), x_scales[0].bitcast(I32).rearrange("(q r) t -> r q t", r=PACK))
         x_w = tile_at([P, T], I32, "x_w", X_AT)
         nc.sync.dma_start(out=x_w[:], in_=x_words[0].rearrange("p t d -> p (t d)").bitcast(I32))
-        q_first = tile_at([P, 1, 2 * N], U8, "q_first", Q_FIRST_AT)
-        nc.sync.dma_start(out=q_first[:].bitcast(I32), in_=q_rows[:, 0:1])
+        q_first = tile_at([P, EARLY, 2 * N], U8, "q_first", Q_FIRST_AT)
+        nc.sync.dma_start(out=q_first[:].bitcast(I32), in_=q_rows[:, 0:EARLY])
         load_scale_rows(q_s[:].bitcast(I32), weight_scale_rows(wq_scales))
         bias_q = tile_at([P, HALVES, ROW], F32, "bias_q", BIAS_AT)
         nc.sync.dma_start(out=bias_q[:, :, 0:E], in_=bias_rows[:, 0:HALVES])
         gates = tile_at([P, S], F32, "gates", GATES_AT)
         nc.sync.dma_start(out=gates[:], in_=gate)
-        q_rest = tile_at([P, E - 1, 2 * N], U8, "q_rest", Q_REST_AT)
-        nc.sync.dma_start(out=q_rest[:].bitcast(I32), in_=q_rows[:, 1:E])
+        q_rest = tile_at([P, E - EARLY, 2 * N], U8, "q_rest", Q_REST_AT)
+        nc.sync.dma_start(out=q_rest[:].bitcast(I32), in_=q_rows[:, EARLY:E])
 
         def entries(e0, e1):
             return offsets[:, e0 * C // LIST : e1 * C // LIST]
@@ -152,7 +153,7 @@ def tile_moe_qkv_kernel(tc, x_words, x_scales, wq_words, wq_scales, wk_words, wk
             nc.sync.dma_start(out=out[b * P : (b + 1) * P, :], in_=windows[b % WINDOWS][:])
 
         def q_weights(e, h):
-            words = q_first[:, 0] if e == 0 else q_rest[:, e - 1]
+            words = q_first[:, e] if e < EARLY else q_rest[:, e - EARLY]
             return words[:, 2 * h * P : 2 * (h + 1) * P].bitcast(FP4X4), q_s[:, e, h * P : (h + 1) * P]
 
         y_q = [tile([P, S], F32, f"y_q{h}") for h in range(HALVES)]

@@ -28,11 +28,13 @@ SEED = 64
 ROW = 8
 
 RAW_BYTES = QUANT * PACK * N * 4
-X_AT = RAW_BYTES - 4 * T
-Q_FIRST_AT = RAW_BYTES
+X_AT = 0
+Q_FIRST_AT = X_AT + 4 * T
 GATES_AT = Q_FIRST_AT + EARLY * 2 * N
 BIAS_AT = GATES_AT + 4 * S
-Q_REST_AT = BIAS_AT + 4 * HALVES * ROW
+V1_AT = BIAS_AT + 4 * T
+V2_AT = V1_AT + RAW_BYTES
+Q_REST_AT = V2_AT - (E - EARLY) * N
 
 
 def tile_moe_qkv_kernel(tc, x_words, x_scales, wq_words, wq_scales, wk_words, wk_scales, wv, bias, gate, offs, out):
@@ -53,29 +55,31 @@ def tile_moe_qkv_kernel(tc, x_words, x_scales, wq_words, wq_scales, wk_words, wk
 
         offsets = keep.tile([P, S // LIST], U16, name="offsets")
         x_s = tile([P, T], U8, "x_s")
-        q_s = tile([P, E, N], U8, "q_s")
-        k_s = tile([P, E, N], U8, "k_s")
-        seeds = [tile_at([P, SEED], F32, "seed0", Q_FIRST_AT - 128), tile_at([P, SEED], F32, "seed1", BIAS_AT - 64)]
-        zeros = [tile([P, SEED], F32, f"zero{i}") for i in range(2)]
-        windows = [tile([P, T], F32, f"window{i}") for i in range(WINDOWS)]
+        planes = tile([P, E, N], U8, "planes")
+        seeds = [tile_at([P, SEED], F32, f"seed{i}", at) for i, at in enumerate((Q_FIRST_AT - 128, BIAS_AT - 64, Q_REST_AT))]
+        zeros = [tile([P, SEED], F32, f"zero{i}") for i in range(WINDOWS)]
+        windows = [tile([P, T], F32, f"window{i}") for i in range(WINDOWS - 1)]
 
         nc.vector.memset(x_s[:].bitcast(I32), 0)
         for seed in seeds:
             nc.vector.memset(seed[:], 0.0)
         nc.vector.tensor_copy(zeros[0][:], seeds[0][:])
-        nc.vector.memset(q_s[:].bitcast(I32), 0)
+        nc.vector.memset(planes[:].bitcast(I32), 0)
         nc.vector.tensor_copy(zeros[1][:], seeds[1][:])
-        nc.vector.memset(windows[2][:], 0.0)
-        nc.vector.memset(k_s[:].bitcast(I32), 0)
-        for window, zero in zip(windows, zeros):
+        nc.vector.tensor_copy(zeros[2][:], seeds[2][:])
+
+        def clear(window, zero):
             nc.scalar.copy(
                 out=window[:].rearrange("p (r c) -> p r c", c=SEED),
                 in_=zero[:].unsqueeze(1).to_broadcast([P, T // SEED, SEED]),
             )
 
-        def load_scale_rows(plane, rows):
+        for window, zero in zip(windows, zeros):
+            clear(window, zero)
+
+        def load_scale_rows(plane, rows, first=0):
             for r in range(PACK):
-                nc.sync.dma_start(out=plane[r:P:32], in_=rows[r])
+                nc.sync.dma_start(out=plane[first + r : P : 32], in_=rows[r])
 
         def weight_scale_rows(scales):
             return scales.bitcast(I32).rearrange("e s (q r) n -> r q (e s) n", r=PACK)
@@ -89,7 +93,7 @@ def tile_moe_qkv_kernel(tc, x_words, x_scales, wq_words, wq_scales, wk_words, wk
         nc.sync.dma_start(out=x_w[:], in_=x_words[0].rearrange("p t d -> p (t d)").bitcast(I32))
         q_first = tile_at([P, EARLY, 2 * N], U8, "q_first", Q_FIRST_AT)
         nc.sync.dma_start(out=q_first[:].bitcast(I32), in_=q_rows[:, 0:EARLY])
-        load_scale_rows(q_s[:].bitcast(I32), weight_scale_rows(wq_scales))
+        load_scale_rows(planes[:].bitcast(I32), weight_scale_rows(wq_scales))
         bias_q = tile_at([P, HALVES, ROW], F32, "bias_q", BIAS_AT)
         nc.sync.dma_start(out=bias_q[:, :, 0:E], in_=bias_rows[:, 0:HALVES])
         gates = tile_at([P, S], F32, "gates", GATES_AT)
@@ -117,12 +121,10 @@ def tile_moe_qkv_kernel(tc, x_words, x_scales, wq_words, wq_scales, wk_words, wk
 
         raw_shape = [P, QUANT, PACK, N]
         v_raw = [load_v(tile(raw_shape, F32, "v_raw0", tag="zero0"), 0)]
-        load_scale_rows(k_s[:].bitcast(I32), weight_scale_rows(wk_scales))
         k_w = tile([P, E, N], I32, "k_w", tag="zero1")
         nc.sync.dma_start(out=k_w[:], in_=wk_words.rearrange("e s p n d -> p (e s) (n d)").bitcast(I32))
         bias_kv = tile([P, 2 * HALVES, ROW], F32, "bias_kv", tag="x_s")
         nc.sync.dma_start(out=bias_kv[:, :, 0:E], in_=bias_rows[:, HALVES : 3 * HALVES])
-        v_raw.append(load_v(tile_at(raw_shape, F32, "v_raw1", 0), QUANT))
 
         def project(y, weights, biases, bank, e0, e1):
             acc = psum.tile([P, 4 * C], F32, name="acc", tag=f"bank{bank}")
@@ -154,13 +156,17 @@ def tile_moe_qkv_kernel(tc, x_words, x_scales, wq_words, wq_scales, wk_words, wk
 
         def q_weights(e, h):
             words = q_first[:, e] if e < EARLY else q_rest[:, e - EARLY]
-            return words[:, 2 * h * P : 2 * (h + 1) * P].bitcast(FP4X4), q_s[:, e, h * P : (h + 1) * P]
+            return words[:, 2 * h * P : 2 * (h + 1) * P].bitcast(FP4X4), planes[:, e, h * P : (h + 1) * P]
 
         y_q = [tile([P, S], F32, f"y_q{h}") for h in range(HALVES)]
         for i, run in enumerate(QUERY_RUNS):
             for h in range(HALVES):
                 project(y_q[h], lambda e: q_weights(e, h), lambda e: bias_q[:, h, e : e + 1], HALVES * i + h, *run)
-        v_raw.append(load_v(tile_at(raw_shape, F32, "v_raw2", Q_REST_AT), 2 * QUANT))
+        load_scale_rows(planes[:].bitcast(I32), weight_scale_rows(wk_scales), PACK)
+        v_raw.append(load_v(tile_at(raw_shape, F32, "v_raw1", V1_AT), QUANT))
+        v_raw.append(load_v(tile_at(raw_shape, F32, "v_raw2", V2_AT), 2 * QUANT))
+        windows.append(tile_at([P, T], F32, "window2", BIAS_AT))
+        clear(windows[2], zeros[2])
 
         for run in QUERY_RUNS:
             for h in range(HALVES):
@@ -175,7 +181,7 @@ def tile_moe_qkv_kernel(tc, x_words, x_scales, wq_words, wq_scales, wk_words, wk
             store(b)
 
         def k_weights(h):
-            return lambda e: (k_w[:, e, h * P : (h + 1) * P].bitcast(FP8X4), k_s[:, e, h * P : (h + 1) * P])
+            return lambda e: (k_w[:, e, h * P : (h + 1) * P].bitcast(FP8X4), planes[PACK:P, e, h * P : (h + 1) * P])
 
         whole_block(tile([P, S], F32, "y_k0"), HALVES, k_weights(0), 6)
 
@@ -198,6 +204,6 @@ def tile_moe_qkv_kernel(tc, x_words, x_scales, wq_words, wq_scales, wk_words, wk
         def v_weights(h):
             return lambda e: (v_w[:, e, h * P : (h + 1) * P].bitcast(FP8X4), v_s[:, e, h * P : (h + 1) * P])
 
-        y_late = tile_at([P, 3, S], F32, "y_late", Q_REST_AT)
+        y_late = tile_at([P, 3, S], F32, "y_late", V2_AT)
         for i, weights in enumerate((k_weights(1), v_weights(0), v_weights(1))):
             whole_block(y_late[:, i], HALVES + 1 + i, weights, 0)

@@ -19,8 +19,9 @@ PACK = 4
 S = E * C
 LIST = 16
 HALVES = N // P
-EARLY = 3
-QUERY_RUNS = ((0, 1), (1, EARLY), (EARLY, E))
+EARLY = 1
+MID = 3
+QUERY_RUNS = ((0, EARLY), (EARLY, MID), (MID, E))
 BANK_RUNS = ((0, 4), (4, E))
 WINDOWS = 3
 QUANT = 2
@@ -97,9 +98,11 @@ def tile_moe_qkv_kernel(tc, x_words, x_scales, wq_words, wq_scales, wk_words, wk
         bias_q = tile_at([P, HALVES, ROW], F32, "bias_q", BIAS_AT)
         nc.sync.dma_start(out=bias_q[:, :, 0:E], in_=bias_rows[:, 0:HALVES])
         gates = tile_at([P, S], F32, "gates", GATES_AT)
-        nc.sync.dma_start(out=gates[:], in_=gate)
         q_rest = tile_at([P, E - EARLY, 2 * N], U8, "q_rest", Q_REST_AT)
-        nc.sync.dma_start(out=q_rest[:].bitcast(I32), in_=q_rows[:, EARLY:E])
+        nc.sync.dma_start(out=gates[:, 0 : EARLY * C], in_=gate[:, 0 : EARLY * C])
+        nc.sync.dma_start(out=q_rest[:, 0 : MID - EARLY].bitcast(I32), in_=q_rows[:, EARLY:MID])
+        nc.sync.dma_start(out=gates[:, EARLY * C : S], in_=gate[:, EARLY * C : S])
+        nc.sync.dma_start(out=q_rest[:, MID - EARLY :].bitcast(I32), in_=q_rows[:, MID:E])
 
         def entries(e0, e1):
             return offsets[:, e0 * C // LIST : e1 * C // LIST]

@@ -28,14 +28,12 @@ QUANT = 2
 SEED = 64
 ROW = 8
 
-RAW_BYTES = QUANT * PACK * N * 4
-X_AT = 0
+K_AT = 0
+X_AT = K_AT + 4 * E * N - 4 * T
 Q_FIRST_AT = X_AT + 4 * T
 GATES_AT = Q_FIRST_AT + EARLY * 2 * N
 BIAS_AT = GATES_AT + 4 * S
-V1_AT = BIAS_AT + 4 * T
-V2_AT = V1_AT + RAW_BYTES
-Q_REST_AT = V2_AT - (E - EARLY) * N
+Q_MID_AT = BIAS_AT + 4 * HALVES * ROW
 
 
 def tile_moe_qkv_kernel(tc, x_words, x_scales, wq_words, wq_scales, wk_words, wk_scales, wv, bias, gate, offs, out):
@@ -57,8 +55,8 @@ def tile_moe_qkv_kernel(tc, x_words, x_scales, wq_words, wq_scales, wk_words, wk
         offsets = keep.tile([P, S // LIST], U16, name="offsets")
         x_s = tile([P, T], U8, "x_s")
         planes = tile([P, E, N], U8, "planes")
-        seeds = [tile_at([P, SEED], F32, f"seed{i}", at) for i, at in enumerate((Q_FIRST_AT - 128, BIAS_AT - 64, Q_REST_AT))]
-        zeros = [tile([P, SEED], F32, f"zero{i}") for i in range(WINDOWS)]
+        seeds = [tile_at([P, SEED], F32, f"seed{i}", at) for i, at in enumerate((Q_FIRST_AT - 128, BIAS_AT - 64))]
+        zeros = [tile([P, SEED], F32, f"zero{i}") for i in range(2)]
         windows = [tile([P, T], F32, f"window{i}") for i in range(WINDOWS - 1)]
 
         nc.vector.memset(x_s[:].bitcast(I32), 0)
@@ -67,7 +65,6 @@ def tile_moe_qkv_kernel(tc, x_words, x_scales, wq_words, wq_scales, wk_words, wk
         nc.vector.tensor_copy(zeros[0][:], seeds[0][:])
         nc.vector.memset(planes[:].bitcast(I32), 0)
         nc.vector.tensor_copy(zeros[1][:], seeds[1][:])
-        nc.vector.tensor_copy(zeros[2][:], seeds[2][:])
 
         def clear(window, zero):
             nc.scalar.copy(
@@ -98,11 +95,12 @@ def tile_moe_qkv_kernel(tc, x_words, x_scales, wq_words, wq_scales, wk_words, wk
         bias_q = tile_at([P, HALVES, ROW], F32, "bias_q", BIAS_AT)
         nc.sync.dma_start(out=bias_q[:, :, 0:E], in_=bias_rows[:, 0:HALVES])
         gates = tile_at([P, S], F32, "gates", GATES_AT)
-        q_rest = tile_at([P, E - EARLY, 2 * N], U8, "q_rest", Q_REST_AT)
+        q_mid = tile_at([P, MID - EARLY, 2 * N], U8, "q_mid", Q_MID_AT)
         nc.sync.dma_start(out=gates[:, 0 : EARLY * C], in_=gate[:, 0 : EARLY * C])
-        nc.sync.dma_start(out=q_rest[:, 0 : MID - EARLY].bitcast(I32), in_=q_rows[:, EARLY:MID])
+        nc.sync.dma_start(out=q_mid[:].bitcast(I32), in_=q_rows[:, EARLY:MID])
         nc.sync.dma_start(out=gates[:, EARLY * C : S], in_=gate[:, EARLY * C : S])
-        nc.sync.dma_start(out=q_rest[:, MID - EARLY :].bitcast(I32), in_=q_rows[:, MID:E])
+        q_late = tile([P, E - MID, 2 * N], U8, "q_late", tag="zero0")
+        nc.sync.dma_start(out=q_late[:].bitcast(I32), in_=q_rows[:, MID:E])
 
         def entries(e0, e1):
             return offsets[:, e0 * C // LIST : e1 * C // LIST]
@@ -119,15 +117,15 @@ def tile_moe_qkv_kernel(tc, x_words, x_scales, wq_words, wq_scales, wk_words, wk
         slot_w = gather(x_w[:].bitcast(U32), U32, "slot_w", QUERY_RUNS)
 
         def load_v(raw, e0):
-            nc.sync.dma_start(out=raw[:], in_=wv[e0 : e0 + QUANT].rearrange("e (p j) n -> p e j n", j=PACK))
+            nc.sync.dma_start(out=raw, in_=wv[e0 : e0 + QUANT].rearrange("e (p j) n -> p e j n", j=PACK))
             return raw
 
         raw_shape = [P, QUANT, PACK, N]
-        v_raw = [load_v(tile(raw_shape, F32, "v_raw0", tag="zero0"), 0)]
-        k_w = tile([P, E, N], I32, "k_w", tag="zero1")
-        nc.sync.dma_start(out=k_w[:], in_=wk_words.rearrange("e s p n d -> p (e s) (n d)").bitcast(I32))
-        bias_kv = tile([P, 2 * HALVES, ROW], F32, "bias_kv", tag="x_s")
+        v_raw = [load_v(tile(raw_shape, F32, "v_raw0", tag="x_s")[:], 0)]
+        bias_kv = tile_at([P, 2 * HALVES, ROW], F32, "bias_kv", Q_FIRST_AT)
         nc.sync.dma_start(out=bias_kv[:, :, 0:E], in_=bias_rows[:, HALVES : 3 * HALVES])
+        k_w = tile_at([P, E, N], I32, "k_w", K_AT)
+        nc.sync.dma_start(out=k_w[:], in_=wk_words.rearrange("e s p n d -> p (e s) (n d)").bitcast(I32))
 
         def project(y, weights, biases, bank, e0, e1):
             acc = psum.tile([P, 4 * C], F32, name="acc", tag=f"bank{bank}")
@@ -158,7 +156,7 @@ def tile_moe_qkv_kernel(tc, x_words, x_scales, wq_words, wq_scales, wk_words, wk
             nc.sync.dma_start(out=out[b * P : (b + 1) * P, :], in_=windows[b % WINDOWS][:])
 
         def q_weights(e, h):
-            words = q_first[:, e] if e < EARLY else q_rest[:, e - EARLY]
+            words = q_first[:, e] if e < EARLY else q_mid[:, e - EARLY] if e < MID else q_late[:, e - MID]
             return words[:, 2 * h * P : 2 * (h + 1) * P].bitcast(FP4X4), planes[:, e, h * P : (h + 1) * P]
 
         y_q = [tile([P, S], F32, f"y_q{h}") for h in range(HALVES)]
@@ -166,10 +164,10 @@ def tile_moe_qkv_kernel(tc, x_words, x_scales, wq_words, wq_scales, wk_words, wk
             for h in range(HALVES):
                 project(y_q[h], lambda e: q_weights(e, h), lambda e: bias_q[:, h, e : e + 1], HALVES * i + h, *run)
         load_scale_rows(planes[:].bitcast(I32), weight_scale_rows(wk_scales), PACK)
-        v_raw.append(load_v(tile_at(raw_shape, F32, "v_raw1", V1_AT), QUANT))
-        v_raw.append(load_v(tile_at(raw_shape, F32, "v_raw2", V2_AT), 2 * QUANT))
-        windows.append(tile_at([P, T], F32, "window2", BIAS_AT))
-        clear(windows[2], zeros[2])
+        v_late = tile([P, 2] + raw_shape[1:], F32, "v_late", tag="zero0")
+        v_raw.extend(load_v(v_late[:, i], (i + 1) * QUANT) for i in range(2))
+        windows.append(tile_at([P, T], F32, "window2", Q_MID_AT))
+        clear(windows[2], zeros[1])
 
         for run in QUERY_RUNS:
             for h in range(HALVES):
@@ -207,6 +205,6 @@ def tile_moe_qkv_kernel(tc, x_words, x_scales, wq_words, wq_scales, wk_words, wk
         def v_weights(h):
             return lambda e: (v_w[:, e, h * P : (h + 1) * P].bitcast(FP8X4), v_s[:, e, h * P : (h + 1) * P])
 
-        y_late = tile_at([P, 3, S], F32, "y_late", V2_AT)
+        y_late = tile([P, 3, S], F32, "y_late", tag="zero0")
         for i, weights in enumerate((k_weights(1), v_weights(0), v_weights(1))):
             whole_block(y_late[:, i], HALVES + 1 + i, weights, 0)

@@ -22,62 +22,75 @@ HALVES = N // P
 EARLY = 1
 MID = 3
 QUERY_RUNS = ((0, EARLY), (EARLY, MID), (MID, E))
-BANK_RUNS = ((0, 4), (4, E))
-WINDOWS = 3
+BYTES_FIRST = 4
 QUANT = 2
+PAIRS = E // QUANT
 SEED = 64
 ROW = 8
 
-K_AT = 0
-X_AT = K_AT + 4 * E * N - 4 * T
+X_AT = 0
 Q_FIRST_AT = X_AT + 4 * T
-GATES_AT = Q_FIRST_AT + EARLY * 2 * N
-BIAS_AT = GATES_AT + 4 * S
-Q_MID_AT = BIAS_AT + 4 * HALVES * ROW
+REST_AT = Q_FIRST_AT + EARLY * 2 * N
+BIAS_Q_AT = REST_AT
+BIAS_KV_AT = BIAS_Q_AT + 4 * HALVES * ROW
+GATES_AT = BIAS_KV_AT + 4 * 2 * HALVES * ROW
+Q_MID_AT = GATES_AT + 4 * S
+Q_LATE_AT = Q_MID_AT + (MID - EARLY) * 2 * N
+K_PLANE_AT = Q_LATE_AT + (E - MID) * 2 * N
+K_AT = K_PLANE_AT + E * N
+RAW_AT = K_AT + 4 * E * N
+RAW = 4 * QUANT * PACK * N
+WINDOW_AT = RAW_AT + PAIRS * RAW
+END_AT = WINDOW_AT + 4 * 4 * T
 
 
 def tile_moe_qkv_kernel(tc, x_words, x_scales, wq_words, wq_scales, wk_words, wk_scales, wv, bias, gate, offs, out):
     nc = tc.nc
-    mult = mybir.AluOpType.mult
-    add_bias = mybir.ActivationFunctionType.Identity
+    add, mult = mybir.AluOpType.add, mybir.AluOpType.mult
+    copy = mybir.ActivationFunctionType.Copy
 
     with ExitStack() as ctx:
         keep = ctx.enter_context(tc.tile_pool(name="keep", bufs=1))
         laid = ctx.enter_context(tc.tile_pool(name="laid", bufs=1))
         psum = ctx.enter_context(tc.psum_pool(name="psum", bufs=1))
 
-        def tile(shape, dtype, name, tag=None):
-            return keep.tile(shape, dtype, name=name, tag=tag or name, align_bytes=64)
+        def tile(shape, dtype, name):
+            return keep.tile(shape, dtype, name=name, align_bytes=64)
 
         def tile_at(shape, dtype, name, place):
             return laid.tile(shape, dtype, name=name, align_bytes=64, offset=place)
 
         offsets = keep.tile([P, S // LIST], U16, name="offsets")
         x_s = tile([P, T], U8, "x_s")
-        planes = tile([P, E, N], U8, "planes")
-        seeds = [tile_at([P, SEED], F32, f"seed{i}", at) for i, at in enumerate((Q_FIRST_AT - 128, BIAS_AT - 64))]
+        q_plane = tile([P, E, N], U8, "q_plane")
+        seeds = [
+            tile_at([P, SEED], F32, "seed0", Q_FIRST_AT - 128),
+            tile_at([P, (END_AT - REST_AT) // 4], F32, "seed1", REST_AT),
+        ]
         zeros = [tile([P, SEED], F32, f"zero{i}") for i in range(2)]
-        windows = [tile([P, T], F32, f"window{i}") for i in range(WINDOWS - 1)]
+        windows = [tile([P, T], F32, f"window{b}") for b in range(HALVES)]
 
         nc.vector.memset(x_s[:].bitcast(I32), 0)
         for seed in seeds:
-            nc.vector.memset(seed[:], 0.0)
+            nc.vector.memset(seed[:, 0:SEED], 0.0)
         nc.vector.tensor_copy(zeros[0][:], seeds[0][:])
-        nc.vector.memset(planes[:].bitcast(I32), 0)
-        nc.vector.tensor_copy(zeros[1][:], seeds[1][:])
+        nc.vector.memset(q_plane[:].bitcast(I32), 0)
+        nc.vector.tensor_copy(zeros[1][:], seeds[1][:, 0:SEED])
 
-        def clear(window, zero):
+        for window, zero in zip(windows, zeros):
             nc.scalar.copy(
                 out=window[:].rearrange("p (r c) -> p r c", c=SEED),
                 in_=zero[:].unsqueeze(1).to_broadcast([P, T // SEED, SEED]),
             )
+        k_plane = tile_at([P, E, N], U8, "k_plane", K_PLANE_AT)
+        nc.gpsimd.memset(k_plane[:].bitcast(I32), 0)
+        for i in range(2 * HALVES):
+            windows.append(tile_at([P, T], F32, f"window{HALVES + i}", WINDOW_AT + 4 * T * i))
+            nc.gpsimd.memset(windows[-1][:], 0.0)
 
-        for window, zero in zip(windows, zeros):
-            clear(window, zero)
-
-        def load_scale_rows(plane, rows, first=0):
+        def load_scale_rows(plane, rows):
             for r in range(PACK):
-                nc.sync.dma_start(out=plane[first + r : P : 32], in_=rows[r])
+                nc.sync.dma_start(out=plane[r:P:32], in_=rows[r])
 
         def weight_scale_rows(scales):
             return scales.bitcast(I32).rearrange("e s (q r) n -> r q (e s) n", r=PACK)
@@ -91,46 +104,56 @@ def tile_moe_qkv_kernel(tc, x_words, x_scales, wq_words, wq_scales, wk_words, wk
         nc.sync.dma_start(out=x_w[:], in_=x_words[0].rearrange("p t d -> p (t d)").bitcast(I32))
         q_first = tile_at([P, EARLY, 2 * N], U8, "q_first", Q_FIRST_AT)
         nc.sync.dma_start(out=q_first[:].bitcast(I32), in_=q_rows[:, 0:EARLY])
-        load_scale_rows(planes[:].bitcast(I32), weight_scale_rows(wq_scales))
-        bias_q = tile_at([P, HALVES, ROW], F32, "bias_q", BIAS_AT)
+        load_scale_rows(q_plane[:].bitcast(I32), weight_scale_rows(wq_scales))
+        bias_q = tile_at([P, HALVES, ROW], F32, "bias_q", BIAS_Q_AT)
         nc.sync.dma_start(out=bias_q[:, :, 0:E], in_=bias_rows[:, 0:HALVES])
         gates = tile_at([P, S], F32, "gates", GATES_AT)
-        q_mid = tile_at([P, MID - EARLY, 2 * N], U8, "q_mid", Q_MID_AT)
         nc.sync.dma_start(out=gates[:, 0 : EARLY * C], in_=gate[:, 0 : EARLY * C])
+        q_mid = tile_at([P, MID - EARLY, 2 * N], U8, "q_mid", Q_MID_AT)
         nc.sync.dma_start(out=q_mid[:].bitcast(I32), in_=q_rows[:, EARLY:MID])
         nc.sync.dma_start(out=gates[:, EARLY * C : S], in_=gate[:, EARLY * C : S])
-        q_late = tile([P, E - MID, 2 * N], U8, "q_late", tag="zero0")
+        q_late = tile_at([P, E - MID, 2 * N], U8, "q_late", Q_LATE_AT)
         nc.sync.dma_start(out=q_late[:].bitcast(I32), in_=q_rows[:, MID:E])
+        load_scale_rows(k_plane[:].bitcast(I32), weight_scale_rows(wk_scales))
+        k_w = tile_at([P, E, N], I32, "k_w", K_AT)
+        nc.sync.dma_start(out=k_w[:], in_=wk_words.rearrange("e s p n d -> p (e s) (n d)").bitcast(I32))
+        bias_kv = tile_at([P, 2 * HALVES, ROW], F32, "bias_kv", BIAS_KV_AT)
+        nc.sync.dma_start(out=bias_kv[:, :, 0:E], in_=bias_rows[:, HALVES : 3 * HALVES])
+        v_raw = []
+        for i in range(PAIRS):
+            v_raw.append(tile_at([P, QUANT, PACK, N], F32, f"v_raw{i}", RAW_AT + i * RAW))
+            nc.sync.dma_start(out=v_raw[i][:], in_=wv[i * QUANT : (i + 1) * QUANT].rearrange("e (p j) n -> p e j n", j=PACK))
 
         def entries(e0, e1):
             return offsets[:, e0 * C // LIST : e1 * C // LIST]
 
-        def gather(table, dtype, name, runs):
-            slots = []
-            for e0, e1 in runs:
-                part = tile([P, (e1 - e0) * C], dtype, f"{name}{e0}")
-                nc.vector.tensor_copy(part[:], table.indirect(entries(e0, e1)))
-                slots.extend(part[:, (e - e0) * C : (e - e0 + 1) * C] for e in range(e0, e1))
-            return slots
+        slot_s, slot_w = [], []
 
-        slot_s = gather(x_s[:], U8, "slot_s", [(0, E)])
-        slot_w = gather(x_w[:].bitcast(U32), U32, "slot_w", QUERY_RUNS)
+        def gather(slots, part, table, e0, e1):
+            nc.vector.tensor_copy(part[:], table.indirect(entries(e0, e1)))
+            slots.extend(part[:, i * C : (i + 1) * C] for i in range(e1 - e0))
 
-        def load_v(raw, e0):
-            nc.sync.dma_start(out=raw, in_=wv[e0 : e0 + QUANT].rearrange("e (p j) n -> p e j n", j=PACK))
-            return raw
+        def gather_words(e0, e1):
+            gather(slot_w, tile([P, (e1 - e0) * C], U32, f"slot_w{e0}"), x_w[:].bitcast(U32), e0, e1)
 
-        raw_shape = [P, QUANT, PACK, N]
-        v_raw = [load_v(tile(raw_shape, F32, "v_raw0", tag="x_s")[:], 0)]
-        bias_kv = tile_at([P, 2 * HALVES, ROW], F32, "bias_kv", Q_FIRST_AT)
-        nc.sync.dma_start(out=bias_kv[:, :, 0:E], in_=bias_rows[:, HALVES : 3 * HALVES])
-        k_w = tile_at([P, E, N], I32, "k_w", K_AT)
-        nc.sync.dma_start(out=k_w[:], in_=wk_words.rearrange("e s p n d -> p (e s) (n d)").bitcast(I32))
+        v_w = tile([P, E, N], U32, "v_w")
+        v_s = tile([P, E, N], U8, "v_s")
 
-        def project(y, weights, biases, bank, e0, e1):
-            acc = psum.tile([P, 4 * C], F32, name="acc", tag=f"bank{bank}")
+        def weights(b, e):
+            cols = slice(b % HALVES * P, (b % HALVES + 1) * P)
+            if b < HALVES:
+                words = q_first[:, e] if e < EARLY else q_mid[:, e - EARLY] if e < MID else q_late[:, e - MID]
+                return words[:, 2 * cols.start : 2 * cols.stop].bitcast(FP4X4), q_plane[:, e, cols]
+            if b < 2 * HALVES:
+                return k_w[:, e, cols].bitcast(FP8X4), k_plane[:, e, cols]
+            return v_w[:, e, cols].bitcast(FP8X4), v_s[:, e, cols]
+
+        def bank(i):
+            return psum.tile([P, 4 * C], F32, name="acc", tag=f"bank{i}")
+
+        def multiply(acc, b, e0, e1):
             for e in range(e0, e1):
-                w_codes, w_scales = weights(e)
+                w_codes, w_scales = weights(b, e)
                 nc.tensor.matmul_mx(
                     out=acc[:, (e - e0) * C : (e - e0 + 1) * C],
                     lhsT=w_codes,
@@ -140,71 +163,82 @@ def tile_moe_qkv_kernel(tc, x_words, x_scales, wq_words, wq_scales, wk_words, wk
                     start=True,
                     stop=True,
                 )
-            for e in range(e0, e1):
-                nc.scalar.activation(
-                    out=y[:, e * C : (e + 1) * C],
-                    in_=acc[:, (e - e0) * C : (e - e0 + 1) * C],
-                    func=add_bias,
-                    bias=biases(e),
-                )
 
-        def scatter(y, b, e0, e1):
-            cols = slice(e0 * C, e1 * C)
-            nc.vector.tensor_tensor(windows[b % WINDOWS][:].indirect(entries(e0, e1)), y[:, cols], gates[:, cols], mult)
+        def finish(y, acc, b, e0, e1):
+            biases = bias_q[:, b] if b < HALVES else bias_kv[:, b - HALVES]
+            for e in range(e0, e1):
+                cols = slice((e - e0) * C, (e - e0 + 1) * C)
+                nc.vector.scalar_tensor_tensor(y[:, cols], acc[:, cols], biases[:, e : e + 1], gates[:, e * C : (e + 1) * C], add, mult)
+
+        def scatter_on_scalar(y, b, e0, e1):
+            nc.scalar.activation(windows[b][:].indirect(entries(e0, e1)), y, copy)
+
+        def scatter_on_vector(y, b, e0, e1):
+            nc.vector.tensor_copy(windows[b][:].indirect(entries(e0, e1)), y)
 
         def store(b):
-            nc.sync.dma_start(out=out[b * P : (b + 1) * P, :], in_=windows[b % WINDOWS][:])
+            nc.sync.dma_start(out=out[b * P : (b + 1) * P, :], in_=windows[b][:])
 
-        def q_weights(e, h):
-            words = q_first[:, e] if e < EARLY else q_mid[:, e - EARLY] if e < MID else q_late[:, e - MID]
-            return words[:, 2 * h * P : 2 * (h + 1) * P].bitcast(FP4X4), planes[:, e, h * P : (h + 1) * P]
+        def part(y, i, b, e0, e1):
+            acc = bank(i)
+            multiply(acc, b, e0, e1)
+            finish(y, acc, b, e0, e1)
+            scatter_on_scalar(y[:], b, e0, e1)
 
-        y_q = [tile([P, S], F32, f"y_q{h}") for h in range(HALVES)]
-        for i, run in enumerate(QUERY_RUNS):
-            for h in range(HALVES):
-                project(y_q[h], lambda e: q_weights(e, h), lambda e: bias_q[:, h, e : e + 1], HALVES * i + h, *run)
-        load_scale_rows(planes[:].bitcast(I32), weight_scale_rows(wk_scales), PACK)
-        v_late = tile([P, 2] + raw_shape[1:], F32, "v_late", tag="zero0")
-        v_raw.extend(load_v(v_late[:, i], (i + 1) * QUANT) for i in range(2))
-        windows.append(tile_at([P, T], F32, "window2", Q_MID_AT))
-        clear(windows[2], zeros[1])
-
-        for run in QUERY_RUNS:
-            for h in range(HALVES):
-                scatter(y_q[h], h, *run)
-        for h in range(HALVES):
-            store(h)
-
-        def whole_block(y, b, weights, bank):
-            for i, run in enumerate(BANK_RUNS):
-                project(y, weights, lambda e: bias_kv[:, b - HALVES, e : e + 1], bank + i, *run)
-            scatter(y, b, 0, E)
+        gather(slot_s, tile([P, BYTES_FIRST * C], U8, "slot_s0"), x_s[:], 0, BYTES_FIRST)
+        for i, (e0, e1) in enumerate(QUERY_RUNS):
+            if e1 > BYTES_FIRST:
+                gather(slot_s, tile_at([P, (E - BYTES_FIRST) * C], U8, "slot_s1", Q_FIRST_AT), x_s[:], BYTES_FIRST, E)
+            gather_words(e0, e1)
+            for b in range(HALVES):
+                part(tile([P, (e1 - e0) * C], F32, f"y{b}_{e0}"), HALVES * i + b, b, e0, e1)
+        for b in range(HALVES):
             store(b)
 
-        def k_weights(h):
-            return lambda e: (k_w[:, e, h * P : (h + 1) * P].bitcast(FP8X4), planes[PACK:P, e, h * P : (h + 1) * P])
+        grouped = [tile([P, QUANT, N, PACK], BF16, f"grouped{i}") for i in range(PAIRS)]
 
-        whole_block(tile([P, S], F32, "y_k0"), HALVES, k_weights(0), 6)
-
-        v_w = tile([P, E, N], U32, "v_w")
-        v_s = tile([P, E, N], U8, "v_s")
-        for i, raw in enumerate(v_raw):
-            e0 = i * QUANT
-            grouped = tile([P, QUANT, N, PACK], BF16, f"grouped{e0}")
-            for e in range(QUANT):
-                nc.scalar.copy(
-                    out=grouped[:, e].rearrange("p (c i) t -> p c t i", i=4),
-                    in_=raw[:, e].rearrange("p t (c i) -> p c t i", i=4),
-                )
-            nc.vector.quantize_mx(
-                out=v_w[:, e0 : e0 + QUANT].rearrange("p e n -> p (e n)").bitcast(FP8X4),
-                scales=v_s[:, e0 : e0 + QUANT].rearrange("p e n -> p (e n)"),
-                in_=grouped[:].rearrange("p e n t -> p (e n t)"),
+        def lay_out(i):
+            nc.vector.tensor_copy(
+                out=grouped[i][:].rearrange("p e (c i) t -> p e c t i", i=4),
+                in_=v_raw[i][:].rearrange("p e t (c i) -> p e c t i", i=4),
             )
 
-        def v_weights(h):
-            return lambda e: (v_w[:, e, h * P : (h + 1) * P].bitcast(FP8X4), v_s[:, e, h * P : (h + 1) * P])
+        def quantise(i):
+            pair = slice(i * QUANT, (i + 1) * QUANT)
+            nc.vector.quantize_mx(
+                out=v_w[:, pair].rearrange("p e n -> p (e n)").bitcast(FP8X4),
+                scales=v_s[:, pair].rearrange("p e n -> p (e n)"),
+                in_=grouped[i][:].rearrange("p e n t -> p (e n t)"),
+            )
 
-        y_late = tile([P, 3, S], F32, "y_late", tag="zero0")
-        for i, weights in enumerate((k_weights(1), v_weights(0), v_weights(1))):
-            whole_block(y_late[:, i], HALVES + 1 + i, weights, 0)
+        K0, K1, V0, V1 = 2, 3, 4, 5
+        half = E // 2
+        part(tile([P, half * C], F32, "y_k0a"), 6, K0, 0, half)
+        lay_out(0)
+        part(tile_at([P, half * C], F32, "y_k1a", RAW_AT), 7, K1, 0, half)
+        quantise(0)
+        lay_out(1)
+        part(tile_at([P, QUANT * C], F32, "y_v1a", RAW_AT + RAW), 0, V1, 0, QUANT)
+        quantise(1)
+        lay_out(2)
+        last = RAW_AT + 2 * RAW
+        part(tile_at([P, half * C], F32, "y_k0b", last), 1, K0, half, E)
+        store(K0)
+        quantise(2)
+        y_v0 = tile_at([P, S], F32, "y_v0", last + 4 * half * C)
+        y_v1 = tile_at([P, S - QUANT * C], F32, "y_v1b", last + 4 * half * C + 4 * S)
+        acc = bank(2)
+        multiply(acc, V0, 0, 4)
+        finish(y_v0[:, 0 : 4 * C], acc, V0, 0, 4)
+        part(tile_at([P, half * C], F32, "y_k1b", last + RAW - 4 * half * C), 3, K1, half, E)
+        acc = bank(4)
+        multiply(acc, V0, 4, E)
+        finish(y_v0[:, 4 * C : S], acc, V0, 4, E)
+        acc = bank(5)
+        multiply(acc, V1, QUANT, E)
+        finish(y_v1, acc, V1, QUANT, E)
+        scatter_on_vector(y_v0[:], V0, 0, E)
+        store(V0)
+        scatter_on_vector(y_v1[:], V1, QUANT, E)
+        store(V1)
+        store(K1)

@@ -27,13 +27,17 @@ QUANT = 2
 PAIRS = E // QUANT
 SEED = 64
 ROW = 8
+HALF = E // 2
+SHARE = 1
 
 X_AT = 0
 Q_FIRST_AT = X_AT + 4 * T
 REST_AT = Q_FIRST_AT + EARLY * 2 * N
 BIAS_Q_AT = REST_AT
 BIAS_KV_AT = BIAS_Q_AT + 4 * HALVES * ROW
-GATES_AT = BIAS_KV_AT + 4 * 2 * HALVES * ROW
+GATES_FIRST_AT = BIAS_KV_AT + 4 * 2 * HALVES * ROW
+LATE_WORDS_AT = GATES_FIRST_AT + (E - BYTES_FIRST) * C
+GATES_AT = LATE_WORDS_AT + 4 * (E - MID) * C
 Q_MID_AT = GATES_AT + 4 * S
 Q_LATE_AT = Q_MID_AT + (MID - EARLY) * 2 * N
 K_PLANE_AT = Q_LATE_AT + (E - MID) * 2 * N
@@ -107,22 +111,26 @@ def tile_moe_qkv_kernel(tc, x_words, x_scales, wq_words, wq_scales, wk_words, wk
         load_scale_rows(q_plane[:].bitcast(I32), weight_scale_rows(wq_scales))
         bias_q = tile_at([P, HALVES, ROW], F32, "bias_q", BIAS_Q_AT)
         nc.sync.dma_start(out=bias_q[:, :, 0:E], in_=bias_rows[:, 0:HALVES])
-        gates = tile_at([P, S], F32, "gates", GATES_AT)
-        nc.sync.dma_start(out=gates[:, 0 : EARLY * C], in_=gate[:, 0 : EARLY * C])
+        gates_first = tile_at([P, EARLY * C], F32, "gates_first", GATES_FIRST_AT)
+        nc.sync.dma_start(out=gates_first[:], in_=gate[:, 0 : EARLY * C])
         q_mid = tile_at([P, MID - EARLY, 2 * N], U8, "q_mid", Q_MID_AT)
         nc.sync.dma_start(out=q_mid[:].bitcast(I32), in_=q_rows[:, EARLY:MID])
-        nc.sync.dma_start(out=gates[:, EARLY * C : S], in_=gate[:, EARLY * C : S])
+        gates = tile_at([P, S], F32, "gates", GATES_AT)
+        nc.sync.dma_start(out=gates[:], in_=gate)
         q_late = tile_at([P, E - MID, 2 * N], U8, "q_late", Q_LATE_AT)
         nc.sync.dma_start(out=q_late[:].bitcast(I32), in_=q_rows[:, MID:E])
         load_scale_rows(k_plane[:].bitcast(I32), weight_scale_rows(wk_scales))
-        k_w = tile_at([P, E, N], I32, "k_w", K_AT)
-        nc.sync.dma_start(out=k_w[:], in_=wk_words.rearrange("e s p n d -> p (e s) (n d)").bitcast(I32))
+        k_rows = wk_words.rearrange("e s p n d -> p (e s) (n d)").bitcast(I32)
+        k_w = [tile_at([P, HALF, N], I32, f"k_w{i}", K_AT + i * 4 * HALF * N) for i in range(2)]
+        nc.sync.dma_start(out=k_w[0][:], in_=k_rows[:, 0:HALF])
         bias_kv = tile_at([P, 2 * HALVES, ROW], F32, "bias_kv", BIAS_KV_AT)
         nc.sync.dma_start(out=bias_kv[:, :, 0:E], in_=bias_rows[:, HALVES : 3 * HALVES])
         v_raw = []
         for i in range(PAIRS):
             v_raw.append(tile_at([P, QUANT, PACK, N], F32, f"v_raw{i}", RAW_AT + i * RAW))
             nc.sync.dma_start(out=v_raw[i][:], in_=wv[i * QUANT : (i + 1) * QUANT].rearrange("e (p j) n -> p e j n", j=PACK))
+            if i == 0:
+                nc.sync.dma_start(out=k_w[1][:], in_=k_rows[:, HALF:E])
 
         def entries(e0, e1):
             return offsets[:, e0 * C // LIST : e1 * C // LIST]
@@ -134,7 +142,9 @@ def tile_moe_qkv_kernel(tc, x_words, x_scales, wq_words, wq_scales, wk_words, wk
             slots.extend(part[:, i * C : (i + 1) * C] for i in range(e1 - e0))
 
         def gather_words(e0, e1):
-            gather(slot_w, tile([P, (e1 - e0) * C], U32, f"slot_w{e0}"), x_w[:].bitcast(U32), e0, e1)
+            shape = [P, (e1 - e0) * C]
+            words = tile(shape, U32, f"slot_w{e0}") if e0 < MID else tile_at(shape, U32, f"slot_w{e0}", LATE_WORDS_AT)
+            gather(slot_w, words, x_w[:].bitcast(U32), e0, e1)
 
         v_w = tile([P, E, N], U32, "v_w")
         v_s = tile([P, E, N], U8, "v_s")
@@ -145,7 +155,7 @@ def tile_moe_qkv_kernel(tc, x_words, x_scales, wq_words, wq_scales, wk_words, wk
                 words = q_first[:, e] if e < EARLY else q_mid[:, e - EARLY] if e < MID else q_late[:, e - MID]
                 return words[:, 2 * cols.start : 2 * cols.stop].bitcast(FP4X4), q_plane[:, e, cols]
             if b < 2 * HALVES:
-                return k_w[:, e, cols].bitcast(FP8X4), k_plane[:, e, cols]
+                return k_w[e // HALF][:, e % HALF, cols].bitcast(FP8X4), k_plane[:, e, cols]
             return v_w[:, e, cols].bitcast(FP8X4), v_s[:, e, cols]
 
         def bank(i):
@@ -166,15 +176,24 @@ def tile_moe_qkv_kernel(tc, x_words, x_scales, wq_words, wq_scales, wk_words, wk
 
         def finish(y, acc, b, e0, e1):
             biases = bias_q[:, b] if b < HALVES else bias_kv[:, b - HALVES]
+            table = gates_first if b < HALVES and e1 <= EARLY else gates
             for e in range(e0, e1):
                 cols = slice((e - e0) * C, (e - e0 + 1) * C)
-                nc.vector.scalar_tensor_tensor(y[:, cols], acc[:, cols], biases[:, e : e + 1], gates[:, e * C : (e + 1) * C], add, mult)
+                nc.vector.scalar_tensor_tensor(y[:, cols], acc[:, cols], biases[:, e : e + 1], table[:, e * C : (e + 1) * C], add, mult)
+
+        def add_bias(y, acc, b, e0, e1):
+            nc.vector.tensor_tensor(
+                y.rearrange("p (e c) -> p e c", c=C),
+                acc.rearrange("p (e c) -> p e c", c=C),
+                bias_kv[:, b - HALVES, e0:e1].unsqueeze(2).to_broadcast([P, e1 - e0, C]),
+                add,
+            )
 
         def scatter_on_scalar(y, b, e0, e1):
             nc.scalar.activation(windows[b][:].indirect(entries(e0, e1)), y, copy)
 
         def scatter_on_vector(y, b, e0, e1):
-            nc.vector.tensor_copy(windows[b][:].indirect(entries(e0, e1)), y)
+            nc.vector.tensor_tensor(windows[b][:].indirect(entries(e0, e1)), y, gates[:, e0 * C : e1 * C], mult)
 
         def store(b):
             nc.sync.dma_start(out=out[b * P : (b + 1) * P, :], in_=windows[b][:])
@@ -188,7 +207,7 @@ def tile_moe_qkv_kernel(tc, x_words, x_scales, wq_words, wq_scales, wk_words, wk
         gather(slot_s, tile([P, BYTES_FIRST * C], U8, "slot_s0"), x_s[:], 0, BYTES_FIRST)
         for i, (e0, e1) in enumerate(QUERY_RUNS):
             if e1 > BYTES_FIRST:
-                gather(slot_s, tile_at([P, (E - BYTES_FIRST) * C], U8, "slot_s1", Q_FIRST_AT), x_s[:], BYTES_FIRST, E)
+                gather(slot_s, tile_at([P, (E - BYTES_FIRST) * C], U8, "slot_s1", GATES_FIRST_AT), x_s[:], BYTES_FIRST, E)
             gather_words(e0, e1)
             for b in range(HALVES):
                 part(tile([P, (e1 - e0) * C], F32, f"y{b}_{e0}"), HALVES * i + b, b, e0, e1)
@@ -212,33 +231,52 @@ def tile_moe_qkv_kernel(tc, x_words, x_scales, wq_words, wq_scales, wk_words, wk
             )
 
         K0, K1, V0, V1 = 2, 3, 4, 5
-        half = E // 2
-        part(tile([P, half * C], F32, "y_k0a"), 6, K0, 0, half)
+
+        def result(name, experts, place):
+            return tile_at([P, experts * C], F32, name, place)
+
+        def value_run(i, e0, e1, place):
+            acc = bank(i)
+            width = (e1 - e0) * C
+            for h in range(HALVES):
+                multiply(acc[:, h * width : (h + 1) * width], V0 + h, e0, e1)
+            for h in range(HALVES):
+                y = result(f"y_v{h}_{e0}", e1 - e0, place + 4 * h * width)
+                finish(y, acc[:, h * width : (h + 1) * width], V0 + h, e0, e1)
+                scatter_on_scalar(y[:], V0 + h, e0, e1)
+
+        acc = bank(6)
+        multiply(acc, K0, 0, HALF)
+        y = tile([P, HALF * C], F32, "y_k0a")
+        add_bias(y[:], acc[:, 0 : HALF * C], K0, 0, HALF)
+        scatter_on_vector(y[:], K0, 0, HALF)
         lay_out(0)
-        part(tile_at([P, half * C], F32, "y_k1a", RAW_AT), 7, K1, 0, half)
+        own = E - SHARE
+        acc_k0 = bank(7)
+        multiply(acc_k0, K0, HALF, E)
+        y = tile([P, SHARE * C], F32, "y_k0c")
+        finish(y, acc_k0[:, (own - HALF) * C : HALF * C], K0, own, E)
+        scatter_on_scalar(y[:], K0, own, E)
         quantise(0)
         lay_out(1)
-        part(tile_at([P, QUANT * C], F32, "y_v1a", RAW_AT + RAW), 0, V1, 0, QUANT)
+        value_run(2, 0, QUANT, RAW_AT + RAW)
         quantise(1)
         lay_out(2)
         last = RAW_AT + 2 * RAW
-        part(tile_at([P, half * C], F32, "y_k0b", last), 1, K0, half, E)
-        store(K0)
+        value_run(3, QUANT, HALF, last)
         quantise(2)
-        y_v0 = tile_at([P, S], F32, "y_v0", last + 4 * half * C)
-        y_v1 = tile_at([P, S - QUANT * C], F32, "y_v1b", last + 4 * half * C + 4 * S)
-        acc = bank(2)
-        multiply(acc, V0, 0, 4)
-        finish(y_v0[:, 0 : 4 * C], acc, V0, 0, 4)
-        part(tile_at([P, half * C], F32, "y_k1b", last + RAW - 4 * half * C), 3, K1, half, E)
-        acc = bank(4)
-        multiply(acc, V0, 4, E)
-        finish(y_v0[:, 4 * C : S], acc, V0, 4, E)
-        acc = bank(5)
-        multiply(acc, V1, QUANT, E)
-        finish(y_v1, acc, V1, QUANT, E)
-        scatter_on_vector(y_v0[:], V0, 0, E)
+        y_k1 = result("y_k1", E, last + 4 * 2 * C)
+        for i in range(2):
+            acc = bank(i)
+            multiply(acc, K1, i * HALF, (i + 1) * HALF)
+            add_bias(y_k1[:, i * HALF * C : (i + 1) * HALF * C], acc[:, 0 : HALF * C], K1, i * HALF, (i + 1) * HALF)
+        y_k0 = result("y_k0b", own - HALF, last + 4 * 8 * C)
+        add_bias(y_k0[:], acc_k0[:, 0 : (own - HALF) * C], K0, HALF, own)
+        for h in range(HALVES):
+            part(result(f"y_v{h}_late", HALF, last + 4 * (10 + h * HALF) * C), 4 + h, V0 + h, HALF, E)
+        scatter_on_vector(y_k0[:], K0, HALF, own)
+        store(K0)
         store(V0)
-        scatter_on_vector(y_v1[:], V1, QUANT, E)
         store(V1)
+        scatter_on_vector(y_k1[:], K1, 0, E)
         store(K1)

@@ -22,30 +22,27 @@ HALVES = N // P
 EARLY = 1
 MID = 3
 QUERY_RUNS = ((0, EARLY), (EARLY, MID), (MID, E))
-BYTES_FIRST = 4
 QUANT = 2
 PAIRS = E // QUANT
 SEED = 64
 ROW = 8
+WINDOWS = 4
 HALF = E // 2
-SHARE = 1
 
 X_AT = 0
 Q_FIRST_AT = X_AT + 4 * T
-REST_AT = Q_FIRST_AT + EARLY * 2 * N
-BIAS_Q_AT = REST_AT
-BIAS_KV_AT = BIAS_Q_AT + 4 * HALVES * ROW
-GATES_FIRST_AT = BIAS_KV_AT + 4 * 2 * HALVES * ROW
-LATE_WORDS_AT = GATES_FIRST_AT + (E - BYTES_FIRST) * C
-GATES_AT = LATE_WORDS_AT + 4 * (E - MID) * C
-Q_MID_AT = GATES_AT + 4 * S
-Q_LATE_AT = Q_MID_AT + (MID - EARLY) * 2 * N
-K_PLANE_AT = Q_LATE_AT + (E - MID) * 2 * N
-K_AT = K_PLANE_AT + E * N
+BIAS_Q_AT = Q_FIRST_AT + MID * 2 * N
+GATES_FIRST_AT = BIAS_Q_AT + 4 * HALVES * ROW
+REST_AT = BIAS_Q_AT
+BIAS_KV_AT = GATES_FIRST_AT + 4 * (E - MID) * C
+GATES_AT = BIAS_KV_AT + 4 * 2 * HALVES * ROW
+Q_LATE_AT = GATES_AT + 4 * S
+WINDOW2_AT = Q_LATE_AT + (E - MID) * 2 * N
+WINDOW3_AT = WINDOW2_AT + 4 * T
+K_AT = WINDOW3_AT + 4 * T - 64
 RAW_AT = K_AT + 4 * E * N
 RAW = 4 * QUANT * PACK * N
-WINDOW_AT = RAW_AT + PAIRS * RAW
-END_AT = WINDOW_AT + 4 * 4 * T
+END_AT = RAW_AT + PAIRS * RAW
 
 
 def tile_moe_qkv_kernel(tc, x_words, x_scales, wq_words, wq_scales, wk_words, wk_scales, wv, bias, gate, offs, out):
@@ -66,7 +63,8 @@ def tile_moe_qkv_kernel(tc, x_words, x_scales, wq_words, wq_scales, wk_words, wk
 
         offsets = keep.tile([P, S // LIST], U16, name="offsets")
         x_s = tile([P, T], U8, "x_s")
-        q_plane = tile([P, E, N], U8, "q_plane")
+        planes = tile([P, 2, E, N], U8, "planes")
+        q_plane, k_plane = planes[:, 0], planes[:, 1]
         seeds = [
             tile_at([P, SEED], F32, "seed0", Q_FIRST_AT - 128),
             tile_at([P, (END_AT - REST_AT) // 4], F32, "seed1", REST_AT),
@@ -77,8 +75,8 @@ def tile_moe_qkv_kernel(tc, x_words, x_scales, wq_words, wq_scales, wk_words, wk
         nc.vector.memset(x_s[:].bitcast(I32), 0)
         for seed in seeds:
             nc.vector.memset(seed[:, 0:SEED], 0.0)
-        nc.vector.tensor_copy(zeros[0][:], seeds[0][:])
-        nc.vector.memset(q_plane[:].bitcast(I32), 0)
+        nc.vector.tensor_copy(zeros[0][:], seeds[0][:, 0:SEED])
+        nc.vector.memset(planes[:].bitcast(I32), 0)
         nc.vector.tensor_copy(zeros[1][:], seeds[1][:, 0:SEED])
 
         for window, zero in zip(windows, zeros):
@@ -86,11 +84,8 @@ def tile_moe_qkv_kernel(tc, x_words, x_scales, wq_words, wq_scales, wk_words, wk
                 out=window[:].rearrange("p (r c) -> p r c", c=SEED),
                 in_=zero[:].unsqueeze(1).to_broadcast([P, T // SEED, SEED]),
             )
-        k_plane = tile_at([P, E, N], U8, "k_plane", K_PLANE_AT)
-        nc.gpsimd.memset(k_plane[:].bitcast(I32), 0)
-        for i in range(2 * HALVES):
-            windows.append(tile_at([P, T], F32, f"window{HALVES + i}", WINDOW_AT + 4 * T * i))
-            nc.gpsimd.memset(windows[-1][:], 0.0)
+        windows.append(tile_at([P, T], F32, "window2", WINDOW2_AT))
+        nc.gpsimd.memset(windows[2][:], 0.0)
 
         def load_scale_rows(plane, rows):
             for r in range(PACK):
@@ -106,31 +101,28 @@ def tile_moe_qkv_kernel(tc, x_words, x_scales, wq_words, wq_scales, wk_words, wk
         load_scale_rows(x_s[:].bitcast(I32), x_scales[0].bitcast(I32).rearrange("(q r) t -> r q t", r=PACK))
         x_w = tile_at([P, T], I32, "x_w", X_AT)
         nc.sync.dma_start(out=x_w[:], in_=x_words[0].rearrange("p t d -> p (t d)").bitcast(I32))
-        q_first = tile_at([P, EARLY, 2 * N], U8, "q_first", Q_FIRST_AT)
-        nc.sync.dma_start(out=q_first[:].bitcast(I32), in_=q_rows[:, 0:EARLY])
-        load_scale_rows(q_plane[:].bitcast(I32), weight_scale_rows(wq_scales))
+        q_first = tile_at([P, MID, 2 * N], U8, "q_first", Q_FIRST_AT)
+        nc.sync.dma_start(out=q_first[:].bitcast(I32), in_=q_rows[:, 0:MID])
+        load_scale_rows(q_plane.bitcast(I32), weight_scale_rows(wq_scales))
         bias_q = tile_at([P, HALVES, ROW], F32, "bias_q", BIAS_Q_AT)
         nc.sync.dma_start(out=bias_q[:, :, 0:E], in_=bias_rows[:, 0:HALVES])
         gates_first = tile_at([P, EARLY * C], F32, "gates_first", GATES_FIRST_AT)
         nc.sync.dma_start(out=gates_first[:], in_=gate[:, 0 : EARLY * C])
-        q_mid = tile_at([P, MID - EARLY, 2 * N], U8, "q_mid", Q_MID_AT)
-        nc.sync.dma_start(out=q_mid[:].bitcast(I32), in_=q_rows[:, EARLY:MID])
         gates = tile_at([P, S], F32, "gates", GATES_AT)
         nc.sync.dma_start(out=gates[:], in_=gate)
         q_late = tile_at([P, E - MID, 2 * N], U8, "q_late", Q_LATE_AT)
         nc.sync.dma_start(out=q_late[:].bitcast(I32), in_=q_rows[:, MID:E])
-        load_scale_rows(k_plane[:].bitcast(I32), weight_scale_rows(wk_scales))
+        load_scale_rows(k_plane.bitcast(I32), weight_scale_rows(wk_scales))
         k_rows = wk_words.rearrange("e s p n d -> p (e s) (n d)").bitcast(I32)
         k_w = [tile_at([P, HALF, N], I32, f"k_w{i}", K_AT + i * 4 * HALF * N) for i in range(2)]
         nc.sync.dma_start(out=k_w[0][:], in_=k_rows[:, 0:HALF])
         bias_kv = tile_at([P, 2 * HALVES, ROW], F32, "bias_kv", BIAS_KV_AT)
         nc.sync.dma_start(out=bias_kv[:, :, 0:E], in_=bias_rows[:, HALVES : 3 * HALVES])
+        nc.sync.dma_start(out=k_w[1][:], in_=k_rows[:, HALF:E])
         v_raw = []
         for i in range(PAIRS):
             v_raw.append(tile_at([P, QUANT, PACK, N], F32, f"v_raw{i}", RAW_AT + i * RAW))
             nc.sync.dma_start(out=v_raw[i][:], in_=wv[i * QUANT : (i + 1) * QUANT].rearrange("e (p j) n -> p e j n", j=PACK))
-            if i == 0:
-                nc.sync.dma_start(out=k_w[1][:], in_=k_rows[:, HALF:E])
 
         def entries(e0, e1):
             return offsets[:, e0 * C // LIST : e1 * C // LIST]
@@ -143,7 +135,7 @@ def tile_moe_qkv_kernel(tc, x_words, x_scales, wq_words, wq_scales, wk_words, wk
 
         def gather_words(e0, e1):
             shape = [P, (e1 - e0) * C]
-            words = tile(shape, U32, f"slot_w{e0}") if e0 < MID else tile_at(shape, U32, f"slot_w{e0}", LATE_WORDS_AT)
+            words = tile(shape, U32, f"slot_w{e0}") if e0 < MID else tile_at(shape, U32, f"slot_w{e0}", GATES_FIRST_AT)
             gather(slot_w, words, x_w[:].bitcast(U32), e0, e1)
 
         v_w = tile([P, E, N], U32, "v_w")
@@ -152,7 +144,7 @@ def tile_moe_qkv_kernel(tc, x_words, x_scales, wq_words, wq_scales, wk_words, wk
         def weights(b, e):
             cols = slice(b % HALVES * P, (b % HALVES + 1) * P)
             if b < HALVES:
-                words = q_first[:, e] if e < EARLY else q_mid[:, e - EARLY] if e < MID else q_late[:, e - MID]
+                words = q_first[:, e] if e < MID else q_late[:, e - MID]
                 return words[:, 2 * cols.start : 2 * cols.stop].bitcast(FP4X4), q_plane[:, e, cols]
             if b < 2 * HALVES:
                 return k_w[e // HALF][:, e % HALF, cols].bitcast(FP8X4), k_plane[:, e, cols]
@@ -182,21 +174,22 @@ def tile_moe_qkv_kernel(tc, x_words, x_scales, wq_words, wq_scales, wk_words, wk
                 nc.vector.scalar_tensor_tensor(y[:, cols], acc[:, cols], biases[:, e : e + 1], table[:, e * C : (e + 1) * C], add, mult)
 
         def add_bias(y, acc, b, e0, e1):
+            biases = bias_q[:, b] if b < HALVES else bias_kv[:, b - HALVES]
             nc.vector.tensor_tensor(
                 y.rearrange("p (e c) -> p e c", c=C),
                 acc.rearrange("p (e c) -> p e c", c=C),
-                bias_kv[:, b - HALVES, e0:e1].unsqueeze(2).to_broadcast([P, e1 - e0, C]),
+                biases[:, e0:e1].unsqueeze(2).to_broadcast([P, e1 - e0, C]),
                 add,
             )
 
         def scatter_on_scalar(y, b, e0, e1):
-            nc.scalar.activation(windows[b][:].indirect(entries(e0, e1)), y, copy)
+            nc.scalar.activation(windows[b % WINDOWS][:].indirect(entries(e0, e1)), y, copy)
 
         def scatter_on_vector(y, b, e0, e1):
-            nc.vector.tensor_tensor(windows[b][:].indirect(entries(e0, e1)), y, gates[:, e0 * C : e1 * C], mult)
+            nc.vector.tensor_tensor(windows[b % WINDOWS][:].indirect(entries(e0, e1)), y, gates[:, e0 * C : e1 * C], mult)
 
         def store(b):
-            nc.sync.dma_start(out=out[b * P : (b + 1) * P, :], in_=windows[b][:])
+            nc.sync.dma_start(out=out[b * P : (b + 1) * P, :], in_=windows[b % WINDOWS][:])
 
         def part(y, i, b, e0, e1):
             acc = bank(i)
@@ -204,15 +197,27 @@ def tile_moe_qkv_kernel(tc, x_words, x_scales, wq_words, wq_scales, wk_words, wk
             finish(y, acc, b, e0, e1)
             scatter_on_scalar(y[:], b, e0, e1)
 
-        gather(slot_s, tile([P, BYTES_FIRST * C], U8, "slot_s0"), x_s[:], 0, BYTES_FIRST)
+        def biased(y, i, b, e0, e1):
+            acc = bank(i)
+            multiply(acc, b, e0, e1)
+            add_bias(y[:], acc[:, 0 : (e1 - e0) * C], b, e0, e1)
+            return y
+
+        Q0, Q1, K0, K1, V0, V1 = range(3 * HALVES)
+        gather(slot_s, tile([P, S], U8, "slot_s"), x_s[:], 0, E)
+        acc_q1 = []
         for i, (e0, e1) in enumerate(QUERY_RUNS):
-            if e1 > BYTES_FIRST:
-                gather(slot_s, tile_at([P, (E - BYTES_FIRST) * C], U8, "slot_s1", GATES_FIRST_AT), x_s[:], BYTES_FIRST, E)
             gather_words(e0, e1)
-            for b in range(HALVES):
-                part(tile([P, (e1 - e0) * C], F32, f"y{b}_{e0}"), HALVES * i + b, b, e0, e1)
-        for b in range(HALVES):
-            store(b)
+            part(tile([P, (e1 - e0) * C], F32, f"y_q0_{e0}"), i, Q0, e0, e1)
+            if i == 0:
+                part(tile([P, EARLY * C], F32, "y_q1a"), 3, Q1, e0, e1)
+            else:
+                acc_q1.append(bank(3 + i))
+                multiply(acc_q1[-1], Q1, e0, e1)
+        y = tile_at([P, (MID - EARLY) * C], F32, "y_q1b", Q_LATE_AT)
+        add_bias(y[:], acc_q1[0][:, 0 : (MID - EARLY) * C], Q1, EARLY, MID)
+        scatter_on_vector(y[:], Q1, EARLY, MID)
+        store(Q0)
 
         grouped = [tile([P, QUANT, N, PACK], BF16, f"grouped{i}") for i in range(PAIRS)]
 
@@ -230,53 +235,40 @@ def tile_moe_qkv_kernel(tc, x_words, x_scales, wq_words, wq_scales, wk_words, wk
                 in_=grouped[i][:].rearrange("p e n t -> p (e n t)"),
             )
 
-        K0, K1, V0, V1 = 2, 3, 4, 5
-
         def result(name, experts, place):
             return tile_at([P, experts * C], F32, name, place)
 
-        def value_run(i, e0, e1, place):
-            acc = bank(i)
-            width = (e1 - e0) * C
-            for h in range(HALVES):
-                multiply(acc[:, h * width : (h + 1) * width], V0 + h, e0, e1)
-            for h in range(HALVES):
-                y = result(f"y_v{h}_{e0}", e1 - e0, place + 4 * h * width)
-                finish(y, acc[:, h * width : (h + 1) * width], V0 + h, e0, e1)
-                scatter_on_scalar(y[:], V0 + h, e0, e1)
+        part(tile([P, HALF * C], F32, "y_k0a"), 6, K0, 0, HALF)
+        acc = bank(7)
+        multiply(acc, K1, 0, HALF)
+        windows.append(tile_at([P, T], F32, "window3", WINDOW3_AT))
+        nc.gpsimd.memset(windows[3][:], 0.0)
+        y = tile([P, HALF * C], F32, "y_k1a")
+        finish(y, acc, K1, 0, HALF)
+        scatter_on_scalar(y[:], K1, 0, HALF)
+        y = result("y_q1c", E - MID, K_AT + 64)
+        add_bias(y[:], acc_q1[1][:, 0 : (E - MID) * C], Q1, MID, E)
+        scatter_on_vector(y[:], Q1, MID, E)
+        store(Q1)
 
-        acc = bank(6)
-        multiply(acc, K0, 0, HALF)
-        y = tile([P, HALF * C], F32, "y_k0a")
-        add_bias(y[:], acc[:, 0 : HALF * C], K0, 0, HALF)
-        scatter_on_vector(y[:], K0, 0, HALF)
         lay_out(0)
-        own = E - SHARE
-        acc_k0 = bank(7)
-        multiply(acc_k0, K0, HALF, E)
-        y = tile([P, SHARE * C], F32, "y_k0c")
-        finish(y, acc_k0[:, (own - HALF) * C : HALF * C], K0, own, E)
-        scatter_on_scalar(y[:], K0, own, E)
+        part(result("y_k0b", HALF, RAW_AT), 3, K0, HALF, E)
+        store(K0)
         quantise(0)
+
         lay_out(1)
-        value_run(2, 0, QUANT, RAW_AT + RAW)
+        part(result("y_k1b", HALF, RAW_AT + RAW), 0, K1, HALF, E)
+        store(K1)
         quantise(1)
+
         lay_out(2)
         last = RAW_AT + 2 * RAW
-        value_run(3, QUANT, HALF, last)
+        part(result("y_v0a", HALF, last), 1, V0, 0, HALF)
         quantise(2)
-        y_k1 = result("y_k1", E, last + 4 * 2 * C)
-        for i in range(2):
-            acc = bank(i)
-            multiply(acc, K1, i * HALF, (i + 1) * HALF)
-            add_bias(y_k1[:, i * HALF * C : (i + 1) * HALF * C], acc[:, 0 : HALF * C], K1, i * HALF, (i + 1) * HALF)
-        y_k0 = result("y_k0b", own - HALF, last + 4 * 8 * C)
-        add_bias(y_k0[:], acc_k0[:, 0 : (own - HALF) * C], K0, HALF, own)
-        for h in range(HALVES):
-            part(result(f"y_v{h}_late", HALF, last + 4 * (10 + h * HALF) * C), 4 + h, V0 + h, HALF, E)
-        scatter_on_vector(y_k0[:], K0, HALF, own)
-        store(K0)
+        y_v1 = result("y_v1", E, last + 4 * HALF * C)
+        for i, (e0, e1) in enumerate(((0, 2 * QUANT), (2 * QUANT, E))):
+            biased(y_v1[:, e0 * C : e1 * C], 2 + i, V1, e0, e1)
+        part(result("y_v0b", HALF, last + 4 * 3 * HALF * C), 4, V0, HALF, E)
         store(V0)
+        scatter_on_vector(y_v1[:], V1, 0, E)
         store(V1)
-        scatter_on_vector(y_k1[:], K1, 0, E)
-        store(K1)

@@ -26,6 +26,7 @@ QUANT = 2
 PAIRS = E // QUANT
 SEED = 64
 ROW = 8
+FIRST = 192
 WINDOWS = 4
 HALF = E // 2
 
@@ -37,7 +38,7 @@ REST_AT = BIAS_Q_AT
 BIAS_KV_AT = GATES_FIRST_AT + 4 * (E - MID) * C
 GATES_AT = BIAS_KV_AT + 4 * 2 * HALVES * ROW
 Q_LATE_AT = GATES_AT + 4 * S
-WINDOW2_AT = Q_LATE_AT + (E - MID) * 2 * N
+WINDOW2_AT = Q_LATE_AT + 4 * 4 * C
 WINDOW3_AT = WINDOW2_AT + 4 * T
 K_AT = WINDOW3_AT + 4 * T - 64
 RAW_AT = K_AT + 4 * E * N
@@ -106,8 +107,8 @@ def tile_moe_qkv_kernel(tc, x_words, x_scales, wq_words, wq_scales, wk_words, wk
         load_scale_rows(q_plane.bitcast(I32), weight_scale_rows(wq_scales))
         bias_q = tile_at([P, HALVES, ROW], F32, "bias_q", BIAS_Q_AT)
         nc.sync.dma_start(out=bias_q[:, :, 0:E], in_=bias_rows[:, 0:HALVES])
-        gates_first = tile_at([P, EARLY * C], F32, "gates_first", GATES_FIRST_AT)
-        nc.sync.dma_start(out=gates_first[:], in_=gate[:, 0 : EARLY * C])
+        gates_first = tile_at([P, FIRST], F32, "gates_first", GATES_FIRST_AT)
+        nc.sync.dma_start(out=gates_first[:], in_=gate[:, 0:FIRST])
         gates = tile_at([P, S], F32, "gates", GATES_AT)
         nc.sync.dma_start(out=gates[:], in_=gate)
         q_late = tile_at([P, E - MID, 2 * N], U8, "q_late", Q_LATE_AT)
@@ -124,19 +125,17 @@ def tile_moe_qkv_kernel(tc, x_words, x_scales, wq_words, wq_scales, wk_words, wk
             v_raw.append(tile_at([P, QUANT, PACK, N], F32, f"v_raw{i}", RAW_AT + i * RAW))
             nc.sync.dma_start(out=v_raw[i][:], in_=wv[i * QUANT : (i + 1) * QUANT].rearrange("e (p j) n -> p e j n", j=PACK))
 
-        def entries(e0, e1):
-            return offsets[:, e0 * C // LIST : e1 * C // LIST]
+        def entries(s0, s1):
+            return offsets[:, s0 // LIST : s1 // LIST]
 
-        slot_s, slot_w = [], []
+        def gather(part, table, e0, e1):
+            nc.vector.tensor_copy(part[:], table.indirect(entries(e0 * C, e1 * C)))
+            return [part[:, i * C : (i + 1) * C] for i in range(e1 - e0)]
 
-        def gather(slots, part, table, e0, e1):
-            nc.vector.tensor_copy(part[:], table.indirect(entries(e0, e1)))
-            slots.extend(part[:, i * C : (i + 1) * C] for i in range(e1 - e0))
-
-        def gather_words(e0, e1):
-            shape = [P, (e1 - e0) * C]
-            words = tile(shape, U32, f"slot_w{e0}") if e0 < MID else tile_at(shape, U32, f"slot_w{e0}", GATES_FIRST_AT)
-            gather(slot_w, words, x_w[:].bitcast(U32), e0, e1)
+        slot_s = gather(tile([P, S], U8, "slot_s"), x_s[:], 0, E)
+        slot_w = []
+        for e0, e1 in QUERY_RUNS[:-1]:
+            slot_w.extend(gather(tile([P, (e1 - e0) * C], U32, f"slot_w{e0}"), x_w[:].bitcast(U32), e0, e1))
 
         v_w = tile([P, E, N], U32, "v_w")
         v_s = tile([P, E, N], U8, "v_s")
@@ -150,10 +149,8 @@ def tile_moe_qkv_kernel(tc, x_words, x_scales, wq_words, wq_scales, wk_words, wk
                 return k_w[e // HALF][:, e % HALF, cols].bitcast(FP8X4), k_plane[:, e, cols]
             return v_w[:, e, cols].bitcast(FP8X4), v_s[:, e, cols]
 
-        def bank(i):
-            return psum.tile([P, 4 * C], F32, name="acc", tag=f"bank{i}")
-
-        def multiply(acc, b, e0, e1):
+        def multiply(bank, b, e0, e1):
+            acc = psum.tile([P, 4 * C], F32, name="acc", tag=f"bank{bank}")
             for e in range(e0, e1):
                 w_codes, w_scales = weights(b, e)
                 nc.tensor.matmul_mx(
@@ -165,59 +162,77 @@ def tile_moe_qkv_kernel(tc, x_words, x_scales, wq_words, wq_scales, wk_words, wk
                     start=True,
                     stop=True,
                 )
+            return lambda s0, s1: acc[:, s0 - e0 * C : s1 - e0 * C]
 
-        def finish(y, acc, b, e0, e1):
-            biases = bias_q[:, b] if b < HALVES else bias_kv[:, b - HALVES]
-            table = gates_first if b < HALVES and e1 <= EARLY else gates
-            for e in range(e0, e1):
-                cols = slice((e - e0) * C, (e - e0 + 1) * C)
-                nc.vector.scalar_tensor_tensor(y[:, cols], acc[:, cols], biases[:, e : e + 1], table[:, e * C : (e + 1) * C], add, mult)
+        def biases(b):
+            return bias_q[:, b] if b < HALVES else bias_kv[:, b - HALVES]
 
-        def add_bias(y, acc, b, e0, e1):
-            biases = bias_q[:, b] if b < HALVES else bias_kv[:, b - HALVES]
+        def finish(y, sums, b, s0, s1, table=gates):
+            for e in range(s0 // C, (s1 - 1) // C + 1):
+                lo, hi = max(s0, e * C), min(s1, (e + 1) * C)
+                nc.vector.scalar_tensor_tensor(y[:, lo - s0 : hi - s0], sums(lo, hi), biases(b)[:, e : e + 1], table[:, lo:hi], add, mult)
+
+        def add_bias(y, sums, b, s0, s1):
+            width = min(C, s1 - s0)
+            e0, count = s0 // C, (s1 - s0) // width
             nc.vector.tensor_tensor(
-                y.rearrange("p (e c) -> p e c", c=C),
-                acc.rearrange("p (e c) -> p e c", c=C),
-                biases[:, e0:e1].unsqueeze(2).to_broadcast([P, e1 - e0, C]),
+                y.rearrange("p (e c) -> p e c", c=width),
+                sums(s0, s1).rearrange("p (e c) -> p e c", c=width),
+                biases(b)[:, e0 : e0 + count].unsqueeze(2).to_broadcast([P, count, width]),
                 add,
             )
 
-        def scatter_on_scalar(y, b, e0, e1):
-            nc.scalar.activation(windows[b % WINDOWS][:].indirect(entries(e0, e1)), y, copy)
+        def scatter_on_scalar(y, b, s0, s1):
+            nc.scalar.activation(windows[b % WINDOWS][:].indirect(entries(s0, s1)), y, copy)
 
-        def scatter_on_vector(y, b, e0, e1):
-            nc.vector.tensor_tensor(windows[b % WINDOWS][:].indirect(entries(e0, e1)), y, gates[:, e0 * C : e1 * C], mult)
+        def scatter_on_vector(y, b, s0, s1):
+            nc.vector.tensor_tensor(windows[b % WINDOWS][:].indirect(entries(s0, s1)), y, gates[:, s0:s1], mult)
 
         def store(b):
             nc.sync.dma_start(out=out[b * P : (b + 1) * P, :], in_=windows[b % WINDOWS][:])
 
-        def part(y, i, b, e0, e1):
-            acc = bank(i)
-            multiply(acc, b, e0, e1)
-            finish(y, acc, b, e0, e1)
-            scatter_on_scalar(y[:], b, e0, e1)
+        def result(name, slots, place=None):
+            return tile([P, slots], F32, name) if place is None else tile_at([P, slots], F32, name, place)
 
-        def biased(y, i, b, e0, e1):
-            acc = bank(i)
-            multiply(acc, b, e0, e1)
-            add_bias(y[:], acc[:, 0 : (e1 - e0) * C], b, e0, e1)
-            return y
+        def for_scalar(sums, b, s0, s1, place=None):
+            y = result(f"y{b}_{s0}", s1 - s0, place)
+            finish(y, sums, b, s0, s1)
+            scatter_on_scalar(y[:], b, s0, s1)
 
         Q0, Q1, K0, K1, V0, V1 = range(3 * HALVES)
-        gather(slot_s, tile([P, S], U8, "slot_s"), x_s[:], 0, E)
-        acc_q1 = []
-        for i, (e0, e1) in enumerate(QUERY_RUNS):
-            gather_words(e0, e1)
-            part(tile([P, (e1 - e0) * C], F32, f"y_q0_{e0}"), i, Q0, e0, e1)
-            if i == 0:
-                part(tile([P, EARLY * C], F32, "y_q1a"), 3, Q1, e0, e1)
-            else:
-                acc_q1.append(bank(3 + i))
-                multiply(acc_q1[-1], Q1, e0, e1)
-        y = tile_at([P, (MID - EARLY) * C], F32, "y_q1b", Q_LATE_AT)
-        add_bias(y[:], acc_q1[0][:, 0 : (MID - EARLY) * C], Q1, EARLY, MID)
-        scatter_on_vector(y[:], Q1, EARLY, MID)
+        early, mid, half = EARLY * C, MID * C, HALF * C
+
+        y = result("y_q0a", early)
+        finish(y, multiply(0, Q0, 0, EARLY), Q0, 0, early, gates_first)
+        scatter_on_scalar(y[:], Q0, 0, early)
+        y = result("y_q1a", FIRST)
+        finish(y, multiply(1, Q1, 0, EARLY), Q1, 0, early, gates_first)
+        q1_mid = multiply(2, Q1, EARLY, MID)
+        finish(y[:, early:FIRST], q1_mid, Q1, early, FIRST, gates_first)
+        scatter_on_scalar(y[:], Q1, 0, FIRST)
+        q0_mid = multiply(3, Q0, EARLY, MID)
+        slot_w.extend(gather(tile_at([P, S - mid], U32, "slot_w3", GATES_FIRST_AT), x_w[:].bitcast(U32), MID, E))
+        for_scalar(q0_mid, Q0, early, mid)
+        q0_late = multiply(4, Q0, MID, E)
+        q1_late = multiply(5, Q1, MID, E)
+        y = result("y_q1b", mid - FIRST, Q_LATE_AT)
+        add_bias(y[:, 0 : 2 * C - FIRST], q1_mid, Q1, FIRST, 2 * C)
+        add_bias(y[:, 2 * C - FIRST : mid - FIRST], q1_mid, Q1, 2 * C, mid)
+        for_scalar(q0_late, Q0, mid, S)
         store(Q0)
+        scatter_on_vector(y[:], Q1, FIRST, mid)
+
+        for_scalar(multiply(6, K0, 0, HALF), K0, 0, half)
+        k1_first = multiply(7, K1, 0, HALF)
+        windows.append(tile_at([P, T], F32, "window3", WINDOW3_AT))
+        nc.gpsimd.memset(windows[3][:], 0.0)
+        y_q1 = result("y_q1c", S - mid, K_AT + 64)
+        add_bias(y_q1[:], q1_late, Q1, mid, S)
+        for_scalar(k1_first, K1, 0, half)
+        scatter_on_vector(y_q1[:], Q1, mid, S)
+        store(Q1)
+        k0_late = multiply(0, K0, HALF, E)
+        k1_late = multiply(1, K1, HALF, E)
 
         grouped = [tile([P, QUANT, N, PACK], BF16, f"grouped{i}") for i in range(PAIRS)]
 
@@ -235,40 +250,27 @@ def tile_moe_qkv_kernel(tc, x_words, x_scales, wq_words, wq_scales, wk_words, wk
                 in_=grouped[i][:].rearrange("p e n t -> p (e n t)"),
             )
 
-        def result(name, experts, place):
-            return tile_at([P, experts * C], F32, name, place)
-
-        part(tile([P, HALF * C], F32, "y_k0a"), 6, K0, 0, HALF)
-        acc = bank(7)
-        multiply(acc, K1, 0, HALF)
-        windows.append(tile_at([P, T], F32, "window3", WINDOW3_AT))
-        nc.gpsimd.memset(windows[3][:], 0.0)
-        y = tile([P, HALF * C], F32, "y_k1a")
-        finish(y, acc, K1, 0, HALF)
-        scatter_on_scalar(y[:], K1, 0, HALF)
-        y = result("y_q1c", E - MID, K_AT + 64)
-        add_bias(y[:], acc_q1[1][:, 0 : (E - MID) * C], Q1, MID, E)
-        scatter_on_vector(y[:], Q1, MID, E)
-        store(Q1)
-
+        pair = QUANT * C
         lay_out(0)
-        part(result("y_k0b", HALF, RAW_AT), 3, K0, HALF, E)
+        for_scalar(k0_late, K0, half, S, RAW_AT)
         store(K0)
         quantise(0)
 
         lay_out(1)
-        part(result("y_k1b", HALF, RAW_AT + RAW), 0, K1, HALF, E)
-        store(K1)
+        for_scalar(multiply(2, V0, 0, QUANT), V0, 0, pair, RAW_AT + RAW)
+        for_scalar(k1_late, K1, half, 5 * C, RAW_AT + RAW + 4 * pair)
         quantise(1)
 
         lay_out(2)
         last = RAW_AT + 2 * RAW
-        part(result("y_v0a", HALF, last), 1, V0, 0, HALF)
+        for_scalar(multiply(3, V0, QUANT, 2 * QUANT), V0, pair, 2 * pair, last)
+        for_scalar(k1_late, K1, 5 * C, S, last + 4 * pair)
+        store(K1)
         quantise(2)
-        y_v1 = result("y_v1", E, last + 4 * HALF * C)
-        for i, (e0, e1) in enumerate(((0, 2 * QUANT), (2 * QUANT, E))):
-            biased(y_v1[:, e0 * C : e1 * C], 2 + i, V1, e0, e1)
-        part(result("y_v0b", HALF, last + 4 * 3 * HALF * C), 4, V0, HALF, E)
+        y_v1 = result("y_v1", S, last + 4 * 2 * pair)
+        add_bias(y_v1[:, 0 : 2 * pair], multiply(4, V1, 0, 2 * QUANT), V1, 0, 2 * pair)
+        add_bias(y_v1[:, 2 * pair : S], multiply(5, V1, 2 * QUANT, E), V1, 2 * pair, S)
+        for_scalar(multiply(6, V0, 2 * QUANT, E), V0, 2 * pair, S, last + 4 * (2 * pair + S))
         store(V0)
-        scatter_on_vector(y_v1[:], V1, 0, E)
+        scatter_on_vector(y_v1[:], V1, 0, S)
         store(V1)

@@ -38,8 +38,9 @@ REST_AT = BIAS_Q_AT
 BIAS_KV_AT = GATES_FIRST_AT + 4 * (E - MID) * C
 GATES_AT = BIAS_KV_AT + 4 * 2 * HALVES * ROW
 Q_LATE_AT = GATES_AT + 4 * S
-WINDOW2_AT = Q_LATE_AT + 4 * 4 * C
-WINDOW3_AT = WINDOW2_AT + 4 * T
+K_PLANE_AT = Q_LATE_AT + (E - MID) * 2 * N
+WINDOW1_AT = K_PLANE_AT + E * N
+WINDOW3_AT = WINDOW1_AT + 4 * T
 K_AT = WINDOW3_AT + 4 * T - 64
 RAW_AT = K_AT + 4 * E * N
 RAW = 4 * QUANT * PACK * N
@@ -64,29 +65,30 @@ def tile_moe_qkv_kernel(tc, x_words, x_scales, wq_words, wq_scales, wk_words, wk
 
         offsets = keep.tile([P, S // LIST], U16, name="offsets")
         x_s = tile([P, T], U8, "x_s")
-        planes = tile([P, 2, E, N], U8, "planes")
-        q_plane, k_plane = planes[:, 0], planes[:, 1]
+        q_plane = tile([P, E, N], U8, "q_plane")
         seeds = [
             tile_at([P, SEED], F32, "seed0", Q_FIRST_AT - 128),
             tile_at([P, (END_AT - REST_AT) // 4], F32, "seed1", REST_AT),
         ]
         zeros = [tile([P, SEED], F32, f"zero{i}") for i in range(2)]
-        windows = [tile([P, T], F32, f"window{b}") for b in range(HALVES)]
+        windows = [tile([P, T], F32, "window0")]
 
         nc.vector.memset(x_s[:].bitcast(I32), 0)
         for seed in seeds:
             nc.vector.memset(seed[:, 0:SEED], 0.0)
         nc.vector.tensor_copy(zeros[0][:], seeds[0][:, 0:SEED])
-        nc.vector.memset(planes[:].bitcast(I32), 0)
+        nc.vector.memset(q_plane[:].bitcast(I32), 0)
         nc.vector.tensor_copy(zeros[1][:], seeds[1][:, 0:SEED])
 
-        for window, zero in zip(windows, zeros):
+        for i, zero in enumerate(zeros):
             nc.scalar.copy(
-                out=window[:].rearrange("p (r c) -> p r c", c=SEED),
-                in_=zero[:].unsqueeze(1).to_broadcast([P, T // SEED, SEED]),
+                out=windows[0][:, i * T // 2 : (i + 1) * T // 2].rearrange("p (r c) -> p r c", c=SEED),
+                in_=zero[:].unsqueeze(1).to_broadcast([P, T // 2 // SEED, SEED]),
             )
-        windows.append(tile_at([P, T], F32, "window2", WINDOW2_AT))
-        nc.gpsimd.memset(windows[2][:], 0.0)
+        k_plane = tile_at([P, E, N], U8, "k_plane", K_PLANE_AT)
+        nc.gpsimd.memset(k_plane[:].bitcast(I32), 0)
+        windows.append(tile_at([P, T], F32, "window1", WINDOW1_AT))
+        nc.gpsimd.memset(windows[1][:], 0.0)
 
         def load_scale_rows(plane, rows):
             for r in range(PACK):
@@ -104,7 +106,7 @@ def tile_moe_qkv_kernel(tc, x_words, x_scales, wq_words, wq_scales, wk_words, wk
         nc.sync.dma_start(out=x_w[:], in_=x_words[0].rearrange("p t d -> p (t d)").bitcast(I32))
         q_first = tile_at([P, MID, 2 * N], U8, "q_first", Q_FIRST_AT)
         nc.sync.dma_start(out=q_first[:].bitcast(I32), in_=q_rows[:, 0:MID])
-        load_scale_rows(q_plane.bitcast(I32), weight_scale_rows(wq_scales))
+        load_scale_rows(q_plane[:].bitcast(I32), weight_scale_rows(wq_scales))
         bias_q = tile_at([P, HALVES, ROW], F32, "bias_q", BIAS_Q_AT)
         nc.sync.dma_start(out=bias_q[:, :, 0:E], in_=bias_rows[:, 0:HALVES])
         gates_first = tile_at([P, FIRST], F32, "gates_first", GATES_FIRST_AT)
@@ -113,7 +115,7 @@ def tile_moe_qkv_kernel(tc, x_words, x_scales, wq_words, wq_scales, wk_words, wk
         nc.sync.dma_start(out=gates[:], in_=gate)
         q_late = tile_at([P, E - MID, 2 * N], U8, "q_late", Q_LATE_AT)
         nc.sync.dma_start(out=q_late[:].bitcast(I32), in_=q_rows[:, MID:E])
-        load_scale_rows(k_plane.bitcast(I32), weight_scale_rows(wk_scales))
+        load_scale_rows(k_plane[:].bitcast(I32), weight_scale_rows(wk_scales))
         k_rows = wk_words.rearrange("e s p n d -> p (e s) (n d)").bitcast(I32)
         k_w = [tile_at([P, HALF, N], I32, f"k_w{i}", K_AT + i * 4 * HALF * N) for i in range(2)]
         nc.sync.dma_start(out=k_w[0][:], in_=k_rows[:, 0:HALF])
@@ -212,6 +214,8 @@ def tile_moe_qkv_kernel(tc, x_words, x_scales, wq_words, wq_scales, wk_words, wk
         scatter_on_scalar(y[:], Q1, 0, FIRST)
         q0_mid = multiply(3, Q0, EARLY, MID)
         slot_w.extend(gather(tile_at([P, S - mid], U32, "slot_w3", GATES_FIRST_AT), x_w[:].bitcast(U32), MID, E))
+        windows.append(tile_at([P, T], F32, "window2", X_AT))
+        nc.gpsimd.memset(windows[2][:], 0.0)
         for_scalar(q0_mid, Q0, early, mid)
         q0_late = multiply(4, Q0, MID, E)
         q1_late = multiply(5, Q1, MID, E)

@@ -30,21 +30,22 @@ FIRST = 192
 WINDOWS = 4
 HALF = E // 2
 
-X_AT = 0
-Q_FIRST_AT = X_AT + 4 * T
-BIAS_Q_AT = Q_FIRST_AT + MID * 2 * N
+REST_AT = 0
+BIAS_Q_AT = REST_AT
 GATES_FIRST_AT = BIAS_Q_AT + 4 * HALVES * ROW
-REST_AT = BIAS_Q_AT
 BIAS_KV_AT = GATES_FIRST_AT + 4 * (E - MID) * C
 GATES_AT = BIAS_KV_AT + 4 * 2 * HALVES * ROW
 Q_LATE_AT = GATES_AT + 4 * S
 K_PLANE_AT = Q_LATE_AT + (E - MID) * 2 * N
 WINDOW1_AT = K_PLANE_AT + E * N
-WINDOW3_AT = WINDOW1_AT + 4 * T
-K_AT = WINDOW3_AT + 4 * T - 64
-RAW_AT = K_AT + 4 * E * N
+RAW_AT = WINDOW1_AT + 4 * T
 RAW = 4 * QUANT * PACK * N
-END_AT = RAW_AT + PAIRS * RAW
+WINDOW3_AT = 112 * 1024
+K_AT = WINDOW3_AT + 4 * T - 64
+END_AT = K_AT + 4 * E * N
+X_AT = END_AT
+Q_FIRST_AT = X_AT + 4 * T
+WINDOW0_AT = Q_FIRST_AT + MID * 2 * N
 
 
 def tile_moe_qkv_kernel(tc, x_words, x_scales, wq_words, wq_scales, wk_words, wk_scales, wv, bias, gate, offs, out):
@@ -71,7 +72,7 @@ def tile_moe_qkv_kernel(tc, x_words, x_scales, wq_words, wq_scales, wk_words, wk
             tile_at([P, (END_AT - REST_AT) // 4], F32, "seed1", REST_AT),
         ]
         zeros = [tile([P, SEED], F32, f"zero{i}") for i in range(2)]
-        windows = [tile([P, T], F32, "window0")]
+        windows = [tile_at([P, T], F32, "window0", WINDOW0_AT)]
 
         nc.vector.memset(x_s[:].bitcast(I32), 0)
         for seed in seeds:

@@ -21,19 +21,17 @@ LIST = 16
 HALVES = N // P
 EARLY = 1
 MID = 3
-QUERY_RUNS = ((0, EARLY), (EARLY, MID), (MID, E))
+QUERY_RUNS = ((0, MID), (MID, E))
 QUANT = 2
 PAIRS = E // QUANT
 SEED = 64
 ROW = 8
-FIRST = 192
 WINDOWS = 4
 HALF = E // 2
 
 REST_AT = 0
 BIAS_Q_AT = REST_AT
-GATES_FIRST_AT = BIAS_Q_AT + 4 * HALVES * ROW
-BIAS_KV_AT = GATES_FIRST_AT + 4 * (E - MID) * C
+BIAS_KV_AT = BIAS_Q_AT + 4 * HALVES * ROW
 GATES_AT = BIAS_KV_AT + 4 * 2 * HALVES * ROW
 Q_LATE_AT = GATES_AT + 4 * S
 K_PLANE_AT = Q_LATE_AT + (E - MID) * 2 * N
@@ -51,7 +49,7 @@ WINDOW0_AT = Q_FIRST_AT + MID * 2 * N
 def tile_moe_qkv_kernel(tc, x_words, x_scales, wq_words, wq_scales, wk_words, wk_scales, wv, bias, gate, offs, out):
     nc = tc.nc
     add, mult = mybir.AluOpType.add, mybir.AluOpType.mult
-    copy = mybir.ActivationFunctionType.Copy
+    copy, identity = mybir.ActivationFunctionType.Copy, mybir.ActivationFunctionType.Identity
 
     with ExitStack() as ctx:
         keep = ctx.enter_context(tc.tile_pool(name="keep", bufs=1))
@@ -110,12 +108,11 @@ def tile_moe_qkv_kernel(tc, x_words, x_scales, wq_words, wq_scales, wk_words, wk
         load_scale_rows(q_plane[:].bitcast(I32), weight_scale_rows(wq_scales))
         bias_q = tile_at([P, HALVES, ROW], F32, "bias_q", BIAS_Q_AT)
         nc.sync.dma_start(out=bias_q[:, :, 0:E], in_=bias_rows[:, 0:HALVES])
-        gates_first = tile_at([P, FIRST], F32, "gates_first", GATES_FIRST_AT)
-        nc.sync.dma_start(out=gates_first[:], in_=gate[:, 0:FIRST])
         gates = tile_at([P, S], F32, "gates", GATES_AT)
-        nc.sync.dma_start(out=gates[:], in_=gate)
+        nc.sync.dma_start(out=gates[:, 0 : MID * C], in_=gate[:, 0 : MID * C])
         q_late = tile_at([P, E - MID, 2 * N], U8, "q_late", Q_LATE_AT)
         nc.sync.dma_start(out=q_late[:].bitcast(I32), in_=q_rows[:, MID:E])
+        nc.sync.dma_start(out=gates[:, MID * C : S], in_=gate[:, MID * C : S])
         load_scale_rows(k_plane[:].bitcast(I32), weight_scale_rows(wk_scales))
         k_rows = wk_words.rearrange("e s p n d -> p (e s) (n d)").bitcast(I32)
         k_w = [tile_at([P, HALF, N], I32, f"k_w{i}", K_AT + i * 4 * HALF * N) for i in range(2)]
@@ -137,7 +134,7 @@ def tile_moe_qkv_kernel(tc, x_words, x_scales, wq_words, wq_scales, wk_words, wk
 
         slot_s = gather(tile([P, S], U8, "slot_s"), x_s[:], 0, E)
         slot_w = []
-        for e0, e1 in QUERY_RUNS[:-1]:
+        for e0, e1 in QUERY_RUNS:
             slot_w.extend(gather(tile([P, (e1 - e0) * C], U32, f"slot_w{e0}"), x_w[:].bitcast(U32), e0, e1))
 
         v_w = tile([P, E, N], U32, "v_w")
@@ -170,10 +167,10 @@ def tile_moe_qkv_kernel(tc, x_words, x_scales, wq_words, wq_scales, wk_words, wk
         def biases(b):
             return bias_q[:, b] if b < HALVES else bias_kv[:, b - HALVES]
 
-        def finish(y, sums, b, s0, s1, table=gates):
+        def finish(y, sums, b, s0, s1):
             for e in range(s0 // C, (s1 - 1) // C + 1):
                 lo, hi = max(s0, e * C), min(s1, (e + 1) * C)
-                nc.vector.scalar_tensor_tensor(y[:, lo - s0 : hi - s0], sums(lo, hi), biases(b)[:, e : e + 1], table[:, lo:hi], add, mult)
+                nc.vector.scalar_tensor_tensor(y[:, lo - s0 : hi - s0], sums(lo, hi), biases(b)[:, e : e + 1], gates[:, lo:hi], add, mult)
 
         def add_bias(y, sums, b, s0, s1):
             width = min(C, s1 - s0)
@@ -184,6 +181,10 @@ def tile_moe_qkv_kernel(tc, x_words, x_scales, wq_words, wq_scales, wk_words, wk
                 biases(b)[:, e0 : e0 + count].unsqueeze(2).to_broadcast([P, count, width]),
                 add,
             )
+
+        def add_bias_on_scalar(y, sums, b, e0, e1):
+            for e in range(e0, e1):
+                nc.scalar.activation(y[:, (e - e0) * C : (e - e0 + 1) * C], sums(e * C, (e + 1) * C), identity, bias=biases(b)[:, e : e + 1])
 
         def scatter_on_scalar(y, b, s0, s1):
             nc.scalar.activation(windows[b % WINDOWS][:].indirect(entries(s0, s1)), y, copy)
@@ -205,36 +206,38 @@ def tile_moe_qkv_kernel(tc, x_words, x_scales, wq_words, wq_scales, wk_words, wk
         Q0, Q1, K0, K1, V0, V1 = range(3 * HALVES)
         early, mid, half = EARLY * C, MID * C, HALF * C
 
-        y = result("y_q0a", early)
-        finish(y, multiply(0, Q0, 0, EARLY), Q0, 0, early, gates_first)
-        scatter_on_scalar(y[:], Q0, 0, early)
-        y = result("y_q1a", FIRST)
-        finish(y, multiply(1, Q1, 0, EARLY), Q1, 0, early, gates_first)
-        q1_mid = multiply(2, Q1, EARLY, MID)
-        finish(y[:, early:FIRST], q1_mid, Q1, early, FIRST, gates_first)
-        scatter_on_scalar(y[:], Q1, 0, FIRST)
-        q0_mid = multiply(3, Q0, EARLY, MID)
-        slot_w.extend(gather(tile_at([P, S - mid], U32, "slot_w3", GATES_FIRST_AT), x_w[:].bitcast(U32), MID, E))
         windows.append(tile_at([P, T], F32, "window2", X_AT))
         nc.gpsimd.memset(windows[2][:], 0.0)
-        for_scalar(q0_mid, Q0, early, mid)
-        q0_late = multiply(4, Q0, MID, E)
-        q1_late = multiply(5, Q1, MID, E)
-        y = result("y_q1b", mid - FIRST, Q_LATE_AT)
-        add_bias(y[:, 0 : 2 * C - FIRST], q1_mid, Q1, FIRST, 2 * C)
-        add_bias(y[:, 2 * C - FIRST : mid - FIRST], q1_mid, Q1, 2 * C, mid)
-        for_scalar(q0_late, Q0, mid, S)
-        store(Q0)
-        scatter_on_vector(y[:], Q1, FIRST, mid)
 
-        for_scalar(multiply(6, K0, 0, HALF), K0, 0, half)
+        pair = QUANT * C
+        y_q1 = result("y_q1a", pair)
+        add_bias_on_scalar(y_q1, multiply(0, Q1, 0, 2), Q1, 0, 2)
+        for_scalar(multiply(1, Q0, 0, EARLY), Q0, 0, early)
+        q0_mid = multiply(2, Q0, EARLY, MID)
+        y = result("y_q1b", pair)
+        add_bias_on_scalar(y, multiply(1, Q1, 2, 3), Q1, 2, 3)
+        for_scalar(q0_mid, Q0, early, mid)
+        add_bias_on_scalar(y[:, C:pair], multiply(3, Q1, 3, 4), Q1, 3, 4)
+        scatter_on_vector(y_q1[:], Q1, 0, pair)
+        for_scalar(multiply(4, Q0, MID, E), Q0, mid, S)
+        store(Q0)
+        scatter_on_vector(y[:], Q1, pair, 2 * pair)
+        q1_late = multiply(5, Q1, 4, E)
+
+        k0_first = multiply(6, K0, 0, HALF)
         k1_first = multiply(7, K1, 0, HALF)
         windows.append(tile_at([P, T], F32, "window3", WINDOW3_AT))
         nc.gpsimd.memset(windows[3][:], 0.0)
-        y_q1 = result("y_q1c", S - mid, K_AT + 64)
-        add_bias(y_q1[:], q1_late, Q1, mid, S)
-        for_scalar(k1_first, K1, 0, half)
-        scatter_on_vector(y_q1[:], Q1, mid, S)
+        for_scalar(k0_first, K0, 0, half)
+        y_k1 = result("y_k1z", C)
+        add_bias(y_k1[:], k1_first, K1, 0, C)
+        y_q1 = result("y_q1c", pair, K_AT + 64)
+        add_bias(y_q1[:], q1_late, Q1, 2 * pair, S)
+        y = result("y_k1a", half - C)
+        finish(y, k1_first, K1, C, half)
+        scatter_on_vector(y_k1[:], K1, 0, C)
+        scatter_on_scalar(y[:], K1, C, half)
+        scatter_on_vector(y_q1[:], Q1, 2 * pair, S)
         store(Q1)
         k0_late = multiply(0, K0, HALF, E)
         k1_late = multiply(1, K1, HALF, E)
@@ -255,7 +258,6 @@ def tile_moe_qkv_kernel(tc, x_words, x_scales, wq_words, wq_scales, wk_words, wk
                 in_=grouped[i][:].rearrange("p e n t -> p (e n t)"),
             )
 
-        pair = QUANT * C
         lay_out(0)
         for_scalar(k0_late, K0, half, S, RAW_AT)
         store(K0)

@@ -271,9 +271,11 @@ def tile_moe_qkv_kernel(tc, x_words, x_scales, wq_words, wq_scales, wk_words, wk
         lay_out(2)
         last = RAW_AT + 2 * RAW
         for_scalar(multiply(3, V0, QUANT, 2 * QUANT), V0, pair, 2 * pair, last)
-        for_scalar(k1_late, K1, 5 * C, S, last + 4 * pair)
-        store(K1)
         quantise(2)
+        y = keep.tile([P, C], F32, name="y_k1c", tag="grouped2", align_bytes=64)
+        finish(y, k1_late, K1, 5 * C, S)
+        scatter_on_scalar(y[:], K1, 5 * C, S)
+        store(K1)
         y_v1 = result("y_v1", S, last + 4 * 2 * pair)
         add_bias(y_v1[:, 0 : 2 * pair], multiply(4, V1, 0, 2 * QUANT), V1, 0, 2 * pair)
         add_bias(y_v1[:, 2 * pair : S], multiply(5, V1, 2 * QUANT, E), V1, 2 * pair, S)

@@ -22,8 +22,9 @@ HALVES = N // P
 EARLY = 1
 MID = 3
 QUERY_RUNS = ((0, MID), (MID, E))
-QUANT = 2
-PAIRS = E // QUANT
+PAIR = 2
+ON_GPSIMD = 3
+KEY_SHARE = 256
 SEED = 64
 ROW = 8
 WINDOWS = 4
@@ -37,7 +38,9 @@ Q_LATE_AT = GATES_AT + 4 * S
 K_PLANE_AT = Q_LATE_AT + (E - MID) * 2 * N
 WINDOW1_AT = K_PLANE_AT + E * N
 RAW_AT = WINDOW1_AT + 4 * T
-RAW = 4 * QUANT * PACK * N
+RAW = 4 * PACK * N
+GROUPED = 2 * PACK * N
+EARLY_GROUPED_AT = RAW_AT + E * RAW
 WINDOW3_AT = 112 * 1024
 K_AT = WINDOW3_AT + 4 * T - 64
 END_AT = K_AT + 4 * E * N
@@ -120,10 +123,11 @@ def tile_moe_qkv_kernel(tc, x_words, x_scales, wq_words, wq_scales, wk_words, wk
         bias_kv = tile_at([P, 2 * HALVES, ROW], F32, "bias_kv", BIAS_KV_AT)
         nc.sync.dma_start(out=bias_kv[:, :, 0:E], in_=bias_rows[:, HALVES : 3 * HALVES])
         nc.sync.dma_start(out=k_w[1][:], in_=k_rows[:, HALF:E])
+        v_rows = wv.rearrange("e (p j) n -> p e j n", j=PACK)
         v_raw = []
-        for i in range(PAIRS):
-            v_raw.append(tile_at([P, QUANT, PACK, N], F32, f"v_raw{i}", RAW_AT + i * RAW))
-            nc.sync.dma_start(out=v_raw[i][:], in_=wv[i * QUANT : (i + 1) * QUANT].rearrange("e (p j) n -> p e j n", j=PACK))
+        for e0, e1 in ((0, 1), (1, 2), (2, 3), (3, 5), (5, 6)):
+            v_raw.append(tile_at([P, e1 - e0, PACK, N], F32, f"v_raw{e0}", RAW_AT + e0 * RAW))
+            nc.sync.dma_start(out=v_raw[-1][:], in_=v_rows[:, e0:e1])
 
         def entries(s0, s1):
             return offsets[:, s0 // LIST : s1 // LIST]
@@ -192,6 +196,9 @@ def tile_moe_qkv_kernel(tc, x_words, x_scales, wq_words, wq_scales, wk_words, wk
         def scatter_on_vector(y, b, s0, s1):
             nc.vector.tensor_tensor(windows[b % WINDOWS][:].indirect(entries(s0, s1)), y, gates[:, s0:s1], mult)
 
+        def copy_scatter_on_vector(y, b, s0, s1):
+            nc.vector.tensor_copy(windows[b % WINDOWS][:].indirect(entries(s0, s1)), y)
+
         def store(b):
             nc.sync.dma_start(out=out[b * P : (b + 1) * P, :], in_=windows[b % WINDOWS][:])
 
@@ -209,12 +216,12 @@ def tile_moe_qkv_kernel(tc, x_words, x_scales, wq_words, wq_scales, wk_words, wk
         windows.append(tile_at([P, T], F32, "window2", X_AT))
         nc.gpsimd.memset(windows[2][:], 0.0)
 
-        pair = QUANT * C
+        pair = PAIR * C
         y_q1 = result("y_q1a", pair)
         add_bias_on_scalar(y_q1, multiply(0, Q1, 0, 2), Q1, 0, 2)
         for_scalar(multiply(1, Q0, 0, EARLY), Q0, 0, early)
         q0_mid = multiply(2, Q0, EARLY, MID)
-        y = result("y_q1b", pair)
+        y = result("y_q1b", pair, EARLY_GROUPED_AT)
         add_bias_on_scalar(y, multiply(1, Q1, 2, 3), Q1, 2, 3)
         for_scalar(q0_mid, Q0, early, mid)
         add_bias_on_scalar(y[:, C:pair], multiply(3, Q1, 3, 4), Q1, 3, 4)
@@ -224,62 +231,66 @@ def tile_moe_qkv_kernel(tc, x_words, x_scales, wq_words, wq_scales, wk_words, wk
         scatter_on_vector(y[:], Q1, pair, 2 * pair)
         q1_late = multiply(5, Q1, 4, E)
 
+        early_grouped = tile_at([P, ON_GPSIMD, N, PACK], BF16, "early_grouped", EARLY_GROUPED_AT)
+
         k0_first = multiply(6, K0, 0, HALF)
         k1_first = multiply(7, K1, 0, HALF)
         windows.append(tile_at([P, T], F32, "window3", WINDOW3_AT))
         nc.gpsimd.memset(windows[3][:], 0.0)
+        for e in range(ON_GPSIMD):
+            nc.gpsimd.tensor_scalar(early_grouped[:, e], v_raw[e][:, 0].rearrange("p t n -> p n t"), 1.0, 0.0, mult, add)
+
+        y_k1 = result("y_k1z", KEY_SHARE)
+        finish(y_k1, k1_first, K1, 0, KEY_SHARE)
         for_scalar(k0_first, K0, 0, half)
-        y_k1 = result("y_k1z", C)
-        add_bias(y_k1[:], k1_first, K1, 0, C)
-        y_q1 = result("y_q1c", pair, K_AT + 64)
-        add_bias(y_q1[:], q1_late, Q1, 2 * pair, S)
-        y = result("y_k1a", half - C)
-        finish(y, k1_first, K1, C, half)
-        scatter_on_vector(y_k1[:], K1, 0, C)
-        scatter_on_scalar(y[:], K1, C, half)
-        scatter_on_vector(y_q1[:], Q1, 2 * pair, S)
-        store(Q1)
+        y = result("y_k1a", half - KEY_SHARE)
+        finish(y, k1_first, K1, KEY_SHARE, half)
+        copy_scatter_on_vector(y_k1[:], K1, 0, KEY_SHARE)
+        scatter_on_scalar(y[:], K1, KEY_SHARE, half)
         k0_late = multiply(0, K0, HALF, E)
         k1_late = multiply(1, K1, HALF, E)
-
-        grouped = [tile([P, QUANT, N, PACK], BF16, f"grouped{i}") for i in range(PAIRS)]
-
-        def lay_out(i):
-            nc.vector.tensor_copy(
-                out=grouped[i][:].rearrange("p e (c i) t -> p e c t i", i=4),
-                in_=v_raw[i][:].rearrange("p e t (c i) -> p e c t i", i=4),
-            )
-
-        def quantise(i):
-            pair = slice(i * QUANT, (i + 1) * QUANT)
-            nc.vector.quantize_mx(
-                out=v_w[:, pair].rearrange("p e n -> p (e n)").bitcast(FP8X4),
-                scales=v_s[:, pair].rearrange("p e n -> p (e n)"),
-                in_=grouped[i][:].rearrange("p e n t -> p (e n t)"),
-            )
-
-        lay_out(0)
-        for_scalar(k0_late, K0, half, S, RAW_AT)
+        y_q1 = result("y_q1c", pair, K_AT + 4 * HALF * N)
+        finish(y_q1, q1_late, Q1, 2 * pair, S)
+        y = result("y_k0b", half)
+        finish(y, k0_late, K0, half, S)
+        copy_scatter_on_vector(y_q1[:], Q1, 2 * pair, S)
+        store(Q1)
+        scatter_on_scalar(y[:], K0, half, S)
         store(K0)
-        quantise(0)
+        for_scalar(k1_late, K1, half, 5 * C)
 
-        lay_out(1)
-        for_scalar(multiply(2, V0, 0, QUANT), V0, 0, pair, RAW_AT + RAW)
-        for_scalar(k1_late, K1, half, 5 * C, RAW_AT + RAW + 4 * pair)
-        quantise(1)
+        def lay_out(grouped, raw):
+            nc.vector.tensor_copy(
+                out=grouped[:].rearrange("p e (c i) t -> p e c t i", i=4),
+                in_=raw[:].rearrange("p e t (c i) -> p e c t i", i=4),
+            )
 
-        lay_out(2)
-        last = RAW_AT + 2 * RAW
-        for_scalar(multiply(3, V0, QUANT, 2 * QUANT), V0, pair, 2 * pair, last)
-        quantise(2)
-        y = keep.tile([P, C], F32, name="y_k1c", tag="grouped2", align_bytes=64)
-        finish(y, k1_late, K1, 5 * C, S)
-        scatter_on_scalar(y[:], K1, 5 * C, S)
+        def quantise(grouped, e0, e1):
+            nc.vector.quantize_mx(
+                out=v_w[:, e0:e1].rearrange("p e n -> p (e n)").bitcast(FP8X4),
+                scales=v_s[:, e0:e1].rearrange("p e n -> p (e n)"),
+                in_=grouped.rearrange("p e n t -> p (e n t)"),
+            )
+
+        quantise(early_grouped[:, 0:2], 0, 2)
+        quantise(early_grouped[:, 2:3], 2, 3)
+        late_at = RAW_AT + 2 * RAW - GROUPED
+        grouped34 = tile_at([P, 2, N, PACK], BF16, "grouped34", late_at)
+        grouped5 = tile_at([P, 1, N, PACK], BF16, "grouped5", late_at + 2 * GROUPED)
+        lay_out(grouped34, v_raw[3])
+        for_scalar(multiply(2, V0, 0, HALF), V0, 0, half)
+        quantise(grouped34[:], 3, 5)
+        lay_out(grouped5, v_raw[4])
+        y_v1 = result("y_v1", S)
+        add_bias(y_v1[:, 0 : 2 * pair], multiply(4, V1, 0, 4), V1, 0, 2 * pair)
+        quantise(grouped5[:], 5, 6)
+        y_v0 = result("y_v0b", half)
+        finish(y_v0[:, 0:pair], multiply(3, V0, HALF, 5), V0, half, 5 * C)
+        for_scalar(k1_late, K1, 5 * C, S, late_at)
         store(K1)
-        y_v1 = result("y_v1", S, last + 4 * 2 * pair)
-        add_bias(y_v1[:, 0 : 2 * pair], multiply(4, V1, 0, 2 * QUANT), V1, 0, 2 * pair)
-        add_bias(y_v1[:, 2 * pair : S], multiply(5, V1, 2 * QUANT, E), V1, 2 * pair, S)
-        for_scalar(multiply(6, V0, 2 * QUANT, E), V0, 2 * pair, S, last + 4 * (2 * pair + S))
+        add_bias(y_v1[:, 2 * pair : S], multiply(5, V1, 4, E), V1, 2 * pair, S)
+        finish(y_v0[:, pair:half], multiply(6, V0, 5, E), V0, 5 * C, S)
+        scatter_on_scalar(y_v0[:], V0, half, S)
         store(V0)
         scatter_on_vector(y_v1[:], V1, 0, S)
         store(V1)

@@ -238,7 +238,14 @@ def tile_moe_qkv_kernel(tc, x_words, x_scales, wq_words, wq_scales, wk_words, wk
         windows.append(tile_at([P, T], F32, "window3", WINDOW3_AT))
         nc.gpsimd.memset(windows[3][:], 0.0)
         for e in range(ON_GPSIMD):
-            nc.gpsimd.tensor_scalar(early_grouped[:, e], v_raw[e][:, 0].rearrange("p t n -> p n t"), 1.0, 0.0, mult, add)
+            nc.gpsimd.tensor_scalar(
+                early_grouped[:, e].rearrange("p (c i) t -> p c t i", i=4),
+                v_raw[e][:, 0].rearrange("p t (c i) -> p c t i", i=4),
+                1.0,
+                0.0,
+                mult,
+                add,
+            )
 
         y_k1 = result("y_k1z", KEY_SHARE)
         finish(y_k1, k1_first, K1, 0, KEY_SHARE)

@@ -24,10 +24,11 @@ MID = 3
 QUERY_RUNS = ((0, MID), (MID, E))
 PAIR = 2
 ON_GPSIMD = 3
-KEY_SHARE = 256
+QUERY_CUT = 448
+KEY_SHARE = 192
 SEED = 64
 ROW = 8
-WINDOWS = 4
+WINDOW_OF = (0, 1, 2, 3, 0, 4)
 HALF = E // 2
 
 REST_AT = 0
@@ -42,11 +43,14 @@ RAW = 4 * PACK * N
 GROUPED = 2 * PACK * N
 EARLY_GROUPED_AT = RAW_AT + E * RAW
 WINDOW3_AT = 112 * 1024
-K_AT = WINDOW3_AT + 4 * T - 64
-END_AT = K_AT + 4 * E * N
+K_AT = WINDOW3_AT + 4 * T
+THIRD_AT = K_AT + 4 * HALF * N
+K_LATE_AT = THIRD_AT + RAW
+END_AT = K_LATE_AT + 4 * HALF * N
 X_AT = END_AT
 Q_FIRST_AT = X_AT + 4 * T
-WINDOW0_AT = Q_FIRST_AT + MID * 2 * N
+WINDOW4_AT = Q_FIRST_AT + MID * 2 * N - 64
+WINDOW0_AT = WINDOW4_AT + 4 * T
 
 
 def tile_moe_qkv_kernel(tc, x_words, x_scales, wq_words, wq_scales, wk_words, wk_scales, wv, bias, gate, offs, out):
@@ -87,6 +91,11 @@ def tile_moe_qkv_kernel(tc, x_words, x_scales, wq_words, wq_scales, wk_words, wk
                 out=windows[0][:, i * T // 2 : (i + 1) * T // 2].rearrange("p (r c) -> p r c", c=SEED),
                 in_=zero[:].unsqueeze(1).to_broadcast([P, T // 2 // SEED, SEED]),
             )
+        last_window = tile_at([P, T], F32, "window3", WINDOW3_AT)
+        nc.scalar.copy(
+            out=last_window[:].rearrange("p (r c) -> p r c", c=SEED),
+            in_=zeros[1][:].unsqueeze(1).to_broadcast([P, T // SEED, SEED]),
+        )
         k_plane = tile_at([P, E, N], U8, "k_plane", K_PLANE_AT)
         nc.gpsimd.memset(k_plane[:].bitcast(I32), 0)
         windows.append(tile_at([P, T], F32, "window1", WINDOW1_AT))
@@ -118,16 +127,16 @@ def tile_moe_qkv_kernel(tc, x_words, x_scales, wq_words, wq_scales, wk_words, wk
         nc.sync.dma_start(out=gates[:, MID * C : S], in_=gate[:, MID * C : S])
         load_scale_rows(k_plane[:].bitcast(I32), weight_scale_rows(wk_scales))
         k_rows = wk_words.rearrange("e s p n d -> p (e s) (n d)").bitcast(I32)
-        k_w = [tile_at([P, HALF, N], I32, f"k_w{i}", K_AT + i * 4 * HALF * N) for i in range(2)]
+        k_w = [tile_at([P, HALF, N], I32, f"k_w{i}", place) for i, place in enumerate((K_AT, K_LATE_AT))]
         nc.sync.dma_start(out=k_w[0][:], in_=k_rows[:, 0:HALF])
         bias_kv = tile_at([P, 2 * HALVES, ROW], F32, "bias_kv", BIAS_KV_AT)
         nc.sync.dma_start(out=bias_kv[:, :, 0:E], in_=bias_rows[:, HALVES : 3 * HALVES])
-        nc.sync.dma_start(out=k_w[1][:], in_=k_rows[:, HALF:E])
         v_rows = wv.rearrange("e (p j) n -> p e j n", j=PACK)
-        v_raw = []
-        for e0, e1 in ((0, 1), (1, 2), (2, 3), (3, 5), (5, 6)):
-            v_raw.append(tile_at([P, e1 - e0, PACK, N], F32, f"v_raw{e0}", RAW_AT + e0 * RAW))
-            nc.sync.dma_start(out=v_raw[-1][:], in_=v_rows[:, e0:e1])
+        v_raw = [tile_at([P, PACK, N], F32, f"v_raw{e}", THIRD_AT if e == 2 else RAW_AT + e * RAW) for e in range(E)]
+        nc.sync.dma_start(out=v_raw[0][:], in_=v_rows[:, 0])
+        nc.sync.dma_start(out=k_w[1][:], in_=k_rows[:, HALF:E])
+        for e in range(1, E):
+            nc.sync.dma_start(out=v_raw[e][:], in_=v_rows[:, e])
 
         def entries(s0, s1):
             return offsets[:, s0 // LIST : s1 // LIST]
@@ -141,8 +150,7 @@ def tile_moe_qkv_kernel(tc, x_words, x_scales, wq_words, wq_scales, wk_words, wk
         for e0, e1 in QUERY_RUNS:
             slot_w.extend(gather(tile([P, (e1 - e0) * C], U32, f"slot_w{e0}"), x_w[:].bitcast(U32), e0, e1))
 
-        v_w = tile([P, E, N], U32, "v_w")
-        v_s = tile([P, E, N], U8, "v_s")
+        v_w, v_s = [], []
 
         def weights(b, e):
             cols = slice(b % HALVES * P, (b % HALVES + 1) * P)
@@ -151,7 +159,7 @@ def tile_moe_qkv_kernel(tc, x_words, x_scales, wq_words, wq_scales, wk_words, wk
                 return words[:, 2 * cols.start : 2 * cols.stop].bitcast(FP4X4), q_plane[:, e, cols]
             if b < 2 * HALVES:
                 return k_w[e // HALF][:, e % HALF, cols].bitcast(FP8X4), k_plane[:, e, cols]
-            return v_w[:, e, cols].bitcast(FP8X4), v_s[:, e, cols]
+            return v_w[e][:, cols].bitcast(FP8X4), v_s[e][:, cols]
 
         def multiply(bank, b, e0, e1):
             acc = psum.tile([P, 4 * C], F32, name="acc", tag=f"bank{bank}")
@@ -186,21 +194,22 @@ def tile_moe_qkv_kernel(tc, x_words, x_scales, wq_words, wq_scales, wk_words, wk
                 add,
             )
 
-        def add_bias_on_scalar(y, sums, b, e0, e1):
-            for e in range(e0, e1):
-                nc.scalar.activation(y[:, (e - e0) * C : (e - e0 + 1) * C], sums(e * C, (e + 1) * C), identity, bias=biases(b)[:, e : e + 1])
+        def add_bias_on_scalar(y, sums, b, s0, s1):
+            for e in range(s0 // C, (s1 - 1) // C + 1):
+                lo, hi = max(s0, e * C), min(s1, (e + 1) * C)
+                nc.scalar.activation(y[:, lo - s0 : hi - s0], sums(lo, hi), identity, bias=biases(b)[:, e : e + 1])
 
         def scatter_on_scalar(y, b, s0, s1):
-            nc.scalar.activation(windows[b % WINDOWS][:].indirect(entries(s0, s1)), y, copy)
+            nc.scalar.activation(windows[WINDOW_OF[b]][:].indirect(entries(s0, s1)), y, copy)
 
         def scatter_on_vector(y, b, s0, s1):
-            nc.vector.tensor_tensor(windows[b % WINDOWS][:].indirect(entries(s0, s1)), y, gates[:, s0:s1], mult)
+            nc.vector.tensor_tensor(windows[WINDOW_OF[b]][:].indirect(entries(s0, s1)), y, gates[:, s0:s1], mult)
 
         def copy_scatter_on_vector(y, b, s0, s1):
-            nc.vector.tensor_copy(windows[b % WINDOWS][:].indirect(entries(s0, s1)), y)
+            nc.vector.tensor_copy(windows[WINDOW_OF[b]][:].indirect(entries(s0, s1)), y)
 
         def store(b):
-            nc.sync.dma_start(out=out[b * P : (b + 1) * P, :], in_=windows[b % WINDOWS][:])
+            nc.sync.dma_start(out=out[b * P : (b + 1) * P, :], in_=windows[WINDOW_OF[b]][:])
 
         def result(name, slots, place=None):
             return tile([P, slots], F32, name) if place is None else tile_at([P, slots], F32, name, place)
@@ -218,34 +227,40 @@ def tile_moe_qkv_kernel(tc, x_words, x_scales, wq_words, wq_scales, wk_words, wk
 
         pair = PAIR * C
         y_q1 = result("y_q1a", pair)
-        add_bias_on_scalar(y_q1, multiply(0, Q1, 0, 2), Q1, 0, 2)
+        add_bias_on_scalar(y_q1, multiply(0, Q1, 0, 2), Q1, 0, pair)
         for_scalar(multiply(1, Q0, 0, EARLY), Q0, 0, early)
         q0_mid = multiply(2, Q0, EARLY, MID)
-        y = result("y_q1b", pair, EARLY_GROUPED_AT)
-        add_bias_on_scalar(y, multiply(1, Q1, 2, 3), Q1, 2, 3)
+        y = result("y_q1b", QUERY_CUT - pair, EARLY_GROUPED_AT)
+        add_bias_on_scalar(y, multiply(1, Q1, 2, 3), Q1, pair, mid)
         for_scalar(q0_mid, Q0, early, mid)
-        add_bias_on_scalar(y[:, C:pair], multiply(3, Q1, 3, 4), Q1, 3, 4)
+        q1_mid = multiply(3, Q1, 3, 4)
+        add_bias_on_scalar(y[:, C:], q1_mid, Q1, mid, QUERY_CUT)
         scatter_on_vector(y_q1[:], Q1, 0, pair)
         for_scalar(multiply(4, Q0, MID, E), Q0, mid, S)
         store(Q0)
-        scatter_on_vector(y[:], Q1, pair, 2 * pair)
+        scatter_on_vector(y[:], Q1, pair, QUERY_CUT)
         q1_late = multiply(5, Q1, 4, E)
 
         early_grouped = tile_at([P, ON_GPSIMD, N, PACK], BF16, "early_grouped", EARLY_GROUPED_AT)
 
         k0_first = multiply(6, K0, 0, HALF)
         k1_first = multiply(7, K1, 0, HALF)
-        windows.append(tile_at([P, T], F32, "window3", WINDOW3_AT))
-        nc.gpsimd.memset(windows[3][:], 0.0)
-        for e in range(ON_GPSIMD):
+        windows.append(last_window)
+        windows.append(tile_at([P, T], F32, "window4", WINDOW4_AT))
+        nc.gpsimd.memset(windows[4][:], 0.0)
+
+        def lay_out_on_gpsimd(grouped, e):
             nc.gpsimd.tensor_scalar(
-                early_grouped[:, e].rearrange("p (c i) t -> p c t i", i=4),
-                v_raw[e][:, 0].rearrange("p t (c i) -> p c t i", i=4),
+                grouped.rearrange("p (c i) t -> p c t i", i=4),
+                v_raw[e][:].rearrange("p t (c i) -> p c t i", i=4),
                 1.0,
                 0.0,
                 mult,
                 add,
             )
+
+        for e in range(ON_GPSIMD):
+            lay_out_on_gpsimd(early_grouped[:, e], e)
 
         y_k1 = result("y_k1z", KEY_SHARE)
         finish(y_k1, k1_first, K1, 0, KEY_SHARE)
@@ -256,48 +271,61 @@ def tile_moe_qkv_kernel(tc, x_words, x_scales, wq_words, wq_scales, wk_words, wk
         scatter_on_scalar(y[:], K1, KEY_SHARE, half)
         k0_late = multiply(0, K0, HALF, E)
         k1_late = multiply(1, K1, HALF, E)
-        y_q1 = result("y_q1c", pair, K_AT + 4 * HALF * N)
-        finish(y_q1, q1_late, Q1, 2 * pair, S)
+        y_q1 = result("y_q1c", S - QUERY_CUT, K_LATE_AT)
+        finish(y_q1, q1_mid, Q1, QUERY_CUT, 2 * pair)
+        finish(y_q1[:, 2 * pair - QUERY_CUT :], q1_late, Q1, 2 * pair, S)
         y = result("y_k0b", half)
         finish(y, k0_late, K0, half, S)
-        copy_scatter_on_vector(y_q1[:], Q1, 2 * pair, S)
+        copy_scatter_on_vector(y_q1[:], Q1, QUERY_CUT, S)
         store(Q1)
         scatter_on_scalar(y[:], K0, half, S)
         store(K0)
         for_scalar(k1_late, K1, half, 5 * C)
 
-        def lay_out(grouped, raw):
-            nc.vector.tensor_copy(
-                out=grouped[:].rearrange("p e (c i) t -> p e c t i", i=4),
-                in_=raw[:].rearrange("p e t (c i) -> p e c t i", i=4),
-            )
+        def quantise(grouped, count, place=None, scales_place=None):
+            first = len(v_w)
+            shape = [P, count * N]
+            words = tile(shape, U32, f"v_w{first}") if place is None else tile_at(shape, U32, f"v_w{first}", place)
+            scales = tile(shape, U8, f"v_s{first}") if scales_place is None else tile_at(shape, U8, f"v_s{first}", scales_place)
+            nc.vector.quantize_mx(out=words[:].bitcast(FP8X4), scales=scales[:], in_=grouped.rearrange("p e n t -> p (e n t)"))
+            v_w.extend(words[:, i * N : (i + 1) * N] for i in range(count))
+            v_s.extend(scales[:, i * N : (i + 1) * N] for i in range(count))
 
-        def quantise(grouped, e0, e1):
-            nc.vector.quantize_mx(
-                out=v_w[:, e0:e1].rearrange("p e n -> p (e n)").bitcast(FP8X4),
-                scales=v_s[:, e0:e1].rearrange("p e n -> p (e n)"),
-                in_=grouped.rearrange("p e n t -> p (e n t)"),
-            )
+        quantise(early_grouped[:, 0:2], 2, THIRD_AT, K_LATE_AT + N)
+        grouped = tile_at([P, 1, N, PACK], BF16, "grouped3", K_LATE_AT + N - GROUPED)
+        nc.vector.tensor_copy(
+            out=grouped[:, 0].rearrange("p (c i) t -> p c t i", i=4),
+            in_=v_raw[3][:].rearrange("p t (c i) -> p c t i", i=4),
+        )
+        quantise(early_grouped[:, 2:3], 1, None, K_LATE_AT + 3 * N)
+        quantise(grouped[:], 1, EARLY_GROUPED_AT + ON_GPSIMD * GROUPED)
+        grouped = tile_at([P, PAIR, N, PACK], BF16, "grouped45", EARLY_GROUPED_AT)
+        for j in range(PAIR):
+            lay_out_on_gpsimd(grouped[:, j], 4 + j)
 
-        quantise(early_grouped[:, 0:2], 0, 2)
-        quantise(early_grouped[:, 2:3], 2, 3)
-        late_at = RAW_AT + 2 * RAW - GROUPED
-        grouped34 = tile_at([P, 2, N, PACK], BF16, "grouped34", late_at)
-        grouped5 = tile_at([P, 1, N, PACK], BF16, "grouped5", late_at + 2 * GROUPED)
-        lay_out(grouped34, v_raw[3])
-        for_scalar(multiply(2, V0, 0, HALF), V0, 0, half)
-        quantise(grouped34[:], 3, 5)
-        lay_out(grouped5, v_raw[4])
-        y_v1 = result("y_v1", S)
-        add_bias(y_v1[:, 0 : 2 * pair], multiply(4, V1, 0, 4), V1, 0, 2 * pair)
-        quantise(grouped5[:], 5, 6)
-        y_v0 = result("y_v0b", half)
-        finish(y_v0[:, 0:pair], multiply(3, V0, HALF, 5), V0, half, 5 * C)
-        for_scalar(k1_late, K1, 5 * C, S, late_at)
+        y_v0 = result("y_v0a", half)
+        finish(y_v0, multiply(2, V0, 0, 2), V0, 0, pair)
+        y = result("y_v1a", half)
+        finish(y, multiply(4, V1, 0, 2), V1, 0, pair)
+        v1_mid = multiply(5, V1, 2, 4)
+        v0_mid = multiply(3, V0, 2, 4)
+        finish(y[:, pair:], v1_mid, V1, pair, half)
+        finish(y_v0[:, pair:half], v0_mid, V0, pair, half)
+        scatter_on_scalar(y_v0[:], V0, 0, half)
+        for_scalar(k1_late, K1, 5 * C, S, EARLY_GROUPED_AT + ON_GPSIMD * GROUPED)
         store(K1)
-        add_bias(y_v1[:, 2 * pair : S], multiply(5, V1, 4, E), V1, 2 * pair, S)
-        finish(y_v0[:, pair:half], multiply(6, V0, 5, E), V0, 5 * C, S)
+        copy_scatter_on_vector(y[:], V1, 0, half)
+        y_v0 = result("y_v0b", half)
+        finish(y_v0, v0_mid, V0, half, 2 * pair)
+        y = result("y_v1b", C, RAW_AT + 5 * RAW)
+        add_bias(y[:], v1_mid, V1, half, 2 * pair)
+        quantise(grouped[:], 2)
+
+        scatter_on_vector(y[:], V1, half, 2 * pair)
+        y = result("y_v1c", pair)
+        add_bias(y[:], multiply(6, V1, 4, E), V1, 2 * pair, S)
+        finish(y_v0[:, C:half], multiply(0, V0, 4, E), V0, 2 * pair, S)
+        scatter_on_vector(y[:], V1, 2 * pair, S)
+        store(V1)
         scatter_on_scalar(y_v0[:], V0, half, S)
         store(V0)
-        scatter_on_vector(y_v1[:], V1, 0, S)
-        store(V1)

@@ -1,6 +1,7 @@
 from contextlib import ExitStack
 
 import concourse.mybir as mybir
+from concourse.masks import make_identity
 
 K, T, E, C, N = 512, 1024, 6, 128, 256
 FLOPS = 2 * K * 3 * N * E * C
@@ -19,65 +20,59 @@ PACK = 4
 S = E * C
 LIST = 16
 HALVES = N // P
-EARLY = 1
-MID = 3
-QUERY_RUNS = ((0, MID), (MID, E))
+HALF = E // 2
 PAIR = 2
-ON_GPSIMD = 3
-QUERY_CUT = 448
-KEY_SHARE = 192
+RUNS = ((0, 1), (1, HALF), (HALF, E))
+WORD_RUNS = ((0, 1), (1, 2 * PAIR), (2 * PAIR, E))
+EARLY_BYTES = 4
+SPREAD = HALF * C // P
 SEED = 64
 ROW = 8
-WINDOW_OF = (0, 1, 2, 3, 0, 4)
-HALF = E // 2
 
-REST_AT = 0
-BIAS_Q_AT = REST_AT
-BIAS_KV_AT = BIAS_Q_AT + 4 * HALVES * ROW
-GATES_AT = BIAS_KV_AT + 4 * 2 * HALVES * ROW
-Q_LATE_AT = GATES_AT + 4 * S
-K_PLANE_AT = Q_LATE_AT + (E - MID) * 2 * N
-WINDOW1_AT = K_PLANE_AT + E * N
-RAW_AT = WINDOW1_AT + 4 * T
 RAW = 4 * PACK * N
 GROUPED = 2 * PACK * N
-EARLY_GROUPED_AT = RAW_AT + E * RAW
-WINDOW3_AT = 112 * 1024
-K_AT = WINDOW3_AT + 4 * T
-THIRD_AT = K_AT + 4 * HALF * N
-K_LATE_AT = THIRD_AT + RAW
-END_AT = K_LATE_AT + 4 * HALF * N
+REST_AT = 0
+IDENTITY_AT = REST_AT
+BIAS_Q_AT = IDENTITY_AT + 4 * P
+BIAS_KV_AT = BIAS_Q_AT + 4 * HALVES * ROW
+Q_MID_AT = BIAS_KV_AT + 4 * 2 * HALVES * ROW
+Q_LATE_AT = Q_MID_AT + PAIR * 2 * N
+K_PLANE_AT = Q_LATE_AT + HALF * 2 * N
+K_AT = K_PLANE_AT + E * N
+RAW_AT = K_AT + 4 * E * N
+WINDOWS_AT = RAW_AT + E * RAW
+END_AT = WINDOWS_AT + (3 * HALVES - 1) * 4 * T
 X_AT = END_AT
+SEED_AT = X_AT + 4 * T - 4 * SEED
 Q_FIRST_AT = X_AT + 4 * T
-WINDOW4_AT = Q_FIRST_AT + MID * 2 * N - 64
-WINDOW0_AT = WINDOW4_AT + 4 * T
+GROUPED_AT = Q_FIRST_AT + 4 * PAIR * C
+V_WORDS_AT = GROUPED_AT + PAIR * GROUPED
+FIRST_RESULT_AT = V_WORDS_AT + 4 * PAIR * N
 
 
 def tile_moe_qkv_kernel(tc, x_words, x_scales, wq_words, wq_scales, wk_words, wk_scales, wv, bias, gate, offs, out):
     nc = tc.nc
     add, mult = mybir.AluOpType.add, mybir.AluOpType.mult
-    copy, identity = mybir.ActivationFunctionType.Copy, mybir.ActivationFunctionType.Identity
+    copy = mybir.ActivationFunctionType.Copy
 
     with ExitStack() as ctx:
         keep = ctx.enter_context(tc.tile_pool(name="keep", bufs=1))
         laid = ctx.enter_context(tc.tile_pool(name="laid", bufs=1))
         psum = ctx.enter_context(tc.psum_pool(name="psum", bufs=1))
 
-        def tile(shape, dtype, name):
-            return keep.tile(shape, dtype, name=name, align_bytes=64)
-
-        def tile_at(shape, dtype, name, place):
+        def tile(shape, dtype, name, place=None):
+            if place is None:
+                return keep.tile(shape, dtype, name=name, align_bytes=64)
             return laid.tile(shape, dtype, name=name, align_bytes=64, offset=place)
 
         offsets = keep.tile([P, S // LIST], U16, name="offsets")
         x_s = tile([P, T], U8, "x_s")
         q_plane = tile([P, E, N], U8, "q_plane")
         seeds = [
-            tile_at([P, SEED], F32, "seed0", Q_FIRST_AT - 128),
-            tile_at([P, (END_AT - REST_AT) // 4], F32, "seed1", REST_AT),
+            tile([P, SEED], F32, "seed0", SEED_AT),
+            tile([P, (END_AT - REST_AT) // 4], F32, "seed1", REST_AT),
         ]
         zeros = [tile([P, SEED], F32, f"zero{i}") for i in range(2)]
-        windows = [tile_at([P, T], F32, "window0", WINDOW0_AT)]
 
         nc.vector.memset(x_s[:].bitcast(I32), 0)
         for seed in seeds:
@@ -86,20 +81,20 @@ def tile_moe_qkv_kernel(tc, x_words, x_scales, wq_words, wq_scales, wk_words, wk
         nc.vector.memset(q_plane[:].bitcast(I32), 0)
         nc.vector.tensor_copy(zeros[1][:], seeds[1][:, 0:SEED])
 
+        identity = tile([P, P], F32, "identity", IDENTITY_AT)
+        make_identity(nc, identity[:])
+
+        windows = [tile([P, T], F32, "window0")]
         for i, zero in enumerate(zeros):
             nc.scalar.copy(
                 out=windows[0][:, i * T // 2 : (i + 1) * T // 2].rearrange("p (r c) -> p r c", c=SEED),
                 in_=zero[:].unsqueeze(1).to_broadcast([P, T // 2 // SEED, SEED]),
             )
-        last_window = tile_at([P, T], F32, "window3", WINDOW3_AT)
-        nc.scalar.copy(
-            out=last_window[:].rearrange("p (r c) -> p r c", c=SEED),
-            in_=zeros[1][:].unsqueeze(1).to_broadcast([P, T // SEED, SEED]),
-        )
-        k_plane = tile_at([P, E, N], U8, "k_plane", K_PLANE_AT)
+        k_plane = tile([P, E, N], U8, "k_plane", K_PLANE_AT)
         nc.gpsimd.memset(k_plane[:].bitcast(I32), 0)
-        windows.append(tile_at([P, T], F32, "window1", WINDOW1_AT))
-        nc.gpsimd.memset(windows[1][:], 0.0)
+        for i in range(3 * HALVES - 1):
+            windows.append(tile([P, T], F32, f"window{1 + i}", WINDOWS_AT + i * 4 * T))
+            nc.gpsimd.memset(windows[-1][:], 0.0)
 
         def load_scale_rows(plane, rows):
             for r in range(PACK):
@@ -109,34 +104,49 @@ def tile_moe_qkv_kernel(tc, x_words, x_scales, wq_words, wq_scales, wk_words, wk
             return scales.bitcast(I32).rearrange("e s (q r) n -> r q (e s) n", r=PACK)
 
         q_rows = wq_words.bitcast(I32).rearrange("e s p b -> p (e s) b")
-        bias_rows = bias.rearrange("(b p) e -> p b e", p=P)
+        k_rows = wk_words.rearrange("e s p n d -> p (e s) (n d)").bitcast(I32)
+        v_rows = wv.rearrange("e (p j) n -> p e j n", j=PACK)
 
         nc.sync.dma_start(offsets[:], offs)
+        gate_row = tile([P, 2, ROW], F32, "gate_row")
+        nc.sync.dma_start(out=gate_row[:, :, 0:SPREAD], in_=gate[0].rearrange("(h p j) -> p h j", h=2, j=SPREAD))
+        q_places = (Q_FIRST_AT, Q_MID_AT, Q_LATE_AT)
+        q_w = [tile([P, e1 - e0, 2 * N], U8, f"q_w{e0}", place) for (e0, e1), place in zip(RUNS, q_places)]
+
+        def load_queries(run):
+            nc.sync.dma_start(out=q_w[run][:].bitcast(I32), in_=q_rows[:, RUNS[run][0] : RUNS[run][1]])
+
+        load_queries(0)
         load_scale_rows(x_s[:].bitcast(I32), x_scales[0].bitcast(I32).rearrange("(q r) t -> r q t", r=PACK))
-        x_w = tile_at([P, T], I32, "x_w", X_AT)
+        x_w = tile([P, T], I32, "x_w", X_AT)
         nc.sync.dma_start(out=x_w[:], in_=x_words[0].rearrange("p t d -> p (t d)").bitcast(I32))
-        q_first = tile_at([P, MID, 2 * N], U8, "q_first", Q_FIRST_AT)
-        nc.sync.dma_start(out=q_first[:].bitcast(I32), in_=q_rows[:, 0:MID])
-        load_scale_rows(q_plane[:].bitcast(I32), weight_scale_rows(wq_scales))
-        bias_q = tile_at([P, HALVES, ROW], F32, "bias_q", BIAS_Q_AT)
+        bias_rows = bias.rearrange("(b p) e -> p b e", p=P)
+        bias_q = tile([P, HALVES, ROW], F32, "bias_q", BIAS_Q_AT)
         nc.sync.dma_start(out=bias_q[:, :, 0:E], in_=bias_rows[:, 0:HALVES])
-        gates = tile_at([P, S], F32, "gates", GATES_AT)
-        nc.sync.dma_start(out=gates[:, 0 : MID * C], in_=gate[:, 0 : MID * C])
-        q_late = tile_at([P, E - MID, 2 * N], U8, "q_late", Q_LATE_AT)
-        nc.sync.dma_start(out=q_late[:].bitcast(I32), in_=q_rows[:, MID:E])
-        nc.sync.dma_start(out=gates[:, MID * C : S], in_=gate[:, MID * C : S])
-        load_scale_rows(k_plane[:].bitcast(I32), weight_scale_rows(wk_scales))
-        k_rows = wk_words.rearrange("e s p n d -> p (e s) (n d)").bitcast(I32)
-        k_w = [tile_at([P, HALF, N], I32, f"k_w{i}", place) for i, place in enumerate((K_AT, K_LATE_AT))]
+        load_scale_rows(q_plane[:].bitcast(I32), weight_scale_rows(wq_scales))
+        load_queries(1)
+        k_w = [tile([P, HALF, N], I32, f"k_w{i}", K_AT + i * 4 * HALF * N) for i in range(2)]
         nc.sync.dma_start(out=k_w[0][:], in_=k_rows[:, 0:HALF])
-        bias_kv = tile_at([P, 2 * HALVES, ROW], F32, "bias_kv", BIAS_KV_AT)
+        load_scale_rows(k_plane[:].bitcast(I32), weight_scale_rows(wk_scales))
+        bias_kv = tile([P, 2 * HALVES, ROW], F32, "bias_kv", BIAS_KV_AT)
         nc.sync.dma_start(out=bias_kv[:, :, 0:E], in_=bias_rows[:, HALVES : 3 * HALVES])
-        v_rows = wv.rearrange("e (p j) n -> p e j n", j=PACK)
-        v_raw = [tile_at([P, PACK, N], F32, f"v_raw{e}", THIRD_AT if e == 2 else RAW_AT + e * RAW) for e in range(E)]
-        nc.sync.dma_start(out=v_raw[0][:], in_=v_rows[:, 0])
-        nc.sync.dma_start(out=k_w[1][:], in_=k_rows[:, HALF:E])
-        for e in range(1, E):
+        load_queries(2)
+        v_raw = [tile([P, PACK, N], F32, f"v_raw{e}", RAW_AT + e * RAW) for e in range(E)]
+        for e in range(PAIR):
             nc.sync.dma_start(out=v_raw[e][:], in_=v_rows[:, e])
+        nc.sync.dma_start(out=k_w[1][:], in_=k_rows[:, HALF:E])
+        for e in range(PAIR, E):
+            nc.sync.dma_start(out=v_raw[e][:], in_=v_rows[:, e])
+
+        gates = tile([P, S], F32, "gates")
+        for h in range(2):
+            spread = psum.tile([P, 4, P], F32, name="spread", tag=f"bank{6 + h}")
+            for j in range(SPREAD):
+                nc.tensor.transpose(spread[:, j], gate_row[:, h, j : j + 1].to_broadcast([P, P]), identity[:])
+            nc.scalar.copy(
+                out=gates[:, h * HALF * C : (h + 1) * HALF * C].rearrange("p (n j) -> p n j", j=SPREAD),
+                in_=spread[:, 0:SPREAD].rearrange("p j n -> p n j"),
+            )
 
         def entries(s0, s1):
             return offsets[:, s0 // LIST : s1 // LIST]
@@ -145,18 +155,24 @@ def tile_moe_qkv_kernel(tc, x_words, x_scales, wq_words, wq_scales, wk_words, wk
             nc.vector.tensor_copy(part[:], table.indirect(entries(e0 * C, e1 * C)))
             return [part[:, i * C : (i + 1) * C] for i in range(e1 - e0)]
 
-        slot_s = gather(tile([P, S], U8, "slot_s"), x_s[:], 0, E)
+        slot_s = gather(tile([P, EARLY_BYTES * C], U8, "slot_s0"), x_s[:], 0, EARLY_BYTES)
         slot_w = []
-        for e0, e1 in QUERY_RUNS:
-            slot_w.extend(gather(tile([P, (e1 - e0) * C], U32, f"slot_w{e0}"), x_w[:].bitcast(U32), e0, e1))
+
+        def gather_words(run, place=None):
+            e0, e1 = WORD_RUNS[run]
+            slot_w.extend(gather(tile([P, (e1 - e0) * C], U32, f"slot_w{e0}", place), x_w[:].bitcast(U32), e0, e1))
+
+        gather_words(0)
+        gather_words(1)
+        q_of = [words[:, e - e0] for words, (e0, e1) in zip(q_w, RUNS) for e in range(e0, e1)]
 
         v_w, v_s = [], []
+        sums = {}
 
         def weights(b, e):
             cols = slice(b % HALVES * P, (b % HALVES + 1) * P)
             if b < HALVES:
-                words = q_first[:, e] if e < MID else q_late[:, e - MID]
-                return words[:, 2 * cols.start : 2 * cols.stop].bitcast(FP4X4), q_plane[:, e, cols]
+                return q_of[e][:, 2 * cols.start : 2 * cols.stop].bitcast(FP4X4), q_plane[:, e, cols]
             if b < 2 * HALVES:
                 return k_w[e // HALF][:, e % HALF, cols].bitcast(FP8X4), k_plane[:, e, cols]
             return v_w[e][:, cols].bitcast(FP8X4), v_s[e][:, cols]
@@ -165,8 +181,9 @@ def tile_moe_qkv_kernel(tc, x_words, x_scales, wq_words, wq_scales, wk_words, wk
             acc = psum.tile([P, 4 * C], F32, name="acc", tag=f"bank{bank}")
             for e in range(e0, e1):
                 w_codes, w_scales = weights(b, e)
+                sums[b, e] = acc[:, (e - e0) * C : (e - e0 + 1) * C]
                 nc.tensor.matmul_mx(
-                    out=acc[:, (e - e0) * C : (e - e0 + 1) * C],
+                    out=sums[b, e],
                     lhsT=w_codes,
                     lhsT_scale=w_scales,
                     rhs=slot_w[e].bitcast(FP8X4),
@@ -174,158 +191,121 @@ def tile_moe_qkv_kernel(tc, x_words, x_scales, wq_words, wq_scales, wk_words, wk
                     start=True,
                     stop=True,
                 )
-            return lambda s0, s1: acc[:, s0 - e0 * C : s1 - e0 * C]
 
-        def biases(b):
-            return bias_q[:, b] if b < HALVES else bias_kv[:, b - HALVES]
+        def piece(b, e0, e1, place=None):
+            return b, e0, e1, tile([P, (e1 - e0) * C], F32, f"y{b}_{e0}", place)
 
-        def finish(y, sums, b, s0, s1):
-            for e in range(s0 // C, (s1 - 1) // C + 1):
-                lo, hi = max(s0, e * C), min(s1, (e + 1) * C)
-                nc.vector.scalar_tensor_tensor(y[:, lo - s0 : hi - s0], sums(lo, hi), biases(b)[:, e : e + 1], gates[:, lo:hi], add, mult)
+        def finish(part, e0, e1):
+            b, first, last, y = part
+            biases = bias_q[:, b] if b < HALVES else bias_kv[:, b - HALVES]
+            for e in range(e0, e1):
+                nc.vector.scalar_tensor_tensor(
+                    y[:, (e - first) * C : (e - first + 1) * C], sums[b, e], biases[:, e : e + 1], gates[:, e * C : (e + 1) * C], add, mult
+                )
 
-        def add_bias(y, sums, b, s0, s1):
-            width = min(C, s1 - s0)
-            e0, count = s0 // C, (s1 - s0) // width
-            nc.vector.tensor_tensor(
-                y.rearrange("p (e c) -> p e c", c=width),
-                sums(s0, s1).rearrange("p (e c) -> p e c", c=width),
-                biases(b)[:, e0 : e0 + count].unsqueeze(2).to_broadcast([P, count, width]),
-                add,
-            )
+        def finished(b, e0, e1, place=None):
+            part = piece(b, e0, e1, place)
+            finish(part, e0, e1)
+            return part
 
-        def add_bias_on_scalar(y, sums, b, s0, s1):
-            for e in range(s0 // C, (s1 - 1) // C + 1):
-                lo, hi = max(s0, e * C), min(s1, (e + 1) * C)
-                nc.scalar.activation(y[:, lo - s0 : hi - s0], sums(lo, hi), identity, bias=biases(b)[:, e : e + 1])
+        def columns(part):
+            b, e0, e1, y = part
+            return windows[b][:].indirect(entries(e0 * C, e1 * C))
 
-        def scatter_on_scalar(y, b, s0, s1):
-            nc.scalar.activation(windows[WINDOW_OF[b]][:].indirect(entries(s0, s1)), y, copy)
+        def scatter_on_scalar(part):
+            nc.scalar.activation(columns(part), part[3][:], copy)
 
-        def scatter_on_vector(y, b, s0, s1):
-            nc.vector.tensor_tensor(windows[WINDOW_OF[b]][:].indirect(entries(s0, s1)), y, gates[:, s0:s1], mult)
-
-        def copy_scatter_on_vector(y, b, s0, s1):
-            nc.vector.tensor_copy(windows[WINDOW_OF[b]][:].indirect(entries(s0, s1)), y)
+        def scatter_on_vector(part):
+            nc.vector.tensor_copy(columns(part), part[3][:])
 
         def store(b):
-            nc.sync.dma_start(out=out[b * P : (b + 1) * P, :], in_=windows[WINDOW_OF[b]][:])
+            nc.sync.dma_start(out=out[b * P : (b + 1) * P, :], in_=windows[b][:])
 
-        def result(name, slots, place=None):
-            return tile([P, slots], F32, name) if place is None else tile_at([P, slots], F32, name, place)
+        def lay_out(e0):
+            grouped = tile([P, PAIR, N, PACK], BF16, f"grouped{e0}", GROUPED_AT)
+            for e in range(e0, e0 + PAIR):
+                nc.gpsimd.tensor_scalar(
+                    grouped[:, e - e0].rearrange("p (c i) t -> p c t i", i=4),
+                    v_raw[e][:].rearrange("p t (c i) -> p c t i", i=4),
+                    1.0,
+                    0.0,
+                    mult,
+                    add,
+                )
+            return grouped
 
-        def for_scalar(sums, b, s0, s1, place=None):
-            y = result(f"y{b}_{s0}", s1 - s0, place)
-            finish(y, sums, b, s0, s1)
-            scatter_on_scalar(y[:], b, s0, s1)
+        def quantise(grouped, place=None):
+            first = len(v_w)
+            words = tile([P, PAIR * N], U32, f"v_w{first}", place)
+            scales = tile([P, PAIR * N], U8, f"v_s{first}")
+            nc.vector.quantize_mx(out=words[:].bitcast(FP8X4), scales=scales[:], in_=grouped[:].rearrange("p e n t -> p (e n t)"))
+            v_w.extend(words[:, i * N : (i + 1) * N] for i in range(PAIR))
+            v_s.extend(scales[:, i * N : (i + 1) * N] for i in range(PAIR))
 
         Q0, Q1, K0, K1, V0, V1 = range(3 * HALVES)
-        early, mid, half = EARLY * C, MID * C, HALF * C
 
-        windows.append(tile_at([P, T], F32, "window2", X_AT))
-        nc.gpsimd.memset(windows[2][:], 0.0)
+        multiply(0, Q0, 0, 1)
+        multiply(1, Q1, 0, 1)
+        multiply(2, Q0, 1, HALF)
+        multiply(3, Q1, 1, HALF)
+        scatter_on_scalar(finished(Q0, 0, 1, FIRST_RESULT_AT))
+        scatter_on_scalar(finished(Q1, 0, 1))
+        gather_words(2, Q_FIRST_AT)
+        scatter_on_scalar(finished(Q0, 1, HALF))
+        slot_s.extend(gather(tile([P, (E - EARLY_BYTES) * C], U8, "slot_s1", FIRST_RESULT_AT), x_s[:], EARLY_BYTES, E))
+        scatter_on_scalar(finished(Q1, 1, HALF))
 
-        pair = PAIR * C
-        y_q1 = result("y_q1a", pair)
-        add_bias_on_scalar(y_q1, multiply(0, Q1, 0, 2), Q1, 0, pair)
-        for_scalar(multiply(1, Q0, 0, EARLY), Q0, 0, early)
-        q0_mid = multiply(2, Q0, EARLY, MID)
-        y = result("y_q1b", QUERY_CUT - pair, EARLY_GROUPED_AT)
-        add_bias_on_scalar(y, multiply(1, Q1, 2, 3), Q1, pair, mid)
-        for_scalar(q0_mid, Q0, early, mid)
-        q1_mid = multiply(3, Q1, 3, 4)
-        add_bias_on_scalar(y[:, C:], q1_mid, Q1, mid, QUERY_CUT)
-        scatter_on_vector(y_q1[:], Q1, 0, pair)
-        for_scalar(multiply(4, Q0, MID, E), Q0, mid, S)
+        multiply(4, K1, 0, HALF)
+        multiply(5, K0, 0, HALF)
+        multiply(6, Q0, HALF, E)
+        multiply(7, Q1, HALF, E)
+        k1 = finished(K1, 0, PAIR)
+        k0 = finished(K0, 0, HALF)
+        scatter_on_scalar(finished(Q0, HALF, E))
         store(Q0)
-        scatter_on_vector(y[:], Q1, pair, QUERY_CUT)
-        q1_late = multiply(5, Q1, 4, E)
-
-        early_grouped = tile_at([P, ON_GPSIMD, N, PACK], BF16, "early_grouped", EARLY_GROUPED_AT)
-
-        k0_first = multiply(6, K0, 0, HALF)
-        k1_first = multiply(7, K1, 0, HALF)
-        windows.append(last_window)
-        windows.append(tile_at([P, T], F32, "window4", WINDOW4_AT))
-        nc.gpsimd.memset(windows[4][:], 0.0)
-
-        def lay_out_on_gpsimd(grouped, e):
-            nc.gpsimd.tensor_scalar(
-                grouped.rearrange("p (c i) t -> p c t i", i=4),
-                v_raw[e][:].rearrange("p t (c i) -> p c t i", i=4),
-                1.0,
-                0.0,
-                mult,
-                add,
-            )
-
-        for e in range(ON_GPSIMD):
-            lay_out_on_gpsimd(early_grouped[:, e], e)
-
-        y_k1 = result("y_k1z", KEY_SHARE)
-        finish(y_k1, k1_first, K1, 0, KEY_SHARE)
-        for_scalar(k0_first, K0, 0, half)
-        y = result("y_k1a", half - KEY_SHARE)
-        finish(y, k1_first, K1, KEY_SHARE, half)
-        copy_scatter_on_vector(y_k1[:], K1, 0, KEY_SHARE)
-        scatter_on_scalar(y[:], K1, KEY_SHARE, half)
-        k0_late = multiply(0, K0, HALF, E)
-        k1_late = multiply(1, K1, HALF, E)
-        y_q1 = result("y_q1c", S - QUERY_CUT, K_LATE_AT)
-        finish(y_q1, q1_mid, Q1, QUERY_CUT, 2 * pair)
-        finish(y_q1[:, 2 * pair - QUERY_CUT :], q1_late, Q1, 2 * pair, S)
-        y = result("y_k0b", half)
-        finish(y, k0_late, K0, half, S)
-        copy_scatter_on_vector(y_q1[:], Q1, QUERY_CUT, S)
+        scatter_on_vector(k1)
+        k1 = finished(K1, PAIR, HALF, Q_LATE_AT)
+        scatter_on_scalar(finished(Q1, HALF, E))
         store(Q1)
-        scatter_on_scalar(y[:], K0, half, S)
-        store(K0)
-        for_scalar(k1_late, K1, half, 5 * C)
+        scatter_on_scalar(k0)
+        scatter_on_vector(k1)
 
-        def quantise(grouped, count, place=None, scales_place=None):
-            first = len(v_w)
-            shape = [P, count * N]
-            words = tile(shape, U32, f"v_w{first}") if place is None else tile_at(shape, U32, f"v_w{first}", place)
-            scales = tile(shape, U8, f"v_s{first}") if scales_place is None else tile_at(shape, U8, f"v_s{first}", scales_place)
-            nc.vector.quantize_mx(out=words[:].bitcast(FP8X4), scales=scales[:], in_=grouped.rearrange("p e n t -> p (e n t)"))
-            v_w.extend(words[:, i * N : (i + 1) * N] for i in range(count))
-            v_s.extend(scales[:, i * N : (i + 1) * N] for i in range(count))
-
-        quantise(early_grouped[:, 0:2], 2, THIRD_AT, K_LATE_AT + N)
-        grouped = tile_at([P, 1, N, PACK], BF16, "grouped3", K_LATE_AT + N - GROUPED)
-        nc.vector.tensor_copy(
-            out=grouped[:, 0].rearrange("p (c i) t -> p c t i", i=4),
-            in_=v_raw[3][:].rearrange("p t (c i) -> p c t i", i=4),
-        )
-        quantise(early_grouped[:, 2:3], 1, None, K_LATE_AT + 3 * N)
-        quantise(grouped[:], 1, EARLY_GROUPED_AT + ON_GPSIMD * GROUPED)
-        grouped = tile_at([P, PAIR, N, PACK], BF16, "grouped45", EARLY_GROUPED_AT)
-        for j in range(PAIR):
-            lay_out_on_gpsimd(grouped[:, j], 4 + j)
-
-        y_v0 = result("y_v0a", half)
-        finish(y_v0, multiply(2, V0, 0, 2), V0, 0, pair)
-        y = result("y_v1a", half)
-        finish(y, multiply(4, V1, 0, 2), V1, 0, pair)
-        v1_mid = multiply(5, V1, 2, 4)
-        v0_mid = multiply(3, V0, 2, 4)
-        finish(y[:, pair:], v1_mid, V1, pair, half)
-        finish(y_v0[:, pair:half], v0_mid, V0, pair, half)
-        scatter_on_scalar(y_v0[:], V0, 0, half)
-        for_scalar(k1_late, K1, 5 * C, S, EARLY_GROUPED_AT + ON_GPSIMD * GROUPED)
+        quantise(lay_out(0))
+        grouped = lay_out(PAIR)
+        multiply(1, K1, HALF, E)
+        multiply(0, K0, HALF, E)
+        multiply(3, V0, 0, PAIR)
+        multiply(2, V1, 0, PAIR)
+        k1 = finished(K1, HALF, E, RAW_AT + RAW)
+        v0, v1 = piece(V0, 0, HALF), piece(V1, 1, HALF)
+        finish(v0, 0, PAIR)
+        finish(v1, 1, PAIR)
+        scatter_on_vector(k1)
         store(K1)
-        copy_scatter_on_vector(y[:], V1, 0, half)
-        y_v0 = result("y_v0b", half)
-        finish(y_v0, v0_mid, V0, half, 2 * pair)
-        y = result("y_v1b", C, RAW_AT + 5 * RAW)
-        add_bias(y[:], v1_mid, V1, half, 2 * pair)
-        quantise(grouped[:], 2)
 
-        scatter_on_vector(y[:], V1, half, 2 * pair)
-        y = result("y_v1c", pair)
-        add_bias(y[:], multiply(6, V1, 4, E), V1, 2 * pair, S)
-        finish(y_v0[:, C:half], multiply(0, V0, 4, E), V0, 2 * pair, S)
-        scatter_on_vector(y[:], V1, 2 * pair, S)
+        filler = finished(V1, 0, 1, RAW_AT + 3 * RAW)
+        quantise(grouped, V_WORDS_AT)
+        grouped = lay_out(2 * PAIR)
+        scatter_on_vector(filler)
+        multiply(5, V0, PAIR, 2 * PAIR)
+        multiply(4, V1, PAIR, 2 * PAIR)
+        finish(v0, PAIR, HALF)
+        scatter_on_scalar(v0)
+        finish(v1, PAIR, HALF)
+        scatter_on_scalar(finished(K0, HALF, E, V_WORDS_AT))
+        store(K0)
+        v0 = piece(V0, HALF, E)
+        finish(v0, HALF, 2 * PAIR)
+        scatter_on_vector(v1)
+
+        filler = finished(V1, HALF, 2 * PAIR, RAW_AT + 5 * RAW)
+        quantise(grouped)
+        scatter_on_vector(filler)
+        multiply(6, V1, 2 * PAIR, E)
+        multiply(7, V0, 2 * PAIR, E)
+        v1 = finished(V1, 2 * PAIR, E)
+        finish(v0, 2 * PAIR, E)
+        scatter_on_vector(v1)
         store(V1)
-        scatter_on_scalar(y_v0[:], V0, half, S)
+        scatter_on_scalar(v0)
         store(V0)

from contextlib import ExitStack

import concourse.mybir as mybir
from concourse.masks import make_identity

K, T, E, C, N = 512, 1024, 6, 128, 256
FLOPS = 2 * K * 3 * N * E * C

F32 = mybir.dt.float32
BF16 = mybir.dt.bfloat16
I32 = mybir.dt.int32
U32 = mybir.dt.uint32
U16 = mybir.dt.uint16
U8 = mybir.dt.uint8
FP8X4 = mybir.dt.float8_e4m3fn_x4
FP4X4 = mybir.dt.float4_e2m1fn_x4

P = 128
PACK = 4
S = E * C
LIST = 16
HALVES = N // P
HALF = E // 2
PAIR = 2
RUNS = ((0, 1), (1, HALF), (HALF, E))
WORD_RUNS = ((0, 1), (1, 2 * PAIR), (2 * PAIR, E))
EARLY_BYTES = 4
SPREAD = HALF * C // P
SEED = 64
ROW = 8

RAW = 4 * PACK * N
GROUPED = 2 * PACK * N
REST_AT = 0
IDENTITY_AT = REST_AT
BIAS_Q_AT = IDENTITY_AT + 4 * P
BIAS_KV_AT = BIAS_Q_AT + 4 * HALVES * ROW
Q_MID_AT = BIAS_KV_AT + 4 * 2 * HALVES * ROW
Q_LATE_AT = Q_MID_AT + PAIR * 2 * N
K_PLANE_AT = Q_LATE_AT + HALF * 2 * N
K_AT = K_PLANE_AT + E * N
RAW_AT = K_AT + 4 * E * N
WINDOWS_AT = RAW_AT + E * RAW
END_AT = WINDOWS_AT + (3 * HALVES - 1) * 4 * T
X_AT = END_AT
SEED_AT = X_AT + 4 * T - 4 * SEED
Q_FIRST_AT = X_AT + 4 * T
GROUPED_AT = Q_FIRST_AT + 4 * PAIR * C
V_WORDS_AT = GROUPED_AT + PAIR * GROUPED
FIRST_RESULT_AT = V_WORDS_AT + 4 * PAIR * N


def tile_moe_qkv_kernel(tc, x_words, x_scales, wq_words, wq_scales, wk_words, wk_scales, wv, bias, gate, offs, out):
    nc = tc.nc
    add, mult = mybir.AluOpType.add, mybir.AluOpType.mult
    copy = mybir.ActivationFunctionType.Copy

    with ExitStack() as ctx:
        keep = ctx.enter_context(tc.tile_pool(name="keep", bufs=1))
        laid = ctx.enter_context(tc.tile_pool(name="laid", bufs=1))
        psum = ctx.enter_context(tc.psum_pool(name="psum", bufs=1))

        def tile(shape, dtype, name, place=None):
            if place is None:
                return keep.tile(shape, dtype, name=name, align_bytes=64)
            return laid.tile(shape, dtype, name=name, align_bytes=64, offset=place)

        offsets = keep.tile([P, S // LIST], U16, name="offsets")
        x_s = tile([P, T], U8, "x_s")
        q_plane = tile([P, E, N], U8, "q_plane")
        seeds = [
            tile([P, SEED], F32, "seed0", SEED_AT),
            tile([P, (END_AT - REST_AT) // 4], F32, "seed1", REST_AT),
        ]
        zeros = [tile([P, SEED], F32, f"zero{i}") for i in range(2)]

        nc.vector.memset(x_s[:].bitcast(I32), 0)
        for seed in seeds:
            nc.vector.memset(seed[:, 0:SEED], 0.0)
        nc.vector.tensor_copy(zeros[0][:], seeds[0][:, 0:SEED])
        nc.vector.memset(q_plane[:].bitcast(I32), 0)
        nc.vector.tensor_copy(zeros[1][:], seeds[1][:, 0:SEED])

        identity = tile([P, P], F32, "identity", IDENTITY_AT)
        make_identity(nc, identity[:])

        windows = [tile([P, T], F32, "window0")]
        for i, zero in enumerate(zeros):
            nc.scalar.copy(
                out=windows[0][:, i * T // 2 : (i + 1) * T // 2].rearrange("p (r c) -> p r c", c=SEED),
                in_=zero[:].unsqueeze(1).to_broadcast([P, T // 2 // SEED, SEED]),
            )
        k_plane = tile([P, E, N], U8, "k_plane", K_PLANE_AT)
        nc.gpsimd.memset(k_plane[:].bitcast(I32), 0)
        for i in range(3 * HALVES - 1):
            windows.append(tile([P, T], F32, f"window{1 + i}", WINDOWS_AT + i * 4 * T))
            nc.gpsimd.memset(windows[-1][:], 0.0)

        def load_scale_rows(plane, rows):
            for r in range(PACK):
                nc.sync.dma_start(out=plane[r:P:32], in_=rows[r])

        def weight_scale_rows(scales):
            return scales.bitcast(I32).rearrange("e s (q r) n -> r q (e s) n", r=PACK)

        q_rows = wq_words.bitcast(I32).rearrange("e s p b -> p (e s) b")
        k_rows = wk_words.rearrange("e s p n d -> p (e s) (n d)").bitcast(I32)
        v_rows = wv.rearrange("e (p j) n -> p e j n", j=PACK)

        nc.sync.dma_start(offsets[:], offs)
        gate_row = tile([P, 2, ROW], F32, "gate_row")
        nc.sync.dma_start(out=gate_row[:, :, 0:SPREAD], in_=gate[0].rearrange("(h p j) -> p h j", h=2, j=SPREAD))
        q_places = (Q_FIRST_AT, Q_MID_AT, Q_LATE_AT)
        q_w = [tile([P, e1 - e0, 2 * N], U8, f"q_w{e0}", place) for (e0, e1), place in zip(RUNS, q_places)]

        def load_queries(run):
            nc.sync.dma_start(out=q_w[run][:].bitcast(I32), in_=q_rows[:, RUNS[run][0] : RUNS[run][1]])

        load_queries(0)
        load_scale_rows(x_s[:].bitcast(I32), x_scales[0].bitcast(I32).rearrange("(q r) t -> r q t", r=PACK))
        x_w = tile([P, T], I32, "x_w", X_AT)
        nc.sync.dma_start(out=x_w[:], in_=x_words[0].rearrange("p t d -> p (t d)").bitcast(I32))
        bias_rows = bias.rearrange("(b p) e -> p b e", p=P)
        bias_q = tile([P, HALVES, ROW], F32, "bias_q", BIAS_Q_AT)
        nc.sync.dma_start(out=bias_q[:, :, 0:E], in_=bias_rows[:, 0:HALVES])
        load_scale_rows(q_plane[:].bitcast(I32), weight_scale_rows(wq_scales))
        load_queries(1)
        k_w = [tile([P, HALF, N], I32, f"k_w{i}", K_AT + i * 4 * HALF * N) for i in range(2)]
        nc.sync.dma_start(out=k_w[0][:], in_=k_rows[:, 0:HALF])
        load_scale_rows(k_plane[:].bitcast(I32), weight_scale_rows(wk_scales))
        bias_kv = tile([P, 2 * HALVES, ROW], F32, "bias_kv", BIAS_KV_AT)
        nc.sync.dma_start(out=bias_kv[:, :, 0:E], in_=bias_rows[:, HALVES : 3 * HALVES])
        load_queries(2)
        v_raw = [tile([P, PACK, N], F32, f"v_raw{e}", RAW_AT + e * RAW) for e in range(E)]
        for e in range(PAIR):
            nc.sync.dma_start(out=v_raw[e][:], in_=v_rows[:, e])
        nc.sync.dma_start(out=k_w[1][:], in_=k_rows[:, HALF:E])
        for e in range(PAIR, E):
            nc.sync.dma_start(out=v_raw[e][:], in_=v_rows[:, e])

        gates = tile([P, S], F32, "gates")
        for h in range(2):
            spread = psum.tile([P, 4, P], F32, name="spread", tag=f"bank{6 + h}")
            for j in range(SPREAD):
                nc.tensor.transpose(spread[:, j], gate_row[:, h, j : j + 1].to_broadcast([P, P]), identity[:])
            nc.scalar.copy(
                out=gates[:, h * HALF * C : (h + 1) * HALF * C].rearrange("p (n j) -> p n j", j=SPREAD),
                in_=spread[:, 0:SPREAD].rearrange("p j n -> p n j"),
            )

        def entries(s0, s1):
            return offsets[:, s0 // LIST : s1 // LIST]

        def gather(part, table, e0, e1):
            nc.vector.tensor_copy(part[:], table.indirect(entries(e0 * C, e1 * C)))
            return [part[:, i * C : (i + 1) * C] for i in range(e1 - e0)]

        slot_s = gather(tile([P, EARLY_BYTES * C], U8, "slot_s0"), x_s[:], 0, EARLY_BYTES)
        slot_w = []

        def gather_words(run, place=None):
            e0, e1 = WORD_RUNS[run]
            slot_w.extend(gather(tile([P, (e1 - e0) * C], U32, f"slot_w{e0}", place), x_w[:].bitcast(U32), e0, e1))

        gather_words(0)
        gather_words(1)
        q_of = [words[:, e - e0] for words, (e0, e1) in zip(q_w, RUNS) for e in range(e0, e1)]

        v_w, v_s = [], []
        sums = {}

        def weights(b, e):
            cols = slice(b % HALVES * P, (b % HALVES + 1) * P)
            if b < HALVES:
                return q_of[e][:, 2 * cols.start : 2 * cols.stop].bitcast(FP4X4), q_plane[:, e, cols]
            if b < 2 * HALVES:
                return k_w[e // HALF][:, e % HALF, cols].bitcast(FP8X4), k_plane[:, e, cols]
            return v_w[e][:, cols].bitcast(FP8X4), v_s[e][:, cols]

        def multiply(bank, b, e0, e1):
            acc = psum.tile([P, 4 * C], F32, name="acc", tag=f"bank{bank}")
            for e in range(e0, e1):
                w_codes, w_scales = weights(b, e)
                sums[b, e] = acc[:, (e - e0) * C : (e - e0 + 1) * C]
                nc.tensor.matmul_mx(
                    out=sums[b, e],
                    lhsT=w_codes,
                    lhsT_scale=w_scales,
                    rhs=slot_w[e].bitcast(FP8X4),
                    rhs_scale=slot_s[e],
                    start=True,
                    stop=True,
                )

        def piece(b, e0, e1, place=None):
            return b, e0, e1, tile([P, (e1 - e0) * C], F32, f"y{b}_{e0}", place)

        def finish(part, e0, e1):
            b, first, last, y = part
            biases = bias_q[:, b] if b < HALVES else bias_kv[:, b - HALVES]
            for e in range(e0, e1):
                nc.vector.scalar_tensor_tensor(
                    y[:, (e - first) * C : (e - first + 1) * C], sums[b, e], biases[:, e : e + 1], gates[:, e * C : (e + 1) * C], add, mult
                )

        def finished(b, e0, e1, place=None):
            part = piece(b, e0, e1, place)
            finish(part, e0, e1)
            return part

        def columns(part):
            b, e0, e1, y = part
            return windows[b][:].indirect(entries(e0 * C, e1 * C))

        def scatter_on_scalar(part):
            nc.scalar.activation(columns(part), part[3][:], copy)

        def scatter_on_vector(part):
            nc.vector.tensor_copy(columns(part), part[3][:])

        def store(b):
            nc.sync.dma_start(out=out[b * P : (b + 1) * P, :], in_=windows[b][:])

        def lay_out(e0):
            grouped = tile([P, PAIR, N, PACK], BF16, f"grouped{e0}", GROUPED_AT)
            for e in range(e0, e0 + PAIR):
                nc.gpsimd.tensor_scalar(
                    grouped[:, e - e0].rearrange("p (c i) t -> p c t i", i=4),
                    v_raw[e][:].rearrange("p t (c i) -> p c t i", i=4),
                    1.0,
                    0.0,
                    mult,
                    add,
                )
            return grouped

        def quantise(grouped, place=None):
            first = len(v_w)
            words = tile([P, PAIR * N], U32, f"v_w{first}", place)
            scales = tile([P, PAIR * N], U8, f"v_s{first}")
            nc.vector.quantize_mx(out=words[:].bitcast(FP8X4), scales=scales[:], in_=grouped[:].rearrange("p e n t -> p (e n t)"))
            v_w.extend(words[:, i * N : (i + 1) * N] for i in range(PAIR))
            v_s.extend(scales[:, i * N : (i + 1) * N] for i in range(PAIR))

        Q0, Q1, K0, K1, V0, V1 = range(3 * HALVES)

        multiply(0, Q0, 0, 1)
        multiply(1, Q1, 0, 1)
        multiply(2, Q0, 1, HALF)
        multiply(3, Q1, 1, HALF)
        scatter_on_scalar(finished(Q0, 0, 1, FIRST_RESULT_AT))
        scatter_on_scalar(finished(Q1, 0, 1))
        gather_words(2, Q_FIRST_AT)
        scatter_on_scalar(finished(Q0, 1, HALF))
        slot_s.extend(gather(tile([P, (E - EARLY_BYTES) * C], U8, "slot_s1", FIRST_RESULT_AT), x_s[:], EARLY_BYTES, E))
        scatter_on_scalar(finished(Q1, 1, HALF))

        multiply(4, K1, 0, HALF)
        multiply(5, K0, 0, HALF)
        multiply(6, Q0, HALF, E)
        multiply(7, Q1, HALF, E)
        k1 = finished(K1, 0, PAIR)
        k0 = finished(K0, 0, HALF)
        scatter_on_scalar(finished(Q0, HALF, E))
        store(Q0)
        scatter_on_vector(k1)
        k1 = finished(K1, PAIR, HALF, Q_LATE_AT)
        scatter_on_scalar(finished(Q1, HALF, E))
        store(Q1)
        scatter_on_scalar(k0)
        scatter_on_vector(k1)

        quantise(lay_out(0))
        grouped = lay_out(PAIR)
        multiply(1, K1, HALF, E)
        multiply(0, K0, HALF, E)
        multiply(3, V0, 0, PAIR)
        multiply(2, V1, 0, PAIR)
        k1 = finished(K1, HALF, E, RAW_AT + RAW)
        v0, v1 = piece(V0, 0, HALF), piece(V1, 1, HALF)
        finish(v0, 0, PAIR)
        finish(v1, 1, PAIR)
        scatter_on_vector(k1)
        store(K1)

        filler = finished(V1, 0, 1, RAW_AT + 3 * RAW)
        quantise(grouped, V_WORDS_AT)
        grouped = lay_out(2 * PAIR)
        scatter_on_vector(filler)
        multiply(5, V0, PAIR, 2 * PAIR)
        multiply(4, V1, PAIR, 2 * PAIR)
        finish(v0, PAIR, HALF)
        scatter_on_scalar(v0)
        finish(v1, PAIR, HALF)
        scatter_on_scalar(finished(K0, HALF, E, V_WORDS_AT))
        store(K0)
        v0 = piece(V0, HALF, E)
        finish(v0, HALF, 2 * PAIR)
        scatter_on_vector(v1)

        filler = finished(V1, HALF, 2 * PAIR, RAW_AT + 5 * RAW)
        quantise(grouped)
        scatter_on_vector(filler)
        multiply(6, V1, 2 * PAIR, E)
        multiply(7, V0, 2 * PAIR, E)
        v1 = finished(V1, 2 * PAIR, E)
        finish(v0, 2 * PAIR, E)
        scatter_on_vector(v1)
        store(V1)
        scatter_on_scalar(v0)
        store(V0)
